import numpy as np
import ml_dtypes


def mxq(x, axis, fmt="e4m3"):
    dtype, down = {"e4m3": (ml_dtypes.float8_e4m3fn, 7), "e5m2": (ml_dtypes.float8_e5m2, 14)}[fmt]
    v = np.moveaxis(np.asarray(x, np.float32).astype(ml_dtypes.bfloat16).astype(np.float64), axis, -1)
    blocks = v.reshape(v.shape[:-1] + (-1, 32))
    amax = np.abs(blocks).max(-1, keepdims=True)
    byte = np.maximum(np.where(amax > 0, np.frexp(amax)[1] - 1 + 127, 0) - down, 1)
    scale = np.exp2(byte - 127.0)
    codes = (blocks / scale).astype(np.float32).astype(dtype).astype(np.float64)
    return np.moveaxis((codes * scale).reshape(v.shape), -1, axis)


WIDE = False


def mx_kscale(k):
    if not WIDE:
        return np.ones(k)
    levels = np.array([10, -10, 5, -5, 0])
    if k % 512:
        return np.exp2(np.random.permutation(np.resize(levels, k // 32))).repeat(32)
    a = np.empty((k // 512, 16))
    for p in range(k // 512):
        a[p, :8] = np.random.permutation(np.resize(levels, 8))
        for g in range(8):
            far = levels[np.abs(levels - a[p, g]) >= 10]
            a[p, g + 8] = far[np.random.randint(len(far))]
    return np.exp2(a.ravel()).repeat(32)


def f64(x):
    return np.asarray(x).astype(np.float64)


def striped(idx):
    return np.tile(np.asarray(idx).reshape(-1, 16).T, (8, 1)).astype(np.uint16)


def unstriped(offs):
    return offs[:16].T.reshape(-1).astype(np.int64)


E2M1 = np.array([0.0, 0.5, 1.0, 1.5, 2.0, 3.0, 4.0, 6.0, -0.0, -0.5, -1.0, -1.5, -2.0, -3.0, -4.0, -6.0])


def pack_weight(w, fmt):
    k, n = w.shape
    w = f64(np.asarray(w, np.float32).astype(ml_dtypes.bfloat16)).reshape(k // 32, 32, n)
    amax = np.abs(w).max(1)
    if fmt == "e4m3":
        byte = np.frexp(amax)[1] - 1 + 127 - 7
    else:
        mant, ex = np.frexp(amax / 6.0)
        byte = np.where(mant > 0.5, ex, ex - 1) + 127
    byte = np.clip(np.where(amax > 0, byte, 1), 1, 254)
    scaled = (w * np.exp2(127.0 - byte)[:, None, :]).reshape(k, n).astype(np.float32)
    by_word = np.ascontiguousarray(scaled.reshape(k // 512, 128, 4, n).transpose(0, 1, 3, 2))
    if fmt == "e4m3":
        words = by_word.astype(ml_dtypes.float8_e4m3fn).view(np.uint8)
    else:
        c = by_word.astype(ml_dtypes.float4_e2m1fn).view(np.uint8) & 0xF
        words = (c[..., 0::2] | (c[..., 1::2] << 4)).reshape(k // 512, 128, 2 * n)
    return np.ascontiguousarray(words), np.ascontiguousarray(byte.astype(np.uint8).reshape(k // 512, 16, n))


def unpack_weight(words, scales, fmt):
    g, _, n = scales.shape
    words = np.ascontiguousarray(words).reshape(g, 128, n, -1)
    if fmt == "e4m3":
        vals = words.view(ml_dtypes.float8_e4m3fn).astype(np.float64)
    else:
        nib = np.empty((g, 128, n, 4), np.uint8)
        nib[..., 0::2] = words & 0xF
        nib[..., 1::2] = words >> 4
        vals = E2M1[nib]
    vals = vals * np.repeat(np.exp2(scales.astype(np.float64) - 127.0), 8, axis=1)[..., None]
    return vals.transpose(0, 1, 3, 2).reshape(g * 512, n)


B, N, T, D, DV, NQ = 1, 512, 2048, 1024, 128, 128


def setup_inputs():
    n = np.random.standard_normal
    idx = np.random.permutation(T)[:B * N]
    s = mx_kscale(D)[:, None]
    u = np.ones(T)
    u[idx] = mx_kscale(B * N)
    r = np.random.uniform(0.5, 2.0, T)
    qp = [pack_weight(x, "e4m3") for x in n((B, D, NQ)) * s * (1.00 / np.sqrt(D))]
    k = n((D, T)) / s
    v = n((DV, T)) / (u * r)
    kp = pack_weight(k, "e2m1")
    return {
        "q_words": np.stack([x[0] for x in qp]),
        "q_scales": np.stack([x[1] for x in qp]),
        "k_words": np.ascontiguousarray(kp[0].reshape(D // 1024, 2, 128, T, 2).transpose(0, 2, 3, 1, 4)).reshape(D // 1024, 128, T, 4),
        "k_scales": kp[1],
        "vT": v.astype(np.float32),
        "vs": np.tile(u * r, (128, 1)).astype(np.float32),
        "offs": striped(idx),
    }


def reference(q_words, q_scales, k_words, k_scales, vT, vs, offs):
    idx = unstriped(offs)
    k = unpack_weight(k_words.reshape(D // 1024, 128, T, 2, 2).transpose(0, 3, 1, 2, 4).reshape(D // 512, 128, 2 * T), k_scales, "e2m1")
    v = f64(vT)
    pick = lambda x: x[:, idx].reshape(x.shape[0], B, N).transpose(1, 0, 2)
    q = np.stack([unpack_weight(q_words[b], q_scales[b], "e4m3") for b in range(B)])
    score = q.transpose(0, 2, 1) @ pick(k)
    p = score / (1.0 + np.exp(-score))
    w = p * pick(f64(vs))[:, :1, :]
    y = mxq(w, 2, "e4m3") @ mxq(pick(v).transpose(0, 2, 1), 1, "e4m3")
    y = y / 16.0
    return y

@@ -1,0 +1,139 @@
+from contextlib import ExitStack
+
+import concourse.mybir as mybir
+from concourse.masks import make_identity
+
+F32 = mybir.dt.float32
+BF16 = mybir.dt.bfloat16
+I32 = mybir.dt.int32
+U32 = mybir.dt.uint32
+U16 = mybir.dt.uint16
+U8 = mybir.dt.uint8
+FP8X4 = mybir.dt.float8_e4m3fn_x4
+FP4X4 = mybir.dt.float4_e2m1fn_x4
+ACT = mybir.ActivationFunctionType
+ALU = mybir.AluOpType
+
+P = 128
+T = 2048
+N = 512
+D = 1024
+DV = 128
+NQ = 128
+PASSES = 2
+PACK = 4
+SHIFT = 16
+
+FLOPS = 2 * NQ * N * D + 2 * NQ * N * DV
+BYTES = 2 * 128 * 128 * 4 + 2 * 16 * 128 + 128 * T * 4 + 2 * 16 * T + DV * T * 4 + T * 4 + 128 * 32 * 2 + NQ * DV * 4
+
+
+def tile_attend_silu_topkq128n512t2048_kernel(tc, q_words, q_scales, k_words, k_scales, vT, vs, offs, out):
+    nc = tc.nc
+    with ExitStack() as ctx:
+        sb = ctx.enter_context(tc.tile_pool(name="sb", bufs=1))
+        ps = ctx.enter_context(tc.psum_pool(name="ps", bufs=1))
+
+        offsets = sb.tile([P, N // 16], U16, name="offsets")
+        kw_pool = sb.tile([P, T], I32, name="kw_pool", align_bytes=64)
+        ks_pool = sb.tile([P, T], U8, name="ks_pool", align_bytes=64)
+        v_pool = sb.tile([P, T], F32, name="v_pool", align_bytes=64)
+        vs_pool = sb.tile([P, T], F32, name="vs_pool", align_bytes=64)
+        qw = sb.tile([P, PASSES, NQ], I32, name="qw", align_bytes=64)
+        qs = sb.tile([P, PASSES * NQ], U8, name="qs", align_bytes=64)
+        ident = sb.tile([P, P], F32, name="ident", align_bytes=64)
+        kw_g = sb.tile([P, N], U32, name="kw_g", align_bytes=64)
+        ks_g = sb.tile([P, N], U8, name="ks_g", align_bytes=64)
+        ks_first = sb.tile([P, N], U8, name="ks_first", align_bytes=64)
+        ks_second = sb.tile([P, N], U8, name="ks_second", align_bytes=64)
+        k_codes = sb.tile([P, PASSES * N * 2], U8, name="k_codes", align_bytes=64)
+        vs_g = sb.tile([P, N], F32, name="vs_g", align_bytes=64)
+        v_g = sb.tile([P, N], BF16, name="v_g", align_bytes=64)
+        p_sb = sb.tile([P, PACK, NQ], F32, name="p_sb", align_bytes=64)
+        w_in = sb.tile([P, NQ, PACK], BF16, name="w_in", align_bytes=64)
+        v_in = sb.tile([P, DV, PACK], BF16, name="v_in", align_bytes=64)
+        w_codes = sb.tile([P, NQ], U32, name="w_codes", align_bytes=64)
+        w_scales = sb.tile([P, NQ], U8, name="w_scales", align_bytes=64)
+        v_codes = sb.tile([P, DV], U32, name="v_codes", align_bytes=64)
+        v_scales = sb.tile([P, DV], U8, name="v_scales", align_bytes=64)
+        y_sb = sb.tile([P, DV], F32, name="y_sb", align_bytes=64)
+
+        scores = [ps.tile([P, NQ], F32, name="score%d" % t) for t in range(PACK)]
+        vs_t = ps.tile([P, PACK, P], F32, name="vs_t")
+        v_t = ps.tile([P, 2, DV], F32, name="v_t")
+        y_ps = ps.tile([P, DV], F32, name="y_ps")
+
+        nc.sync.dma_start(offsets[:], offs)
+        nc.sync.dma_start(kw_pool[:], k_words[0].rearrange("g t r -> g (t r)").bitcast(I32))
+        nc.sync.dma_start(v_pool[:], vT)
+
+        nc.vector.memset(ks_pool[:].bitcast(I32), 0)
+        ks_rows = k_scales.bitcast(I32).rearrange("o (a i) c -> i a o c", i=4)
+        for i in range(4):
+            nc.scalar.dma_start(ks_pool[:].bitcast(I32)[i:P:SHIFT, :], ks_rows[i])
+        nc.vector.memset(vs_pool[:], 0.0)
+        nc.scalar.dma_start(vs_pool[0:1, :], vs[0:1, :])
+        nc.vector.memset(ks_second[:].bitcast(I32), 0)
+
+        nc.gpsimd.memset(qs[:], 0)
+        nc.gpsimd.dma_start(qw[:], q_words[0].rearrange("o g q r -> g o (q r)").bitcast(I32))
+        qs_rows = q_scales[0].bitcast(I32).rearrange("o (a i) c -> i a o c", i=4)
+        for i in range(4):
+            nc.gpsimd.dma_start(qs[:].bitcast(I32)[i:P:32, :].rearrange("a (o c) -> a o c", o=PASSES), qs_rows[i])
+        make_identity(nc, ident[:])
+
+        nc.vector.tensor_copy(ks_g[:], ks_pool[:].indirect(offsets[:]))
+        nc.vector.tensor_copy(
+            ks_first[:].rearrange("p (t m) -> p t m", t=PACK), ks_g[:].rearrange("p (m t) -> p t m", t=PACK)
+        )
+        nc.scalar.dma_start(ks_second[:].bitcast(I32)[0 : P - SHIFT, :], ks_first[:].bitcast(I32)[SHIFT:P, :])
+        nc.vector.tensor_copy(vs_g[:], vs_pool[:].indirect(offsets[:]))
+        for t in range(PACK):
+            nc.tensor.transpose(vs_t[:, t, :], vs_g[:, t:N:PACK], ident[:])
+        nc.vector.tensor_copy(kw_g[:].rearrange("p (t m) -> p m t", t=PACK), kw_pool[:].bitcast(U32).indirect(offsets[:]))
+
+        halves_in = kw_g[:].bitcast(U16).rearrange("p (c o) -> p o c", o=PASSES)
+        halves_out = k_codes[:].bitcast(U16).rearrange("p (o c) -> p o c", o=PASSES)
+        for h in range(2):
+            cols = slice(h * N // 2, (h + 1) * N // 2)
+            nc.vector.tensor_copy(halves_out[:, :, cols], halves_in[:, :, cols])
+
+        k_planes = [ks_first, ks_second]
+        for t in range(PACK):
+            for o in range(PASSES):
+                start = (o * N + t * P) * 2
+                nc.tensor.matmul_mx(
+                    out=scores[t][:],
+                    lhsT=k_codes[:, start : start + 2 * P].bitcast(FP4X4),
+                    lhsT_scale=k_planes[o][:, t * P : (t + 1) * P],
+                    rhs=qw[:, o, :].bitcast(FP8X4),
+                    rhs_scale=qs[:, o * NQ : (o + 1) * NQ],
+                    start=(o == 0),
+                    stop=(o == PASSES - 1),
+                )
+            nc.scalar.activation(p_sb[:, t, :], scores[t][:], ACT.Silu)
+
+        nc.vector.tensor_copy(v_g[:].rearrange("p (u m r) -> p m u r", u=2, r=2), v_pool[:].indirect(offsets[:]))
+        nc.vector.tensor_tensor(
+            w_in[:],
+            p_sb[:].rearrange("p t q -> p q t"),
+            vs_t[:, :, 0:1].rearrange("p t a -> p a t").to_broadcast([P, NQ, PACK]),
+            ALU.mult,
+        )
+        v_words = v_g[:].bitcast(F32)
+        for u in range(2):
+            nc.tensor.transpose(v_t[:, u, :], v_words[:, u * P : (u + 1) * P], ident[:])
+        nc.scalar.copy(v_in[:].bitcast(F32), v_t[:].rearrange("p u e -> p e u"))
+        nc.vector.quantize_mx(out=w_codes[:].bitcast(FP8X4), scales=w_scales[:], in_=w_in[:].rearrange("p q t -> p (q t)"))
+        nc.vector.quantize_mx(out=v_codes[:].bitcast(FP8X4), scales=v_scales[:], in_=v_in[:].rearrange("p e t -> p (e t)"))
+        nc.tensor.matmul_mx(
+            out=y_ps[:],
+            lhsT=w_codes[:].bitcast(FP8X4),
+            lhsT_scale=w_scales[:],
+            rhs=v_codes[:].bitcast(FP8X4),
+            rhs_scale=v_scales[:],
+            start=True,
+            stop=True,
+        )
+        nc.vector.tensor_scalar(y_sb[:], y_ps[:], 1.0 / 16.0, None, ALU.mult)
+        nc.sync.dma_start(out[0], y_sb[:])

@@ -32,17 +32,15 @@ def tile_attend_silu_topkq128n512t2048_kernel(tc, q_words, q_scales, k_words, k_
     nc = tc.nc
     with ExitStack() as ctx:
         sb = ctx.enter_context(tc.tile_pool(name="sb", bufs=1))
+        big = ctx.enter_context(tc.tile_pool(name="big", bufs=1))
         ps = ctx.enter_context(tc.psum_pool(name="ps", bufs=1))
 
         offsets = sb.tile([P, N // 16], U16, name="offsets")
-        kw_pool = sb.tile([P, T], I32, name="kw_pool", align_bytes=64)
         ks_pool = sb.tile([P, T], U8, name="ks_pool", align_bytes=64)
-        v_pool = sb.tile([P, T], F32, name="v_pool", align_bytes=64)
-        vs_pool = sb.tile([P, T], F32, name="vs_pool", align_bytes=64)
+        vs_pool = big.tile([P, T], F32, name="vs_pool", offset=8 * T)
         qw = sb.tile([P, PASSES, NQ], I32, name="qw", align_bytes=64)
         qs = sb.tile([P, PASSES * NQ], U8, name="qs", align_bytes=64)
         ident = sb.tile([P, P], F32, name="ident", align_bytes=64)
-        kw_g = sb.tile([P, N], U32, name="kw_g", align_bytes=64)
         ks_g = sb.tile([P, N], U8, name="ks_g", align_bytes=64)
         ks_first = sb.tile([P, N], U8, name="ks_first", align_bytes=64)
         ks_second = sb.tile([P, N], U8, name="ks_second", align_bytes=64)
@@ -64,23 +62,25 @@ def tile_attend_silu_topkq128n512t2048_kernel(tc, q_words, q_scales, k_words, k_
         y_ps = ps.tile([P, DV], F32, name="y_ps")
 
         nc.sync.dma_start(offsets[:], offs)
-        nc.sync.dma_start(kw_pool[:], k_words[0].rearrange("g t r -> g (t r)").bitcast(I32))
-        nc.sync.dma_start(v_pool[:], vT)
-
+        nc.scalar.dma_start(qw[:], q_words[0].rearrange("o g q r -> g o (q r)").bitcast(I32))
         nc.vector.memset(ks_pool[:].bitcast(I32), 0)
         ks_rows = k_scales.bitcast(I32).rearrange("o (a i) c -> i a o c", i=4)
         for i in range(4):
-            nc.scalar.dma_start(ks_pool[:].bitcast(I32)[i:P:SHIFT, :], ks_rows[i])
+            nc.sync.dma_start(ks_pool[:].bitcast(I32)[i:P:SHIFT, :], ks_rows[i])
+        zeros = big.tile([P, N // 4], I32, name="zeros", offset=4 * T - N // 2)
+        nc.vector.memset(zeros[:], 0)
+        nc.vector.tensor_copy(ks_second[:].bitcast(I32), zeros[:])
+        make_identity(nc, ident[:])
+        kw_pool = big.tile([P, T], I32, name="kw_pool", offset=0)
+        nc.sync.dma_start(kw_pool[:], k_words[0].rearrange("g t r -> g (t r)").bitcast(I32))
+        v_pool = big.tile([P, T], F32, name="v_pool", offset=4 * T)
+        nc.sync.dma_start(v_pool[:], vT)
         nc.vector.memset(vs_pool[:], 0.0)
         nc.scalar.dma_start(vs_pool[0:1, :], vs[0:1, :])
-        nc.vector.memset(ks_second[:].bitcast(I32), 0)
-
-        nc.gpsimd.memset(qs[:], 0)
-        nc.gpsimd.dma_start(qw[:], q_words[0].rearrange("o g q r -> g o (q r)").bitcast(I32))
+        nc.vector.memset(qs[:].bitcast(I32), 0)
         qs_rows = q_scales[0].bitcast(I32).rearrange("o (a i) c -> i a o c", i=4)
         for i in range(4):
-            nc.gpsimd.dma_start(qs[:].bitcast(I32)[i:P:32, :].rearrange("a (o c) -> a o c", o=PASSES), qs_rows[i])
-        make_identity(nc, ident[:])
+            nc.scalar.dma_start(qs[:].bitcast(I32)[i:P:32, :].rearrange("a (o c) -> a o c", o=PASSES), qs_rows[i])
 
         nc.vector.tensor_copy(ks_g[:], ks_pool[:].indirect(offsets[:]))
         nc.vector.tensor_copy(
@@ -90,17 +90,17 @@ def tile_attend_silu_topkq128n512t2048_kernel(tc, q_words, q_scales, k_words, k_
         nc.vector.tensor_copy(vs_g[:], vs_pool[:].indirect(offsets[:]))
         for t in range(PACK):
             nc.tensor.transpose(vs_t[:, t, :], vs_g[:, t:N:PACK], ident[:])
+        kw_g = big.tile([P, N], U32, name="kw_g", offset=8 * T)
         nc.vector.tensor_copy(kw_g[:].rearrange("p (t m) -> p m t", t=PACK), kw_pool[:].bitcast(U32).indirect(offsets[:]))
 
         halves_in = kw_g[:].bitcast(U16).rearrange("p (c o) -> p o c", o=PASSES)
         halves_out = k_codes[:].bitcast(U16).rearrange("p (o c) -> p o c", o=PASSES)
-        for h in range(2):
-            cols = slice(h * N // 2, (h + 1) * N // 2)
-            nc.vector.tensor_copy(halves_out[:, :, cols], halves_in[:, :, cols])
+        for o in range(PASSES):
+            nc.vector.tensor_copy(halves_out[:, o, :], halves_in[:, o, :])
 
         k_planes = [ks_first, ks_second]
-        for t in range(PACK):
-            for o in range(PASSES):
+        for o in range(PASSES):
+            for t in range(PACK):
                 start = (o * N + t * P) * 2
                 nc.tensor.matmul_mx(
                     out=scores[t][:],
@@ -111,6 +111,7 @@ def tile_attend_silu_topkq128n512t2048_kernel(tc, q_words, q_scales, k_words, k_
                     start=(o == 0),
                     stop=(o == PASSES - 1),
                 )
+        for t in range(PACK):
             nc.scalar.activation(p_sb[:, t, :], scores[t][:], ACT.Silu)
 
         nc.vector.tensor_copy(v_g[:].rearrange("p (u m r) -> p m u r", u=2, r=2), v_pool[:].indirect(offsets[:]))

@@ -36,7 +36,7 @@ def tile_attend_silu_topkq128n512t2048_kernel(tc, q_words, q_scales, k_words, k_
         ps = ctx.enter_context(tc.psum_pool(name="ps", bufs=1))
 
         offsets = sb.tile([P, N // 16], U16, name="offsets")
-        ks_pool = sb.tile([P, T], U8, name="ks_pool", align_bytes=64)
+        ks_pool = big.tile([P, T], U8, name="ks_pool", offset=12 * T)
         vs_pool = big.tile([P, T], F32, name="vs_pool", offset=8 * T)
         qw = sb.tile([P, PASSES, NQ], I32, name="qw", align_bytes=64)
         qs = sb.tile([P, PASSES * NQ], U8, name="qs", align_bytes=64)
@@ -44,9 +44,7 @@ def tile_attend_silu_topkq128n512t2048_kernel(tc, q_words, q_scales, k_words, k_
         ks_g = sb.tile([P, N], U8, name="ks_g", align_bytes=64)
         ks_first = sb.tile([P, N], U8, name="ks_first", align_bytes=64)
         ks_second = sb.tile([P, N], U8, name="ks_second", align_bytes=64)
-        k_codes = sb.tile([P, PASSES * N * 2], U8, name="k_codes", align_bytes=64)
-        vs_g = sb.tile([P, N], F32, name="vs_g", align_bytes=64)
-        v_g = sb.tile([P, N], BF16, name="v_g", align_bytes=64)
+        vs_g = big.tile([P, N], F32, name="vs_g", offset=13 * T, align_bytes=64)
         p_sb = sb.tile([P, PACK, NQ], F32, name="p_sb", align_bytes=64)
         w_in = sb.tile([P, NQ, PACK], BF16, name="w_in", align_bytes=64)
         v_in = sb.tile([P, DV, PACK], BF16, name="v_in", align_bytes=64)
@@ -56,43 +54,47 @@ def tile_attend_silu_topkq128n512t2048_kernel(tc, q_words, q_scales, k_words, k_
         v_scales = sb.tile([P, DV], U8, name="v_scales", align_bytes=64)
         y_sb = sb.tile([P, DV], F32, name="y_sb", align_bytes=64)
 
-        scores = [ps.tile([P, NQ], F32, name="score%d" % t) for t in range(PACK)]
+        scores = [ps.tile([P, NQ], F32, name="score%d" % t, tag="bank%d" % t) for t in range(PACK)]
         vs_t = ps.tile([P, PACK, P], F32, name="vs_t")
-        v_t = ps.tile([P, 2, DV], F32, name="v_t")
         y_ps = ps.tile([P, DV], F32, name="y_ps")
 
         nc.sync.dma_start(offsets[:], offs)
+        nc.scalar.dma_start(vs_pool[P - 1 : P, :], vs[0:1, :])
         nc.scalar.dma_start(qw[:], q_words[0].rearrange("o g q r -> g o (q r)").bitcast(I32))
         nc.vector.memset(ks_pool[:].bitcast(I32), 0)
         ks_rows = k_scales.bitcast(I32).rearrange("o (a i) c -> i a o c", i=4)
         for i in range(4):
-            nc.sync.dma_start(ks_pool[:].bitcast(I32)[i:P:SHIFT, :], ks_rows[i])
+            (nc.sync, nc.scalar)[i % 2].dma_start(ks_pool[:].bitcast(I32)[i:P:SHIFT, :], ks_rows[i])
         zeros = big.tile([P, N // 4], I32, name="zeros", offset=4 * T - N // 2)
-        nc.vector.memset(zeros[:], 0)
+        nc.gpsimd.memset(zeros[:], 0)
         nc.vector.tensor_copy(ks_second[:].bitcast(I32), zeros[:])
         make_identity(nc, ident[:])
+        nc.vector.memset(qs[:].bitcast(I32), 0)
         kw_pool = big.tile([P, T], I32, name="kw_pool", offset=0)
         nc.sync.dma_start(kw_pool[:], k_words[0].rearrange("g t r -> g (t r)").bitcast(I32))
         v_pool = big.tile([P, T], F32, name="v_pool", offset=4 * T)
         nc.sync.dma_start(v_pool[:], vT)
-        nc.vector.memset(vs_pool[:], 0.0)
-        nc.scalar.dma_start(vs_pool[0:1, :], vs[0:1, :])
-        nc.vector.memset(qs[:].bitcast(I32), 0)
+        nc.vector.memset(vs_pool[0 : P - 1, :].bitcast(I32), 0)
         qs_rows = q_scales[0].bitcast(I32).rearrange("o (a i) c -> i a o c", i=4)
         for i in range(4):
             nc.scalar.dma_start(qs[:].bitcast(I32)[i:P:32, :].rearrange("a (o c) -> a o c", o=PASSES), qs_rows[i])
 
+        nc.vector.tensor_copy(vs_g[:], vs_pool[:].indirect(offsets[:]))
+        for t in range(PACK):
+            nc.tensor.transpose(vs_t[:, t, :], vs_g[:, t:N:PACK], ident[:])
         nc.vector.tensor_copy(ks_g[:], ks_pool[:].indirect(offsets[:]))
         nc.vector.tensor_copy(
             ks_first[:].rearrange("p (t m) -> p t m", t=PACK), ks_g[:].rearrange("p (m t) -> p t m", t=PACK)
         )
-        nc.scalar.dma_start(ks_second[:].bitcast(I32)[0 : P - SHIFT, :], ks_first[:].bitcast(I32)[SHIFT:P, :])
-        nc.vector.tensor_copy(vs_g[:], vs_pool[:].indirect(offsets[:]))
-        for t in range(PACK):
-            nc.tensor.transpose(vs_t[:, t, :], vs_g[:, t:N:PACK], ident[:])
-        kw_g = big.tile([P, N], U32, name="kw_g", offset=8 * T)
+        for first, count in ((0, 64), (64, 4), (96, 4)):
+            nc.scalar.dma_start(
+                ks_second[:].bitcast(I32)[first : first + count, :],
+                ks_first[:].bitcast(I32)[first + SHIFT : first + SHIFT + count, :],
+            )
+        kw_g = big.tile([P, N], U32, name="kw_g", offset=12 * T)
         nc.vector.tensor_copy(kw_g[:].rearrange("p (t m) -> p m t", t=PACK), kw_pool[:].bitcast(U32).indirect(offsets[:]))
 
+        k_codes = big.tile([P, PASSES * N * 2], U8, name="k_codes", offset=13 * T, align_bytes=64)
         halves_in = kw_g[:].bitcast(U16).rearrange("p (c o) -> p o c", o=PASSES)
         halves_out = k_codes[:].bitcast(U16).rearrange("p (o c) -> p o c", o=PASSES)
         for o in range(PASSES):
@@ -114,13 +116,15 @@ def tile_attend_silu_topkq128n512t2048_kernel(tc, q_words, q_scales, k_words, k_
         for t in range(PACK):
             nc.scalar.activation(p_sb[:, t, :], scores[t][:], ACT.Silu)
 
+        v_g = big.tile([P, N], BF16, name="v_g", offset=12 * T)
         nc.vector.tensor_copy(v_g[:].rearrange("p (u m r) -> p m u r", u=2, r=2), v_pool[:].indirect(offsets[:]))
         nc.vector.tensor_tensor(
             w_in[:],
             p_sb[:].rearrange("p t q -> p q t"),
-            vs_t[:, :, 0:1].rearrange("p t a -> p a t").to_broadcast([P, NQ, PACK]),
+            vs_t[:, :, P - 1 : P].rearrange("p t a -> p a t").to_broadcast([P, NQ, PACK]),
             ALU.mult,
         )
+        v_t = ps.tile([P, 2, DV], F32, name="v_t", tag="bank0")
         v_words = v_g[:].bitcast(F32)
         for u in range(2):
             nc.tensor.transpose(v_t[:, u, :], v_words[:, u * P : (u + 1) * P], ident[:])

@@ -61,23 +61,23 @@ def tile_attend_silu_topkq128n512t2048_kernel(tc, q_words, q_scales, k_words, k_
         nc.sync.dma_start(offsets[:], offs)
         nc.scalar.dma_start(vs_pool[P - 1 : P, :], vs[0:1, :])
         nc.scalar.dma_start(qw[:], q_words[0].rearrange("o g q r -> g o (q r)").bitcast(I32))
+        zeros = big.tile([P, N // 4], I32, name="zeros", offset=4 * T - N // 2)
+        nc.vector.memset(zeros[:], 0)
         nc.vector.memset(ks_pool[:].bitcast(I32), 0)
         ks_rows = k_scales.bitcast(I32).rearrange("o (a i) c -> i a o c", i=4)
         for i in range(4):
-            (nc.sync, nc.scalar)[i % 2].dma_start(ks_pool[:].bitcast(I32)[i:P:SHIFT, :], ks_rows[i])
-        zeros = big.tile([P, N // 4], I32, name="zeros", offset=4 * T - N // 2)
-        nc.gpsimd.memset(zeros[:], 0)
+            nc.sync.dma_start(ks_pool[:].bitcast(I32)[i:P:SHIFT, :], ks_rows[i])
         nc.vector.tensor_copy(ks_second[:].bitcast(I32), zeros[:])
         make_identity(nc, ident[:])
-        nc.vector.memset(qs[:].bitcast(I32), 0)
+        nc.vector.tensor_copy(qs[:].bitcast(I32), zeros[:, 0 : PASSES * NQ // 4])
         kw_pool = big.tile([P, T], I32, name="kw_pool", offset=0)
         nc.sync.dma_start(kw_pool[:], k_words[0].rearrange("g t r -> g (t r)").bitcast(I32))
-        v_pool = big.tile([P, T], F32, name="v_pool", offset=4 * T)
-        nc.sync.dma_start(v_pool[:], vT)
         nc.vector.memset(vs_pool[0 : P - 1, :].bitcast(I32), 0)
         qs_rows = q_scales[0].bitcast(I32).rearrange("o (a i) c -> i a o c", i=4)
         for i in range(4):
-            nc.scalar.dma_start(qs[:].bitcast(I32)[i:P:32, :].rearrange("a (o c) -> a o c", o=PASSES), qs_rows[i])
+            nc.sync.dma_start(qs[:].bitcast(I32)[i:P:32, :].rearrange("a (o c) -> a o c", o=PASSES), qs_rows[i])
+        v_pool = big.tile([P, T], F32, name="v_pool", offset=4 * T)
+        nc.sync.dma_start(v_pool[:], vT)
 
         nc.vector.tensor_copy(vs_g[:], vs_pool[:].indirect(offsets[:]))
         for t in range(PACK):
@@ -86,11 +86,7 @@ def tile_attend_silu_topkq128n512t2048_kernel(tc, q_words, q_scales, k_words, k_
         nc.vector.tensor_copy(
             ks_first[:].rearrange("p (t m) -> p t m", t=PACK), ks_g[:].rearrange("p (m t) -> p t m", t=PACK)
         )
-        for first, count in ((0, 64), (64, 4), (96, 4)):
-            nc.scalar.dma_start(
-                ks_second[:].bitcast(I32)[first : first + count, :],
-                ks_first[:].bitcast(I32)[first + SHIFT : first + SHIFT + count, :],
-            )
+        nc.scalar.dma_start(ks_second[:].bitcast(I32)[0 : P - SHIFT, :], ks_first[:].bitcast(I32)[SHIFT:P, :])
         kw_g = big.tile([P, N], U32, name="kw_g", offset=12 * T)
         nc.vector.tensor_copy(kw_g[:].rearrange("p (t m) -> p m t", t=PACK), kw_pool[:].bitcast(U32).indirect(offsets[:]))
 

@@ -22,7 +22,9 @@ DV = 128
 NQ = 128
 PASSES = 2
 PACK = 4
-SHIFT = 16
+RUN = 8
+QUAD = 32
+ROWS = 4
 
 FLOPS = 2 * NQ * N * D + 2 * NQ * N * DV
 BYTES = 2 * 128 * 128 * 4 + 2 * 16 * 128 + 128 * T * 4 + 2 * 16 * T + DV * T * 4 + T * 4 + 128 * 32 * 2 + NQ * DV * 4
@@ -32,19 +34,25 @@ def tile_attend_silu_topkq128n512t2048_kernel(tc, q_words, q_scales, k_words, k_
     nc = tc.nc
     with ExitStack() as ctx:
         sb = ctx.enter_context(tc.tile_pool(name="sb", bufs=1))
-        big = ctx.enter_context(tc.tile_pool(name="big", bufs=1))
         ps = ctx.enter_context(tc.psum_pool(name="ps", bufs=1))
 
         offsets = sb.tile([P, N // 16], U16, name="offsets")
-        ks_pool = big.tile([P, T], U8, name="ks_pool", offset=12 * T)
-        vs_pool = big.tile([P, T], F32, name="vs_pool", offset=8 * T)
+        ks_pool = sb.tile([P, T + 4], U8, name="ks_pool")
+        vs_pool = sb.tile([P, T], F32, name="vs_pool")
+        kw_pool = sb.tile([P, T], I32, name="kw_pool")
+        v_pool = sb.tile([P, T], F32, name="v_pool")
         qw = sb.tile([P, PASSES, NQ], I32, name="qw", align_bytes=64)
-        qs = sb.tile([P, PASSES * NQ], U8, name="qs", align_bytes=64)
         ident = sb.tile([P, P], F32, name="ident", align_bytes=64)
+        warm = sb.tile([P, 1], F32, name="warm")
+        warm_in = sb.tile([P, 1], F32, name="warm_in")
         ks_g = sb.tile([P, N], U8, name="ks_g", align_bytes=64)
-        ks_first = sb.tile([P, N], U8, name="ks_first", align_bytes=64)
-        ks_second = sb.tile([P, N], U8, name="ks_second", align_bytes=64)
-        vs_g = big.tile([P, N], F32, name="vs_g", offset=13 * T, align_bytes=64)
+        staged = sb.tile([P, N + NQ], U8, name="staged", align_bytes=64)
+        planes = sb.tile([P, PASSES * (N + NQ) + 4], U8, name="planes", align_bytes=64)
+        vs_g = sb.tile([P, N], F32, name="vs_g", align_bytes=64)
+        vs_dealt = sb.tile([P, N], F32, name="vs_dealt", align_bytes=64)
+        kw_g = sb.tile([P, N], U32, name="kw_g", align_bytes=64)
+        k_codes = [sb.tile([P, PASSES * P * 2], U8, name="k_codes%d" % t, align_bytes=64) for t in range(PACK)]
+        v_g = sb.tile([P, N], BF16, name="v_g", align_bytes=64)
         p_sb = sb.tile([P, PACK, NQ], F32, name="p_sb", align_bytes=64)
         w_in = sb.tile([P, NQ, PACK], BF16, name="w_in", align_bytes=64)
         v_in = sb.tile([P, DV, PACK], BF16, name="v_in", align_bytes=64)
@@ -54,73 +62,71 @@ def tile_attend_silu_topkq128n512t2048_kernel(tc, q_words, q_scales, k_words, k_
         v_scales = sb.tile([P, DV], U8, name="v_scales", align_bytes=64)
         y_sb = sb.tile([P, DV], F32, name="y_sb", align_bytes=64)
 
-        scores = [ps.tile([P, NQ], F32, name="score%d" % t, tag="bank%d" % t) for t in range(PACK)]
+        scores = [ps.tile([P, NQ], F32, name="score%d" % t) for t in range(PACK)]
         vs_t = ps.tile([P, PACK, P], F32, name="vs_t")
+        v_t = ps.tile([P, 2, DV], F32, name="v_t")
         y_ps = ps.tile([P, DV], F32, name="y_ps")
 
+        last = P - QUAD
         nc.sync.dma_start(offsets[:], offs)
-        nc.scalar.dma_start(vs_pool[P - 1 : P, :], vs[0:1, :])
-        nc.scalar.dma_start(qw[:], q_words[0].rearrange("o g q r -> g o (q r)").bitcast(I32))
-        zeros = big.tile([P, N // 4], I32, name="zeros", offset=4 * T - N // 2)
-        nc.vector.memset(zeros[:], 0)
-        nc.vector.memset(ks_pool[:].bitcast(I32), 0)
-        ks_rows = k_scales.bitcast(I32).rearrange("o (a i) c -> i a o c", i=4)
-        for i in range(4):
-            nc.sync.dma_start(ks_pool[:].bitcast(I32)[i:P:SHIFT, :], ks_rows[i])
-        nc.vector.tensor_copy(ks_second[:].bitcast(I32), zeros[:])
-        make_identity(nc, ident[:])
-        nc.vector.tensor_copy(qs[:].bitcast(I32), zeros[:, 0 : PASSES * NQ // 4])
-        kw_pool = big.tile([P, T], I32, name="kw_pool", offset=0)
+        nc.sync.dma_start(ks_pool[:].bitcast(I32)[last:P, 0 : T // 4], k_scales.bitcast(I32).rearrange("o f c -> f o c"))
+        nc.sync.dma_start(vs_pool[P - 1 : P, :], vs[0:1, :])
+        nc.sync.dma_start(staged[:].bitcast(I32)[last:P, N // 4 :], q_scales[0].bitcast(I32).rearrange("o f c -> f o c"))
         nc.sync.dma_start(kw_pool[:], k_words[0].rearrange("g t r -> g (t r)").bitcast(I32))
-        nc.vector.memset(vs_pool[0 : P - 1, :].bitcast(I32), 0)
-        qs_rows = q_scales[0].bitcast(I32).rearrange("o (a i) c -> i a o c", i=4)
-        for i in range(4):
-            nc.sync.dma_start(qs[:].bitcast(I32)[i:P:32, :].rearrange("a (o c) -> a o c", o=PASSES), qs_rows[i])
-        v_pool = big.tile([P, T], F32, name="v_pool", offset=4 * T)
+        nc.sync.dma_start(qw[:], q_words[0].rearrange("o g q r -> g o (q r)").bitcast(I32))
         nc.sync.dma_start(v_pool[:], vT)
+        nc.vector.memset(warm_in[:], 0.0)
+        nc.vector.memset(ks_pool[:].bitcast(I32)[0:last, :], 0)
+        nc.vector.memset(planes[:].bitcast(I32), 0)
+        nc.gpsimd.memset(vs_pool[0 : P - 1, :].bitcast(I32), 0)
+        make_identity(nc, ident[:])
+        nc.scalar.activation(warm[:], warm_in[:], ACT.Silu)
 
-        nc.vector.tensor_copy(vs_g[:], vs_pool[:].indirect(offsets[:]))
-        for t in range(PACK):
-            nc.tensor.transpose(vs_t[:, t, :], vs_g[:, t:N:PACK], ident[:])
-        nc.vector.tensor_copy(ks_g[:], ks_pool[:].indirect(offsets[:]))
+        nc.vector.tensor_copy(ks_g[:], ks_pool[:, 0:T].indirect(offsets[:]))
         nc.vector.tensor_copy(
-            ks_first[:].rearrange("p (t m) -> p t m", t=PACK), ks_g[:].rearrange("p (m t) -> p t m", t=PACK)
+            staged[:].bitcast(I32)[last:P, 0 : N // 4].rearrange("p (t b w) -> p t b w", t=PACK, w=RUN // 4),
+            ks_g[:].bitcast(I32)[last:P, :].rearrange("p (b t w) -> p t b w", t=PACK, w=RUN // 4),
         )
-        nc.scalar.dma_start(ks_second[:].bitcast(I32)[0 : P - SHIFT, :], ks_first[:].bitcast(I32)[SHIFT:P, :])
-        kw_g = big.tile([P, N], U32, name="kw_g", offset=12 * T)
-        nc.vector.tensor_copy(kw_g[:].rearrange("p (t m) -> p m t", t=PACK), kw_pool[:].bitcast(U32).indirect(offsets[:]))
+        for a in range(P // QUAD):
+            nc.scalar.dma_start(
+                planes[:].bitcast(I32)[a * QUAD : a * QUAD + ROWS, 0 : PASSES * (N + NQ) // 4].rearrange("i (o c) -> i o c", o=PASSES),
+                staged[:].bitcast(I32)[last + a * ROWS * PASSES : last + (a + 1) * ROWS * PASSES, :],
+            )
+        nc.vector.tensor_copy(vs_g[:], vs_pool[:].indirect(offsets[:]))
+        nc.scalar.copy(
+            vs_dealt[:].rearrange("p (t b j) -> p t b j", t=PACK, j=RUN),
+            vs_g[:].rearrange("p (b t j) -> p t b j", t=PACK, j=RUN),
+        )
+        for t in range(PACK):
+            nc.tensor.transpose(vs_t[:, t, :], vs_dealt[:, t * P : (t + 1) * P], ident[:])
 
-        k_codes = big.tile([P, PASSES * N * 2], U8, name="k_codes", offset=13 * T, align_bytes=64)
-        halves_in = kw_g[:].bitcast(U16).rearrange("p (c o) -> p o c", o=PASSES)
-        halves_out = k_codes[:].bitcast(U16).rearrange("p (o c) -> p o c", o=PASSES)
-        for o in range(PASSES):
-            nc.vector.tensor_copy(halves_out[:, o, :], halves_in[:, o, :])
-
-        k_planes = [ks_first, ks_second]
-        for o in range(PASSES):
-            for t in range(PACK):
-                start = (o * N + t * P) * 2
+        nc.vector.tensor_copy(kw_g[:], kw_pool[:].bitcast(U32).indirect(offsets[:]))
+        halves = kw_g[:].bitcast(U16).rearrange("p (b t j o) -> p t o b j", t=PACK, j=RUN, o=PASSES)
+        for t in range(PACK):
+            nc.vector.tensor_copy(
+                k_codes[t][:].bitcast(U16).rearrange("p (o b j) -> p o b j", o=PASSES, j=RUN), halves[:, t]
+            )
+            for o in range(PASSES):
                 nc.tensor.matmul_mx(
                     out=scores[t][:],
-                    lhsT=k_codes[:, start : start + 2 * P].bitcast(FP4X4),
-                    lhsT_scale=k_planes[o][:, t * P : (t + 1) * P],
+                    lhsT=k_codes[t][:, o * 2 * P : (o + 1) * 2 * P].bitcast(FP4X4),
+                    lhsT_scale=planes[:, o * (N + NQ) + t * P : o * (N + NQ) + (t + 1) * P],
                     rhs=qw[:, o, :].bitcast(FP8X4),
-                    rhs_scale=qs[:, o * NQ : (o + 1) * NQ],
+                    rhs_scale=planes[:, o * (N + NQ) + N : (o + 1) * (N + NQ)],
                     start=(o == 0),
                     stop=(o == PASSES - 1),
                 )
-        for t in range(PACK):
             nc.scalar.activation(p_sb[:, t, :], scores[t][:], ACT.Silu)
 
-        v_g = big.tile([P, N], BF16, name="v_g", offset=12 * T)
-        nc.vector.tensor_copy(v_g[:].rearrange("p (u m r) -> p m u r", u=2, r=2), v_pool[:].indirect(offsets[:]))
+        nc.vector.tensor_copy(
+            v_g[:].rearrange("p (u b j r) -> p b u r j", u=2, j=RUN, r=2), v_pool[:].indirect(offsets[:])
+        )
         nc.vector.tensor_tensor(
             w_in[:],
             p_sb[:].rearrange("p t q -> p q t"),
             vs_t[:, :, P - 1 : P].rearrange("p t a -> p a t").to_broadcast([P, NQ, PACK]),
             ALU.mult,
         )
-        v_t = ps.tile([P, 2, DV], F32, name="v_t", tag="bank0")
         v_words = v_g[:].bitcast(F32)
         for u in range(2):
             nc.tensor.transpose(v_t[:, u, :], v_words[:, u * P : (u + 1) * P], ident[:])

@@ -25,6 +25,7 @@ PACK = 4
 RUN = 8
 QUAD = 32
 ROWS = 4
+EARLY = 1024
 
 FLOPS = 2 * NQ * N * D + 2 * NQ * N * DV
 BYTES = 2 * 128 * 128 * 4 + 2 * 16 * 128 + 128 * T * 4 + 2 * 16 * T + DV * T * 4 + T * 4 + 128 * 32 * 2 + NQ * DV * 4
@@ -34,18 +35,19 @@ def tile_attend_silu_topkq128n512t2048_kernel(tc, q_words, q_scales, k_words, k_
     nc = tc.nc
     with ExitStack() as ctx:
         sb = ctx.enter_context(tc.tile_pool(name="sb", bufs=1))
+        big = ctx.enter_context(tc.tile_pool(name="big", bufs=1))
         ps = ctx.enter_context(tc.psum_pool(name="ps", bufs=1))
 
         offsets = sb.tile([P, N // 16], U16, name="offsets")
         ks_pool = sb.tile([P, T + 4], U8, name="ks_pool")
         vs_pool = sb.tile([P, T], F32, name="vs_pool")
         kw_pool = sb.tile([P, T], I32, name="kw_pool")
-        v_pool = sb.tile([P, T], F32, name="v_pool")
+        v_early = big.tile([P, EARLY], F32, name="v_early", offset=4 * T)
         qw = sb.tile([P, PASSES, NQ], I32, name="qw", align_bytes=64)
         ident = sb.tile([P, P], F32, name="ident", align_bytes=64)
         warm = sb.tile([P, 1], F32, name="warm")
         warm_in = sb.tile([P, 1], F32, name="warm_in")
-        ks_g = sb.tile([P, N], U8, name="ks_g", align_bytes=64)
+        ks_g = big.tile([P, N], U8, name="ks_g", offset=4 * T - N)
         staged = sb.tile([P, N + NQ], U8, name="staged", align_bytes=64)
         planes = sb.tile([P, PASSES * (N + NQ) + 4], U8, name="planes", align_bytes=64)
         vs_g = sb.tile([P, N], F32, name="vs_g", align_bytes=64)
@@ -53,8 +55,6 @@ def tile_attend_silu_topkq128n512t2048_kernel(tc, q_words, q_scales, k_words, k_
         kw_g = sb.tile([P, N], U32, name="kw_g", align_bytes=64)
         k_codes = [sb.tile([P, PASSES * P * 2], U8, name="k_codes%d" % t, align_bytes=64) for t in range(PACK)]
         v_g = sb.tile([P, N], BF16, name="v_g", align_bytes=64)
-        p_sb = sb.tile([P, PACK, NQ], F32, name="p_sb", align_bytes=64)
-        w_in = sb.tile([P, NQ, PACK], BF16, name="w_in", align_bytes=64)
         v_in = sb.tile([P, DV, PACK], BF16, name="v_in", align_bytes=64)
         w_codes = sb.tile([P, NQ], U32, name="w_codes", align_bytes=64)
         w_scales = sb.tile([P, NQ], U8, name="w_scales", align_bytes=64)
@@ -62,9 +62,8 @@ def tile_attend_silu_topkq128n512t2048_kernel(tc, q_words, q_scales, k_words, k_
         v_scales = sb.tile([P, DV], U8, name="v_scales", align_bytes=64)
         y_sb = sb.tile([P, DV], F32, name="y_sb", align_bytes=64)
 
-        scores = [ps.tile([P, NQ], F32, name="score%d" % t) for t in range(PACK)]
+        scores = [ps.tile([P, NQ], F32, name="score%d" % t, tag="bank%d" % t) for t in range(PACK)]
         vs_t = ps.tile([P, PACK, P], F32, name="vs_t")
-        v_t = ps.tile([P, 2, DV], F32, name="v_t")
         y_ps = ps.tile([P, DV], F32, name="y_ps")
 
         last = P - QUAD
@@ -74,7 +73,7 @@ def tile_attend_silu_topkq128n512t2048_kernel(tc, q_words, q_scales, k_words, k_
         nc.sync.dma_start(staged[:].bitcast(I32)[last:P, N // 4 :], q_scales[0].bitcast(I32).rearrange("o f c -> f o c"))
         nc.sync.dma_start(kw_pool[:], k_words[0].rearrange("g t r -> g (t r)").bitcast(I32))
         nc.sync.dma_start(qw[:], q_words[0].rearrange("o g q r -> g o (q r)").bitcast(I32))
-        nc.sync.dma_start(v_pool[:], vT)
+        nc.sync.dma_start(v_early[:], vT[:, 0:EARLY])
         nc.vector.memset(warm_in[:], 0.0)
         nc.vector.memset(ks_pool[:].bitcast(I32)[0:last, :], 0)
         nc.vector.memset(planes[:].bitcast(I32), 0)
@@ -87,11 +86,13 @@ def tile_attend_silu_topkq128n512t2048_kernel(tc, q_words, q_scales, k_words, k_
             staged[:].bitcast(I32)[last:P, 0 : N // 4].rearrange("p (t b w) -> p t b w", t=PACK, w=RUN // 4),
             ks_g[:].bitcast(I32)[last:P, :].rearrange("p (b t w) -> p t b w", t=PACK, w=RUN // 4),
         )
+        v_pool = big.tile([P, T], F32, name="v_pool", offset=0)
         for a in range(P // QUAD):
-            nc.scalar.dma_start(
+            nc.sync.dma_start(
                 planes[:].bitcast(I32)[a * QUAD : a * QUAD + ROWS, 0 : PASSES * (N + NQ) // 4].rearrange("i (o c) -> i o c", o=PASSES),
                 staged[:].bitcast(I32)[last + a * ROWS * PASSES : last + (a + 1) * ROWS * PASSES, :],
             )
+        nc.sync.dma_start(v_pool[:, EARLY:T], vT[:, EARLY:T])
         nc.vector.tensor_copy(vs_g[:], vs_pool[:].indirect(offsets[:]))
         nc.scalar.copy(
             vs_dealt[:].rearrange("p (t b j) -> p t b j", t=PACK, j=RUN),
@@ -100,6 +101,8 @@ def tile_attend_silu_topkq128n512t2048_kernel(tc, q_words, q_scales, k_words, k_
         for t in range(PACK):
             nc.tensor.transpose(vs_t[:, t, :], vs_dealt[:, t * P : (t + 1) * P], ident[:])
 
+        nc.scalar.copy(v_pool[:, 0:EARLY], v_early[:])
+        p_sb = big.tile([P, PACK, NQ], F32, name="p_sb", offset=4 * T)
         nc.vector.tensor_copy(kw_g[:], kw_pool[:].bitcast(U32).indirect(offsets[:]))
         halves = kw_g[:].bitcast(U16).rearrange("p (b t j o) -> p t o b j", t=PACK, j=RUN, o=PASSES)
         for t in range(PACK):
@@ -121,12 +124,14 @@ def tile_attend_silu_topkq128n512t2048_kernel(tc, q_words, q_scales, k_words, k_
         nc.vector.tensor_copy(
             v_g[:].rearrange("p (u b j r) -> p b u r j", u=2, j=RUN, r=2), v_pool[:].indirect(offsets[:])
         )
+        w_in = big.tile([P, NQ, PACK], BF16, name="w_in", offset=0, align_bytes=64)
         nc.vector.tensor_tensor(
             w_in[:],
             p_sb[:].rearrange("p t q -> p q t"),
             vs_t[:, :, P - 1 : P].rearrange("p t a -> p a t").to_broadcast([P, NQ, PACK]),
             ALU.mult,
         )
+        v_t = ps.tile([P, 2, DV], F32, name="v_t", tag="bank0")
         v_words = v_g[:].bitcast(F32)
         for u in range(2):
             nc.tensor.transpose(v_t[:, u, :], v_words[:, u * P : (u + 1) * P], ident[:])

@@ -51,7 +51,6 @@ def tile_attend_silu_topkq128n512t2048_kernel(tc, q_words, q_scales, k_words, k_
         staged = sb.tile([P, N + NQ], U8, name="staged", align_bytes=64)
         planes = sb.tile([P, PASSES * (N + NQ) + 4], U8, name="planes", align_bytes=64)
         vs_g = sb.tile([P, N], F32, name="vs_g", align_bytes=64)
-        vs_dealt = sb.tile([P, N], F32, name="vs_dealt", align_bytes=64)
         kw_g = sb.tile([P, N], U32, name="kw_g", align_bytes=64)
         k_codes = [sb.tile([P, PASSES * P * 2], U8, name="k_codes%d" % t, align_bytes=64) for t in range(PACK)]
         v_g = sb.tile([P, N], BF16, name="v_g", align_bytes=64)
@@ -93,13 +92,12 @@ def tile_attend_silu_topkq128n512t2048_kernel(tc, q_words, q_scales, k_words, k_
                 staged[:].bitcast(I32)[last + a * ROWS * PASSES : last + (a + 1) * ROWS * PASSES, :],
             )
         nc.sync.dma_start(v_pool[:, EARLY:T], vT[:, EARLY:T])
-        nc.vector.tensor_copy(vs_g[:], vs_pool[:].indirect(offsets[:]))
-        nc.scalar.copy(
-            vs_dealt[:].rearrange("p (t b j) -> p t b j", t=PACK, j=RUN),
-            vs_g[:].rearrange("p (b t j) -> p t b j", t=PACK, j=RUN),
+        nc.vector.tensor_copy(
+            vs_g[:].bitcast(U32).rearrange("p (t b j) -> p b t j", t=PACK, j=RUN),
+            vs_pool[:].bitcast(U32).indirect(offsets[:]),
         )
         for t in range(PACK):
-            nc.tensor.transpose(vs_t[:, t, :], vs_dealt[:, t * P : (t + 1) * P], ident[:])
+            nc.tensor.transpose(vs_t[:, t, :], vs_g[:, t * P : (t + 1) * P], ident[:])
 
         nc.scalar.copy(v_pool[:, 0:EARLY], v_early[:])
         p_sb = big.tile([P, PACK, NQ], F32, name="p_sb", offset=4 * T)

@@ -52,7 +52,7 @@ def tile_attend_silu_topkq128n512t2048_kernel(tc, q_words, q_scales, k_words, k_
         planes = sb.tile([P, PASSES * (N + NQ) + 4], U8, name="planes", align_bytes=64)
         vs_g = sb.tile([P, N], F32, name="vs_g", align_bytes=64)
         kw_g = sb.tile([P, N], U32, name="kw_g", align_bytes=64)
-        k_codes = [sb.tile([P, PASSES * P * 2], U8, name="k_codes%d" % t, align_bytes=64) for t in range(PACK)]
+        k_codes = sb.tile([P, PACK * PASSES * P * 2], U8, name="k_codes", align_bytes=64)
         v_g = sb.tile([P, N], BF16, name="v_g", align_bytes=64)
         v_in = sb.tile([P, DV, PACK], BF16, name="v_in", align_bytes=64)
         w_codes = sb.tile([P, NQ], U32, name="w_codes", align_bytes=64)
@@ -82,12 +82,12 @@ def tile_attend_silu_topkq128n512t2048_kernel(tc, q_words, q_scales, k_words, k_
 
         nc.vector.tensor_copy(ks_g[:], ks_pool[:, 0:T].indirect(offsets[:]))
         nc.vector.tensor_copy(
-            staged[:].bitcast(I32)[last:P, 0 : N // 4].rearrange("p (t b w) -> p t b w", t=PACK, w=RUN // 4),
-            ks_g[:].bitcast(I32)[last:P, :].rearrange("p (b t w) -> p t b w", t=PACK, w=RUN // 4),
+            staged[:].bitcast(I32)[:, 0 : N // 4].rearrange("p (t b w) -> p t b w", t=PACK, w=RUN // 4),
+            ks_g[:].bitcast(I32).rearrange("p (b t w) -> p t b w", t=PACK, w=RUN // 4),
         )
         v_pool = big.tile([P, T], F32, name="v_pool", offset=0)
         for a in range(P // QUAD):
-            nc.sync.dma_start(
+            (nc.sync, nc.sync, nc.sync, nc.sync)[a].dma_start(
                 planes[:].bitcast(I32)[a * QUAD : a * QUAD + ROWS, 0 : PASSES * (N + NQ) // 4].rearrange("i (o c) -> i o c", o=PASSES),
                 staged[:].bitcast(I32)[last + a * ROWS * PASSES : last + (a + 1) * ROWS * PASSES, :],
             )
@@ -101,16 +101,20 @@ def tile_attend_silu_topkq128n512t2048_kernel(tc, q_words, q_scales, k_words, k_
 
         nc.scalar.copy(v_pool[:, 0:EARLY], v_early[:])
         p_sb = big.tile([P, PACK, NQ], F32, name="p_sb", offset=4 * T)
-        nc.vector.tensor_copy(kw_g[:], kw_pool[:].bitcast(U32).indirect(offsets[:]))
-        halves = kw_g[:].bitcast(U16).rearrange("p (b t j o) -> p t o b j", t=PACK, j=RUN, o=PASSES)
-        for t in range(PACK):
+        for h in range(2):
             nc.vector.tensor_copy(
-                k_codes[t][:].bitcast(U16).rearrange("p (o b j) -> p o b j", o=PASSES, j=RUN), halves[:, t]
+                kw_g[:, h * N // 2 : (h + 1) * N // 2],
+                kw_pool[:].bitcast(U32).indirect(offsets[:, h * N // 32 : (h + 1) * N // 32]),
             )
+        halves = kw_g[:].bitcast(U16).rearrange("p (h b t j o) -> p h t o b j", h=2, t=PACK, j=RUN, o=PASSES)
+        parted = k_codes[:].bitcast(U16).rearrange("p (t o h b j) -> p h t o b j", h=2, t=PACK, j=RUN, o=PASSES)
+        nc.vector.tensor_copy(parted[:, 0], halves[:, 0])
+        for t in range(PACK):
+            nc.vector.tensor_copy(parted[:, 1, t], halves[:, 1, t])
             for o in range(PASSES):
                 nc.tensor.matmul_mx(
                     out=scores[t][:],
-                    lhsT=k_codes[t][:, o * 2 * P : (o + 1) * 2 * P].bitcast(FP4X4),
+                    lhsT=k_codes[:, (t * PASSES + o) * 2 * P : (t * PASSES + o + 1) * 2 * P].bitcast(FP4X4),
                     lhsT_scale=planes[:, o * (N + NQ) + t * P : o * (N + NQ) + (t + 1) * P],
                     rhs=qw[:, o, :].bitcast(FP8X4),
                     rhs_scale=planes[:, o * (N + NQ) + N : (o + 1) * (N + NQ)],
@@ -123,18 +127,16 @@ def tile_attend_silu_topkq128n512t2048_kernel(tc, q_words, q_scales, k_words, k_
             v_g[:].rearrange("p (u b j r) -> p b u r j", u=2, j=RUN, r=2), v_pool[:].indirect(offsets[:])
         )
         w_in = big.tile([P, NQ, PACK], BF16, name="w_in", offset=0, align_bytes=64)
-        nc.vector.tensor_tensor(
-            w_in[:],
-            p_sb[:].rearrange("p t q -> p q t"),
-            vs_t[:, :, P - 1 : P].rearrange("p t a -> p a t").to_broadcast([P, NQ, PACK]),
-            ALU.mult,
-        )
+        spans = [slice(h * NQ // 2, (h + 1) * NQ // 2) for h in range(2)]
+        for qs in spans:
+            nc.vector.tensor_tensor(w_in[:, qs, :], p_sb[:, :, qs].rearrange("p t q -> p q t"), vs_t[:, :, P - 1 : P].rearrange("p t a -> p a t").to_broadcast([P, NQ // 2, PACK]), ALU.mult)
         v_t = ps.tile([P, 2, DV], F32, name="v_t", tag="bank0")
         v_words = v_g[:].bitcast(F32)
         for u in range(2):
             nc.tensor.transpose(v_t[:, u, :], v_words[:, u * P : (u + 1) * P], ident[:])
         nc.scalar.copy(v_in[:].bitcast(F32), v_t[:].rearrange("p u e -> p e u"))
-        nc.vector.quantize_mx(out=w_codes[:].bitcast(FP8X4), scales=w_scales[:], in_=w_in[:].rearrange("p q t -> p (q t)"))
+        for qs in spans:
+            nc.vector.quantize_mx(out=w_codes[:, qs].bitcast(FP8X4), scales=w_scales[:, qs], in_=w_in[:, qs, :].rearrange("p q t -> p (q t)"))
         nc.vector.quantize_mx(out=v_codes[:].bitcast(FP8X4), scales=v_scales[:], in_=v_in[:].rearrange("p e t -> p (e t)"))
         nc.tensor.matmul_mx(
             out=y_ps[:],

@@ -134,10 +134,12 @@ def tile_attend_silu_topkq128n512t2048_kernel(tc, q_words, q_scales, k_words, k_
         v_words = v_g[:].bitcast(F32)
         for u in range(2):
             nc.tensor.transpose(v_t[:, u, :], v_words[:, u * P : (u + 1) * P], ident[:])
-        nc.scalar.copy(v_in[:].bitcast(F32), v_t[:].rearrange("p u e -> p e u"))
+        for es in spans:
+            nc.scalar.copy(v_in[:, es, :].bitcast(F32), v_t[:, :, es].rearrange("p u e -> p e u"))
         for qs in spans:
             nc.vector.quantize_mx(out=w_codes[:, qs].bitcast(FP8X4), scales=w_scales[:, qs], in_=w_in[:, qs, :].rearrange("p q t -> p (q t)"))
-        nc.vector.quantize_mx(out=v_codes[:].bitcast(FP8X4), scales=v_scales[:], in_=v_in[:].rearrange("p e t -> p (e t)"))
+        for es in spans:
+            nc.vector.quantize_mx(out=v_codes[:, es].bitcast(FP8X4), scales=v_scales[:, es], in_=v_in[:, es, :].rearrange("p e t -> p (e t)"))
         nc.tensor.matmul_mx(
             out=y_ps[:],
             lhsT=w_codes[:].bitcast(FP8X4),

@@ -63,7 +63,7 @@ def tile_attend_silu_topkq128n512t2048_kernel(tc, q_words, q_scales, k_words, k_
 
         scores = [ps.tile([P, NQ], F32, name="score%d" % t, tag="bank%d" % t) for t in range(PACK)]
         vs_t = ps.tile([P, PACK, P], F32, name="vs_t")
-        y_ps = ps.tile([P, DV], F32, name="y_ps")
+        y_ps = [ps.tile([P, DV // 2], F32, name="y_ps%d" % h) for h in range(2)]
 
         last = P - QUAD
         nc.sync.dma_start(offsets[:], offs)
@@ -140,14 +140,16 @@ def tile_attend_silu_topkq128n512t2048_kernel(tc, q_words, q_scales, k_words, k_
             nc.vector.quantize_mx(out=w_codes[:, qs].bitcast(FP8X4), scales=w_scales[:, qs], in_=w_in[:, qs, :].rearrange("p q t -> p (q t)"))
         for es in spans:
             nc.vector.quantize_mx(out=v_codes[:, es].bitcast(FP8X4), scales=v_scales[:, es], in_=v_in[:, es, :].rearrange("p e t -> p (e t)"))
-        nc.tensor.matmul_mx(
-            out=y_ps[:],
-            lhsT=w_codes[:].bitcast(FP8X4),
-            lhsT_scale=w_scales[:],
-            rhs=v_codes[:].bitcast(FP8X4),
-            rhs_scale=v_scales[:],
-            start=True,
-            stop=True,
-        )
-        nc.vector.tensor_scalar(y_sb[:], y_ps[:], 1.0 / 16.0, None, ALU.mult)
+        for h, es in enumerate(spans):
+            nc.tensor.matmul_mx(
+                out=y_ps[h][:],
+                lhsT=w_codes[:].bitcast(FP8X4),
+                lhsT_scale=w_scales[:],
+                rhs=v_codes[:, es].bitcast(FP8X4),
+                rhs_scale=v_scales[:, es],
+                start=True,
+                stop=True,
+            )
+        nc.vector.tensor_scalar(y_sb[:, spans[0]], y_ps[0][:], 1.0 / 16.0, None, ALU.mult)
+        nc.scalar.activation(y_sb[:, spans[1]], y_ps[1][:], ACT.Copy, scale=1.0 / 16.0)
         nc.sync.dma_start(out[0], y_sb[:])

@@ -61,7 +61,7 @@ def tile_attend_silu_topkq128n512t2048_kernel(tc, q_words, q_scales, k_words, k_
         v_scales = sb.tile([P, DV], U8, name="v_scales", align_bytes=64)
         y_sb = sb.tile([P, DV], F32, name="y_sb", align_bytes=64)
 
-        scores = [ps.tile([P, NQ], F32, name="score%d" % t, tag="bank%d" % t) for t in range(PACK)]
+        scores = [ps.tile([P, 2, NQ], F32, name="score%d" % u, tag="bank%d" % u) for u in range(2)]
         vs_t = ps.tile([P, PACK, P], F32, name="vs_t")
         y_ps = [ps.tile([P, DV // 2], F32, name="y_ps%d" % h) for h in range(2)]
 
@@ -100,7 +100,7 @@ def tile_attend_silu_topkq128n512t2048_kernel(tc, q_words, q_scales, k_words, k_
             nc.tensor.transpose(vs_t[:, t, :], vs_g[:, t * P : (t + 1) * P], ident[:])
 
         nc.scalar.copy(v_pool[:, 0:EARLY], v_early[:])
-        p_sb = big.tile([P, PACK, NQ], F32, name="p_sb", offset=4 * T)
+        p_sb = big.tile([P, 2, NQ, 2], F32, name="p_sb", offset=4 * T)
         for h in range(2):
             nc.vector.tensor_copy(
                 kw_g[:, h * N // 2 : (h + 1) * N // 2],
@@ -113,7 +113,7 @@ def tile_attend_silu_topkq128n512t2048_kernel(tc, q_words, q_scales, k_words, k_
             nc.vector.tensor_copy(parted[:, 1, t], halves[:, 1, t])
             for o in range(PASSES):
                 nc.tensor.matmul_mx(
-                    out=scores[t][:],
+                    out=scores[t // 2][:, t % 2, :],
                     lhsT=k_codes[:, (t * PASSES + o) * 2 * P : (t * PASSES + o + 1) * 2 * P].bitcast(FP4X4),
                     lhsT_scale=planes[:, o * (N + NQ) + t * P : o * (N + NQ) + (t + 1) * P],
                     rhs=qw[:, o, :].bitcast(FP8X4),
@@ -121,7 +121,8 @@ def tile_attend_silu_topkq128n512t2048_kernel(tc, q_words, q_scales, k_words, k_
                     start=(o == 0),
                     stop=(o == PASSES - 1),
                 )
-            nc.scalar.activation(p_sb[:, t, :], scores[t][:], ACT.Silu)
+            if t % 2 == 1:
+                nc.scalar.activation(p_sb[:, t // 2], scores[t // 2][:].rearrange("p r q -> p q r"), ACT.Silu)
 
         nc.vector.tensor_copy(
             v_g[:].rearrange("p (u b j r) -> p b u r j", u=2, j=RUN, r=2), v_pool[:].indirect(offsets[:])
@@ -129,7 +130,7 @@ def tile_attend_silu_topkq128n512t2048_kernel(tc, q_words, q_scales, k_words, k_
         w_in = big.tile([P, NQ, PACK], BF16, name="w_in", offset=0, align_bytes=64)
         spans = [slice(h * NQ // 2, (h + 1) * NQ // 2) for h in range(2)]
         for qs in spans:
-            nc.vector.tensor_tensor(w_in[:, qs, :], p_sb[:, :, qs].rearrange("p t q -> p q t"), vs_t[:, :, P - 1 : P].rearrange("p t a -> p a t").to_broadcast([P, NQ // 2, PACK]), ALU.mult)
+            nc.vector.tensor_tensor(w_in[:, qs, :].rearrange("p q (u r) -> p q u r", r=2), p_sb[:, :, qs, :].rearrange("p u q r -> p q u r"), vs_t[:, :, P - 1 : P].rearrange("p t a -> p a t").to_broadcast([P, NQ // 2, PACK]).rearrange("p q (u r) -> p q u r", r=2), ALU.mult)
         v_t = ps.tile([P, 2, DV], F32, name="v_t", tag="bank0")
         v_words = v_g[:].bitcast(F32)
         for u in range(2):

@@ -62,7 +62,7 @@ def tile_attend_silu_topkq128n512t2048_kernel(tc, q_words, q_scales, k_words, k_
         y_sb = sb.tile([P, DV], F32, name="y_sb", align_bytes=64)
 
         scores = [ps.tile([P, 2, NQ], F32, name="score%d" % u, tag="bank%d" % u) for u in range(2)]
-        vs_t = ps.tile([P, PACK, P], F32, name="vs_t")
+        vs_t = ps.tile([P, N], F32, name="vs_t")
         y_ps = [ps.tile([P, DV // 2], F32, name="y_ps%d" % h) for h in range(2)]
 
         last = P - QUAD
@@ -96,8 +96,8 @@ def tile_attend_silu_topkq128n512t2048_kernel(tc, q_words, q_scales, k_words, k_
             vs_g[:].bitcast(U32).rearrange("p (t b j) -> p b t j", t=PACK, j=RUN),
             vs_pool[:].bitcast(U32).indirect(offsets[:]),
         )
-        for t in range(PACK):
-            nc.tensor.transpose(vs_t[:, t, :], vs_g[:, t * P : (t + 1) * P], ident[:])
+        for t in reversed(range(PACK)):
+            nc.tensor.transpose(vs_t[:, t : t + P], vs_g[:, t * P : (t + 1) * P], ident[:])
 
         nc.scalar.copy(v_pool[:, 0:EARLY], v_early[:])
         p_sb = big.tile([P, 2, NQ, 2], F32, name="p_sb", offset=4 * T)
@@ -130,7 +130,7 @@ def tile_attend_silu_topkq128n512t2048_kernel(tc, q_words, q_scales, k_words, k_
         w_in = big.tile([P, NQ, PACK], BF16, name="w_in", offset=0, align_bytes=64)
         spans = [slice(h * NQ // 2, (h + 1) * NQ // 2) for h in range(2)]
         for qs in spans:
-            nc.vector.tensor_tensor(w_in[:, qs, :].rearrange("p q (u r) -> p q u r", r=2), p_sb[:, :, qs, :].rearrange("p u q r -> p q u r"), vs_t[:, :, P - 1 : P].rearrange("p t a -> p a t").to_broadcast([P, NQ // 2, PACK]).rearrange("p q (u r) -> p q u r", r=2), ALU.mult)
+            nc.vector.tensor_tensor(w_in[:, qs, :].rearrange("p q (u r) -> p q u r", r=2), p_sb[:, :, qs, :].rearrange("p u q r -> p q u r"), vs_t[:, P - 1 : P - 1 + PACK].unsqueeze(1).to_broadcast([P, NQ // 2, PACK]).rearrange("p q (u r) -> p q u r", r=2), ALU.mult)
         v_t = ps.tile([P, 2, DV], F32, name="v_t", tag="bank0")
         v_words = v_g[:].bitcast(F32)
         for u in range(2):

@@ -151,6 +151,6 @@ def tile_attend_silu_topkq128n512t2048_kernel(tc, q_words, q_scales, k_words, k_
                 start=True,
                 stop=True,
             )
-        nc.vector.tensor_scalar(y_sb[:, spans[0]], y_ps[0][:], 1.0 / 16.0, None, ALU.mult)
+        nc.scalar.activation(y_sb[:, spans[0]], y_ps[0][:], ACT.Copy, scale=1.0 / 16.0)
         nc.scalar.activation(y_sb[:, spans[1]], y_ps[1][:], ACT.Copy, scale=1.0 / 16.0)
         nc.sync.dma_start(out[0], y_sb[:])

@@ -39,17 +39,17 @@ def tile_attend_silu_topkq128n512t2048_kernel(tc, q_words, q_scales, k_words, k_
         ps = ctx.enter_context(tc.psum_pool(name="ps", bufs=1))
 
         offsets = sb.tile([P, N // 16], U16, name="offsets")
-        ks_pool = sb.tile([P, T + 4], U8, name="ks_pool")
-        vs_pool = sb.tile([P, T], F32, name="vs_pool")
-        kw_pool = sb.tile([P, T], I32, name="kw_pool")
-        v_early = big.tile([P, EARLY], F32, name="v_early", offset=4 * T)
-        qw = sb.tile([P, PASSES, NQ], I32, name="qw", align_bytes=64)
+        ks_pool = sb.tile([P, T + 4], U8, name="ks_pool", align_bytes=256)
+        vs_pool = sb.tile([P, T], F32, name="vs_pool", align_bytes=256)
+        kw_pool = sb.tile([P, T], I32, name="kw_pool", align_bytes=256)
+        v_early = big.tile([P, EARLY], F32, name="v_early", offset=4 * T, align_bytes=256)
+        qw = sb.tile([P, PASSES, NQ], I32, name="qw", align_bytes=256)
         ident = sb.tile([P, P], F32, name="ident", align_bytes=64)
         warm = sb.tile([P, 1], F32, name="warm")
         warm_in = sb.tile([P, 1], F32, name="warm_in")
         ks_g = big.tile([P, N], U8, name="ks_g", offset=4 * T - N)
-        staged = sb.tile([P, N + NQ], U8, name="staged", align_bytes=64)
-        planes = sb.tile([P, PASSES * (N + NQ) + 4], U8, name="planes", align_bytes=64)
+        staged = sb.tile([P, N + NQ], U8, name="staged", align_bytes=256)
+        planes = sb.tile([P, PASSES * (N + NQ) + 4], U8, name="planes", align_bytes=256)
         vs_g = sb.tile([P, N], F32, name="vs_g", align_bytes=64)
         kw_g = sb.tile([P, N], U32, name="kw_g", align_bytes=64)
         k_codes = sb.tile([P, PACK * PASSES * P * 2], U8, name="k_codes", align_bytes=64)
@@ -59,7 +59,7 @@ def tile_attend_silu_topkq128n512t2048_kernel(tc, q_words, q_scales, k_words, k_
         w_scales = sb.tile([P, NQ], U8, name="w_scales", align_bytes=64)
         v_codes = sb.tile([P, DV], U32, name="v_codes", align_bytes=64)
         v_scales = sb.tile([P, DV], U8, name="v_scales", align_bytes=64)
-        y_sb = sb.tile([P, DV], F32, name="y_sb", align_bytes=64)
+        y_sb = sb.tile([P, DV], F32, name="y_sb", align_bytes=256)
 
         scores = [ps.tile([P, 2, NQ], F32, name="score%d" % u, tag="bank%d" % u) for u in range(2)]
         vs_t = ps.tile([P, N], F32, name="vs_t")
@@ -85,7 +85,7 @@ def tile_attend_silu_topkq128n512t2048_kernel(tc, q_words, q_scales, k_words, k_
             staged[:].bitcast(I32)[:, 0 : N // 4].rearrange("p (t b w) -> p t b w", t=PACK, w=RUN // 4),
             ks_g[:].bitcast(I32).rearrange("p (b t w) -> p t b w", t=PACK, w=RUN // 4),
         )
-        v_pool = big.tile([P, T], F32, name="v_pool", offset=0)
+        v_pool = big.tile([P, T], F32, name="v_pool", offset=0, align_bytes=256)
         for a in range(P // QUAD):
             (nc.sync, nc.sync, nc.sync, nc.sync)[a].dma_start(
                 planes[:].bitcast(I32)[a * QUAD : a * QUAD + ROWS, 0 : PASSES * (N + NQ) // 4].rearrange("i (o c) -> i o c", o=PASSES),

@@ -42,12 +42,12 @@ def tile_attend_silu_topkq128n512t2048_kernel(tc, q_words, q_scales, k_words, k_
         ks_pool = sb.tile([P, T + 4], U8, name="ks_pool", align_bytes=256)
         vs_pool = sb.tile([P, T], F32, name="vs_pool", align_bytes=256)
         kw_pool = sb.tile([P, T], I32, name="kw_pool", align_bytes=256)
-        v_early = big.tile([P, EARLY], F32, name="v_early", offset=4 * T, align_bytes=256)
+        v_pool = big.tile([P, T], F32, name="v_pool", offset=0, align_bytes=256)
         qw = sb.tile([P, PASSES, NQ], I32, name="qw", align_bytes=256)
         ident = sb.tile([P, P], F32, name="ident", align_bytes=64)
         warm = sb.tile([P, 1], F32, name="warm")
         warm_in = sb.tile([P, 1], F32, name="warm_in")
-        ks_g = big.tile([P, N], U8, name="ks_g", offset=4 * T - N)
+        ks_g = big.tile([P, N], U8, name="ks_g", offset=4 * T)
         staged = sb.tile([P, N + NQ], U8, name="staged", align_bytes=256)
         planes = sb.tile([P, PASSES * (N + NQ) + 4], U8, name="planes", align_bytes=256)
         vs_g = sb.tile([P, N], F32, name="vs_g", align_bytes=64)
@@ -72,7 +72,8 @@ def tile_attend_silu_topkq128n512t2048_kernel(tc, q_words, q_scales, k_words, k_
         nc.sync.dma_start(staged[:].bitcast(I32)[last:P, N // 4 :], q_scales[0].bitcast(I32).rearrange("o f c -> f o c"))
         nc.sync.dma_start(kw_pool[:], k_words[0].rearrange("g t r -> g (t r)").bitcast(I32))
         nc.sync.dma_start(qw[:], q_words[0].rearrange("o g q r -> g o (q r)").bitcast(I32))
-        nc.sync.dma_start(v_early[:], vT[:, 0:EARLY])
+        nc.sync.dma_start(v_pool[:, 0:EARLY], vT[:, 0:EARLY])
+        nc.vector.memset(v_pool[:, EARLY : EARLY + 1], 0.0)
         nc.vector.memset(warm_in[:], 0.0)
         nc.vector.memset(ks_pool[:].bitcast(I32)[0:last, :], 0)
         nc.vector.memset(planes[:].bitcast(I32), 0)
@@ -85,7 +86,8 @@ def tile_attend_silu_topkq128n512t2048_kernel(tc, q_words, q_scales, k_words, k_
             staged[:].bitcast(I32)[:, 0 : N // 4].rearrange("p (t b w) -> p t b w", t=PACK, w=RUN // 4),
             ks_g[:].bitcast(I32).rearrange("p (b t w) -> p t b w", t=PACK, w=RUN // 4),
         )
-        v_pool = big.tile([P, T], F32, name="v_pool", offset=0, align_bytes=256)
+        no_bias = big.tile([P, 1], F32, name="no_bias", offset=4 * T)
+        nc.scalar.copy(no_bias[:], v_pool[:, EARLY : EARLY + 1])
         for a in range(P // QUAD):
             (nc.sync, nc.sync, nc.sync, nc.sync)[a].dma_start(
                 planes[:].bitcast(I32)[a * QUAD : a * QUAD + ROWS, 0 : PASSES * (N + NQ) // 4].rearrange("i (o c) -> i o c", o=PASSES),
@@ -99,8 +101,7 @@ def tile_attend_silu_topkq128n512t2048_kernel(tc, q_words, q_scales, k_words, k_
         for t in reversed(range(PACK)):
             nc.tensor.transpose(vs_t[:, t : t + P], vs_g[:, t * P : (t + 1) * P], ident[:])
 
-        nc.scalar.copy(v_pool[:, 0:EARLY], v_early[:])
-        p_sb = big.tile([P, 2, NQ, 2], F32, name="p_sb", offset=4 * T)
+        p_sb = sb.tile([P, 2, NQ, 2], F32, name="p_sb", align_bytes=64)
         for h in range(2):
             nc.vector.tensor_copy(
                 kw_g[:, h * N // 2 : (h + 1) * N // 2],
@@ -122,7 +123,7 @@ def tile_attend_silu_topkq128n512t2048_kernel(tc, q_words, q_scales, k_words, k_
                     stop=(o == PASSES - 1),
                 )
             if t % 2 == 1:
-                nc.scalar.activation(p_sb[:, t // 2], scores[t // 2][:].rearrange("p r q -> p q r"), ACT.Silu)
+                nc.scalar.activation(p_sb[:, t // 2], scores[t // 2][:].rearrange("p r q -> p q r"), ACT.Silu, bias=no_bias[:])
 
         nc.vector.tensor_copy(
             v_g[:].rearrange("p (u b j r) -> p b u r j", u=2, j=RUN, r=2), v_pool[:].indirect(offsets[:])

@@ -66,8 +66,8 @@ def tile_attend_silu_topkq128n512t2048_kernel(tc, q_words, q_scales, k_words, k_
         y_ps = [ps.tile([P, DV // 2], F32, name="y_ps%d" % h) for h in range(2)]
 
         last = P - QUAD
-        nc.sync.dma_start(offsets[:], offs)
         nc.sync.dma_start(ks_pool[:].bitcast(I32)[last:P, 0 : T // 4], k_scales.bitcast(I32).rearrange("o f c -> f o c"))
+        nc.sync.dma_start(offsets[:], offs)
         nc.sync.dma_start(vs_pool[P - 1 : P, :], vs[0:1, :])
         nc.sync.dma_start(staged[:].bitcast(I32)[last:P, N // 4 :], q_scales[0].bitcast(I32).rearrange("o f c -> f o c"))
         nc.sync.dma_start(kw_pool[:], k_words[0].rearrange("g t r -> g (t r)").bitcast(I32))
@@ -81,11 +81,13 @@ def tile_attend_silu_topkq128n512t2048_kernel(tc, q_words, q_scales, k_words, k_
         make_identity(nc, ident[:])
         nc.scalar.activation(warm[:], warm_in[:], ACT.Silu)
 
-        nc.vector.tensor_copy(ks_g[:], ks_pool[:, 0:T].indirect(offsets[:]))
-        nc.vector.tensor_copy(
-            staged[:].bitcast(I32)[:, 0 : N // 4].rearrange("p (t b w) -> p t b w", t=PACK, w=RUN // 4),
-            ks_g[:].bitcast(I32).rearrange("p (b t w) -> p t b w", t=PACK, w=RUN // 4),
-        )
+        for h in range(2):
+            nc.vector.tensor_copy(ks_g[:, h * N // 2 : (h + 1) * N // 2], ks_pool[:, 0:T].indirect(offsets[:, h * N // 32 : (h + 1) * N // 32]))
+        for h in range(2):
+            nc.vector.tensor_copy(
+                staged[:].bitcast(I32)[:, 0 : N // 4].rearrange("p (t h b w) -> p h t b w", h=2, t=PACK, w=RUN // 4)[:, h],
+                ks_g[:].bitcast(I32).rearrange("p (h b t w) -> p h t b w", h=2, t=PACK, w=RUN // 4)[:, h],
+            )
         no_bias = big.tile([P, 1], F32, name="no_bias", offset=4 * T)
         nc.scalar.copy(no_bias[:], v_pool[:, EARLY : EARLY + 1])
         for a in range(P // QUAD):

@@ -127,6 +127,8 @@ def tile_attend_silu_topkq128n512t2048_kernel(tc, q_words, q_scales, k_words, k_
             if t % 2 == 1:
                 nc.scalar.activation(p_sb[:, t // 2], scores[t // 2][:].rearrange("p r q -> p q r"), ACT.Silu, bias=no_bias[:])
 
+        spare = ps.tile([P, P], F32, name="spare")
+        nc.tensor.transpose(spare[:], p_sb[:, 0, 0 : NQ // 2, :].rearrange("p q r -> p (q r)"), ident[:])
         nc.vector.tensor_copy(
             v_g[:].rearrange("p (u b j r) -> p b u r j", u=2, j=RUN, r=2), v_pool[:].indirect(offsets[:])
         )

@@ -124,8 +124,11 @@ def tile_attend_silu_topkq128n512t2048_kernel(tc, q_words, q_scales, k_words, k_
                     start=(o == 0),
                     stop=(o == PASSES - 1),
                 )
-            if t % 2 == 1:
-                nc.scalar.activation(p_sb[:, t // 2], scores[t // 2][:].rearrange("p r q -> p q r"), ACT.Silu, bias=no_bias[:])
+            if t == 1:
+                nc.scalar.activation(p_sb[:, 0], scores[0][:].rearrange("p r q -> p q r"), ACT.Silu, bias=no_bias[:])
+        for h in range(2):
+            qs = slice(h * NQ // 2, (h + 1) * NQ // 2)
+            nc.scalar.activation(p_sb[:, 1, qs], scores[1][:, :, qs].rearrange("p r q -> p q r"), ACT.Silu, bias=no_bias[:])
 
         spare = ps.tile([P, P], F32, name="spare")
         nc.tensor.transpose(spare[:], p_sb[:, 0, 0 : NQ // 2, :].rearrange("p q r -> p (q r)"), ident[:])

@@ -135,7 +135,7 @@ def tile_attend_silu_topkq128n512t2048_kernel(tc, q_words, q_scales, k_words, k_
         nc.vector.tensor_copy(
             v_g[:].rearrange("p (u b j r) -> p b u r j", u=2, j=RUN, r=2), v_pool[:].indirect(offsets[:])
         )
-        w_in = big.tile([P, NQ, PACK], BF16, name="w_in", offset=0, align_bytes=64)
+        w_in = sb.tile([P, NQ, PACK], BF16, name="w_in", align_bytes=64)
         spans = [slice(h * NQ // 2, (h + 1) * NQ // 2) for h in range(2)]
         for qs in spans:
             nc.vector.tensor_tensor(w_in[:, qs, :].rearrange("p q (u r) -> p q u r", r=2), p_sb[:, :, qs, :].rearrange("p u q r -> p q u r"), vs_t[:, P - 1 : P - 1 + PACK].unsqueeze(1).to_broadcast([P, NQ // 2, PACK]).rearrange("p q (u r) -> p q u r", r=2), ALU.mult)

@@ -109,6 +109,8 @@ def tile_attend_silu_topkq128n512t2048_kernel(tc, q_words, q_scales, k_words, k_
                 kw_g[:, h * N // 2 : (h + 1) * N // 2],
                 kw_pool[:].bitcast(U32).indirect(offsets[:, h * N // 32 : (h + 1) * N // 32]),
             )
+        late_zero = sb.tile([P, 1], F32, name="late_zero")
+        nc.gpsimd.tensor_scalar(late_zero[:], v_pool[:, T - 1 : T], 0.0, 0.0, ALU.is_gt, ALU.mult)
         halves = kw_g[:].bitcast(U16).rearrange("p (h b t j o) -> p h t o b j", h=2, t=PACK, j=RUN, o=PASSES)
         parted = k_codes[:].bitcast(U16).rearrange("p (t o h b j) -> p h t o b j", h=2, t=PACK, j=RUN, o=PASSES)
         nc.vector.tensor_copy(parted[:, 0], halves[:, 0])
@@ -128,7 +130,7 @@ def tile_attend_silu_topkq128n512t2048_kernel(tc, q_words, q_scales, k_words, k_
                 nc.scalar.activation(p_sb[:, 0], scores[0][:].rearrange("p r q -> p q r"), ACT.Silu, bias=no_bias[:])
         for h in range(2):
             qs = slice(h * NQ // 2, (h + 1) * NQ // 2)
-            nc.scalar.activation(p_sb[:, 1, qs], scores[1][:, :, qs].rearrange("p r q -> p q r"), ACT.Silu, bias=no_bias[:])
+            nc.scalar.activation(p_sb[:, 1, qs], scores[1][:, :, qs].rearrange("p r q -> p q r"), ACT.Silu, bias=late_zero[:])
 
         spare = ps.tile([P, P], F32, name="spare")
         nc.tensor.transpose(spare[:], p_sb[:, 0, 0 : NQ // 2, :].rearrange("p q r -> p (q r)"), ident[:])

@@ -111,11 +111,24 @@ def tile_attend_silu_topkq128n512t2048_kernel(tc, q_words, q_scales, k_words, k_
             )
         late_zero = sb.tile([P, 1], F32, name="late_zero")
         nc.gpsimd.tensor_scalar(late_zero[:], v_pool[:, T - 1 : T], 0.0, 0.0, ALU.is_gt, ALU.mult)
+        nc.tensor.matmul_mx(
+            out=vs_t[:, N // 2 :],
+            lhsT=kw_g[:, N // 2 : N // 2 + P // 2].bitcast(FP4X4),
+            lhsT_scale=staged[:, 0:P],
+            rhs=qw[:].rearrange("p o q -> p (o q)").bitcast(FP8X4),
+            rhs_scale=staged[:, 0 : PASSES * NQ],
+            start=True,
+            stop=True,
+        )
         halves = kw_g[:].bitcast(U16).rearrange("p (h b t j o) -> p h t o b j", h=2, t=PACK, j=RUN, o=PASSES)
         parted = k_codes[:].bitcast(U16).rearrange("p (t o h b j) -> p h t o b j", h=2, t=PACK, j=RUN, o=PASSES)
-        nc.vector.tensor_copy(parted[:, 0], halves[:, 0])
+        for t in range(2):
+            nc.vector.tensor_copy(parted[:, 0, t], halves[:, 0, t])
         for t in range(PACK):
-            nc.vector.tensor_copy(parted[:, 1, t], halves[:, 1, t])
+            if t < 2:
+                nc.vector.tensor_copy(parted[:, 1, t], halves[:, 1, t])
+            else:
+                nc.vector.tensor_copy(parted[:, :, t], halves[:, :, t])
             for o in range(PASSES):
                 nc.tensor.matmul_mx(
                     out=scores[t // 2][:, t % 2, :],

@@ -112,11 +112,11 @@ def tile_attend_silu_topkq128n512t2048_kernel(tc, q_words, q_scales, k_words, k_
         late_zero = sb.tile([P, 1], F32, name="late_zero")
         nc.gpsimd.tensor_scalar(late_zero[:], v_pool[:, T - 1 : T], 0.0, 0.0, ALU.is_gt, ALU.mult)
         nc.tensor.matmul_mx(
-            out=vs_t[:, N // 2 :],
+            out=vs_t[:, N // 2 : N // 2 + NQ],
             lhsT=kw_g[:, N // 2 : N // 2 + P // 2].bitcast(FP4X4),
             lhsT_scale=staged[:, 0:P],
-            rhs=qw[:].rearrange("p o q -> p (o q)").bitcast(FP8X4),
-            rhs_scale=staged[:, 0 : PASSES * NQ],
+            rhs=qw[:, 0, :].bitcast(FP8X4),
+            rhs_scale=staged[:, 0:NQ],
             start=True,
             stop=True,
         )
@@ -162,6 +162,16 @@ def tile_attend_silu_topkq128n512t2048_kernel(tc, q_words, q_scales, k_words, k_
             nc.scalar.copy(v_in[:, es, :].bitcast(F32), v_t[:, :, es].rearrange("p u e -> p e u"))
         for qs in spans:
             nc.vector.quantize_mx(out=w_codes[:, qs].bitcast(FP8X4), scales=w_scales[:, qs], in_=w_in[:, qs, :].rearrange("p q t -> p (q t)"))
+        spare_mx = ps.tile([P, NQ // 2], F32, name="spare_mx")
+        nc.tensor.matmul_mx(
+            out=spare_mx[:],
+            lhsT=qw[:, 0, :].bitcast(FP8X4),
+            lhsT_scale=planes[:, N : N + NQ],
+            rhs=w_codes[:, spans[0]].bitcast(FP8X4),
+            rhs_scale=w_scales[:, spans[0]],
+            start=True,
+            stop=True,
+        )
         for es in spans:
             nc.vector.quantize_mx(out=v_codes[:, es].bitcast(FP8X4), scales=v_scales[:, es], in_=v_in[:, es, :].rearrange("p e t -> p (e t)"))
         for h, es in enumerate(spans):

@@ -25,7 +25,7 @@ PACK = 4
 RUN = 8
 QUAD = 32
 ROWS = 4
-EARLY = 1024
+EARLY = 1088
 
 FLOPS = 2 * NQ * N * D + 2 * NQ * N * DV
 BYTES = 2 * 128 * 128 * 4 + 2 * 16 * 128 + 128 * T * 4 + 2 * 16 * T + DV * T * 4 + T * 4 + 128 * 32 * 2 + NQ * DV * 4
@@ -68,10 +68,10 @@ def tile_attend_silu_topkq128n512t2048_kernel(tc, q_words, q_scales, k_words, k_
         last = P - QUAD
         nc.sync.dma_start(ks_pool[:].bitcast(I32)[last:P, 0 : T // 4], k_scales.bitcast(I32).rearrange("o f c -> f o c"))
         nc.sync.dma_start(offsets[:], offs)
+        nc.sync.dma_start(qw[:], q_words[0].rearrange("o g q r -> g o (q r)").bitcast(I32))
         nc.sync.dma_start(vs_pool[P - 1 : P, :], vs[0:1, :])
         nc.sync.dma_start(staged[:].bitcast(I32)[last:P, N // 4 :], q_scales[0].bitcast(I32).rearrange("o f c -> f o c"))
         nc.sync.dma_start(kw_pool[:], k_words[0].rearrange("g t r -> g (t r)").bitcast(I32))
-        nc.sync.dma_start(qw[:], q_words[0].rearrange("o g q r -> g o (q r)").bitcast(I32))
         nc.sync.dma_start(v_pool[:, 0:EARLY], vT[:, 0:EARLY])
         nc.vector.memset(v_pool[:, EARLY : EARLY + 1], 0.0)
         nc.vector.memset(warm_in[:], 0.0)

@@ -110,7 +110,7 @@ def tile_attend_silu_topkq128n512t2048_kernel(tc, q_words, q_scales, k_words, k_
                 kw_pool[:].bitcast(U32).indirect(offsets[:, h * N // 32 : (h + 1) * N // 32]),
             )
         late_zero = sb.tile([P, 1], F32, name="late_zero")
-        nc.gpsimd.tensor_scalar(late_zero[:], v_pool[:, T - 1 : T], 0.0, 0.0, ALU.is_gt, ALU.mult)
+        nc.gpsimd.tensor_scalar(late_zero[:], v_pool[:, T - 1 : T], no_bias[:], 0.0, ALU.is_gt, ALU.mult)
         nc.tensor.matmul_mx(
             out=vs_t[:, N // 2 : N // 2 + NQ],
             lhsT=kw_g[:, N // 2 : N // 2 + P // 2].bitcast(FP4X4),
@@ -140,7 +140,7 @@ def tile_attend_silu_topkq128n512t2048_kernel(tc, q_words, q_scales, k_words, k_
                     stop=(o == PASSES - 1),
                 )
             if t == 1:
-                nc.scalar.activation(p_sb[:, 0], scores[0][:].rearrange("p r q -> p q r"), ACT.Silu, bias=no_bias[:])
+                nc.scalar.activation(p_sb[:, 0], scores[0][:].rearrange("p r q -> p q r"), ACT.Silu, bias=late_zero[:])
         for h in range(2):
             qs = slice(h * NQ // 2, (h + 1) * NQ // 2)
             nc.scalar.activation(p_sb[:, 1, qs], scores[1][:, :, qs].rearrange("p r q -> p q r"), ACT.Silu, bias=late_zero[:])
@@ -152,8 +152,12 @@ def tile_attend_silu_topkq128n512t2048_kernel(tc, q_words, q_scales, k_words, k_
         )
         w_in = sb.tile([P, NQ, PACK], BF16, name="w_in", align_bytes=64)
         spans = [slice(h * NQ // 2, (h + 1) * NQ // 2) for h in range(2)]
-        for qs in spans:
-            nc.vector.tensor_tensor(w_in[:, qs, :].rearrange("p q (u r) -> p q u r", r=2), p_sb[:, :, qs, :].rearrange("p u q r -> p q u r"), vs_t[:, P - 1 : P - 1 + PACK].unsqueeze(1).to_broadcast([P, NQ // 2, PACK]).rearrange("p q (u r) -> p q u r", r=2), ALU.mult)
+        w_pairs = w_in[:].rearrange("p q (u r) -> p q u r", r=2)
+        p_pairs = p_sb[:].rearrange("p u q r -> p q u r")
+        vs_pairs = vs_t[:, P - 1 : P - 1 + PACK].unsqueeze(1).to_broadcast([P, NQ // 2, PACK]).rearrange("p q (u r) -> p q u r", r=2)
+        for u in range(2):
+            nc.vector.tensor_tensor(w_pairs[:, spans[0], u], p_pairs[:, spans[0], u], vs_pairs[:, :, u], ALU.mult)
+        nc.vector.tensor_tensor(w_pairs[:, spans[1]], p_pairs[:, spans[1]], vs_pairs, ALU.mult)
         v_t = ps.tile([P, 2, DV], F32, name="v_t", tag="bank0")
         v_words = v_g[:].bitcast(F32)
         for u in range(2):

@@ -111,15 +111,6 @@ def tile_attend_silu_topkq128n512t2048_kernel(tc, q_words, q_scales, k_words, k_
             )
         late_zero = sb.tile([P, 1], F32, name="late_zero")
         nc.gpsimd.tensor_scalar(late_zero[:], v_pool[:, T - 1 : T], no_bias[:], 0.0, ALU.is_gt, ALU.mult)
-        nc.tensor.matmul_mx(
-            out=vs_t[:, N // 2 : N // 2 + NQ],
-            lhsT=kw_g[:, N // 2 : N // 2 + P // 2].bitcast(FP4X4),
-            lhsT_scale=staged[:, 0:P],
-            rhs=qw[:, 0, :].bitcast(FP8X4),
-            rhs_scale=staged[:, 0:NQ],
-            start=True,
-            stop=True,
-        )
         halves = kw_g[:].bitcast(U16).rearrange("p (h b t j o) -> p h t o b j", h=2, t=PACK, j=RUN, o=PASSES)
         parted = k_codes[:].bitcast(U16).rearrange("p (t o h b j) -> p h t o b j", h=2, t=PACK, j=RUN, o=PASSES)
         for t in range(2):
@@ -166,16 +157,6 @@ def tile_attend_silu_topkq128n512t2048_kernel(tc, q_words, q_scales, k_words, k_
             nc.scalar.copy(v_in[:, es, :].bitcast(F32), v_t[:, :, es].rearrange("p u e -> p e u"))
         for qs in spans:
             nc.vector.quantize_mx(out=w_codes[:, qs].bitcast(FP8X4), scales=w_scales[:, qs], in_=w_in[:, qs, :].rearrange("p q t -> p (q t)"))
-        spare_mx = ps.tile([P, NQ // 2], F32, name="spare_mx")
-        nc.tensor.matmul_mx(
-            out=spare_mx[:],
-            lhsT=qw[:, 0, :].bitcast(FP8X4),
-            lhsT_scale=planes[:, N : N + NQ],
-            rhs=w_codes[:, spans[0]].bitcast(FP8X4),
-            rhs_scale=w_scales[:, spans[0]],
-            start=True,
-            stop=True,
-        )
         for es in spans:
             nc.vector.quantize_mx(out=v_codes[:, es].bitcast(FP8X4), scales=v_scales[:, es], in_=v_in[:, es, :].rearrange("p e t -> p (e t)"))
         for h, es in enumerate(spans):

@@ -113,13 +113,9 @@ def tile_attend_silu_topkq128n512t2048_kernel(tc, q_words, q_scales, k_words, k_
         nc.gpsimd.tensor_scalar(late_zero[:], v_pool[:, T - 1 : T], no_bias[:], 0.0, ALU.is_gt, ALU.mult)
         halves = kw_g[:].bitcast(U16).rearrange("p (h b t j o) -> p h t o b j", h=2, t=PACK, j=RUN, o=PASSES)
         parted = k_codes[:].bitcast(U16).rearrange("p (t o h b j) -> p h t o b j", h=2, t=PACK, j=RUN, o=PASSES)
-        for t in range(2):
-            nc.vector.tensor_copy(parted[:, 0, t], halves[:, 0, t])
+        nc.vector.tensor_copy(parted[:, 0], halves[:, 0])
         for t in range(PACK):
-            if t < 2:
-                nc.vector.tensor_copy(parted[:, 1, t], halves[:, 1, t])
-            else:
-                nc.vector.tensor_copy(parted[:, :, t], halves[:, :, t])
+            nc.vector.tensor_copy(parted[:, 1, t], halves[:, 1, t])
             for o in range(PASSES):
                 nc.tensor.matmul_mx(
                     out=scores[t // 2][:, t % 2, :],

@@ -81,13 +81,11 @@ def tile_attend_silu_topkq128n512t2048_kernel(tc, q_words, q_scales, k_words, k_
         make_identity(nc, ident[:])
         nc.scalar.activation(warm[:], warm_in[:], ACT.Silu)
 
-        for h in range(2):
-            nc.vector.tensor_copy(ks_g[:, h * N // 2 : (h + 1) * N // 2], ks_pool[:, 0:T].indirect(offsets[:, h * N // 32 : (h + 1) * N // 32]))
-        for h in range(2):
-            nc.vector.tensor_copy(
-                staged[:].bitcast(I32)[:, 0 : N // 4].rearrange("p (t h b w) -> p h t b w", h=2, t=PACK, w=RUN // 4)[:, h],
-                ks_g[:].bitcast(I32).rearrange("p (h b t w) -> p h t b w", h=2, t=PACK, w=RUN // 4)[:, h],
-            )
+        nc.vector.tensor_copy(ks_g[:], ks_pool[:, 0:T].indirect(offsets[:]))
+        nc.vector.tensor_copy(
+            staged[:].bitcast(I32)[:, 0 : N // 4].rearrange("p (t b w) -> p t b w", t=PACK, w=RUN // 4),
+            ks_g[:].bitcast(I32).rearrange("p (b t w) -> p t b w", t=PACK, w=RUN // 4),
+        )
         no_bias = big.tile([P, 1], F32, name="no_bias", offset=4 * T)
         nc.scalar.copy(no_bias[:], v_pool[:, EARLY : EARLY + 1])
         for a in range(P // QUAD):

@@ -107,8 +107,6 @@ def tile_attend_silu_topkq128n512t2048_kernel(tc, q_words, q_scales, k_words, k_
                 kw_g[:, h * N // 2 : (h + 1) * N // 2],
                 kw_pool[:].bitcast(U32).indirect(offsets[:, h * N // 32 : (h + 1) * N // 32]),
             )
-        late_zero = sb.tile([P, 1], F32, name="late_zero")
-        nc.gpsimd.tensor_scalar(late_zero[:], v_pool[:, T - 1 : T], no_bias[:], 0.0, ALU.is_gt, ALU.mult)
         halves = kw_g[:].bitcast(U16).rearrange("p (h b t j o) -> p h t o b j", h=2, t=PACK, j=RUN, o=PASSES)
         parted = k_codes[:].bitcast(U16).rearrange("p (t o h b j) -> p h t o b j", h=2, t=PACK, j=RUN, o=PASSES)
         nc.vector.tensor_copy(parted[:, 0], halves[:, 0])
@@ -125,24 +123,23 @@ def tile_attend_silu_topkq128n512t2048_kernel(tc, q_words, q_scales, k_words, k_
                     stop=(o == PASSES - 1),
                 )
             if t == 1:
-                nc.scalar.activation(p_sb[:, 0], scores[0][:].rearrange("p r q -> p q r"), ACT.Silu, bias=late_zero[:])
+                nc.scalar.activation(p_sb[:, 0], scores[0][:].rearrange("p r q -> p q r"), ACT.Silu, bias=no_bias[:])
         for h in range(2):
             qs = slice(h * NQ // 2, (h + 1) * NQ // 2)
-            nc.scalar.activation(p_sb[:, 1, qs], scores[1][:, :, qs].rearrange("p r q -> p q r"), ACT.Silu, bias=late_zero[:])
+            nc.scalar.activation(p_sb[:, 1, qs], scores[1][:, :, qs].rearrange("p r q -> p q r"), ACT.Silu, bias=no_bias[:])
 
         spare = ps.tile([P, P], F32, name="spare")
         nc.tensor.transpose(spare[:], p_sb[:, 0, 0 : NQ // 2, :].rearrange("p q r -> p (q r)"), ident[:])
         nc.vector.tensor_copy(
             v_g[:].rearrange("p (u b j r) -> p b u r j", u=2, j=RUN, r=2), v_pool[:].indirect(offsets[:])
         )
-        w_in = sb.tile([P, NQ, PACK], BF16, name="w_in", align_bytes=64)
+        w_in = big.tile([P, NQ, PACK], BF16, name="w_in", offset=0, align_bytes=64)
         spans = [slice(h * NQ // 2, (h + 1) * NQ // 2) for h in range(2)]
         w_pairs = w_in[:].rearrange("p q (u r) -> p q u r", r=2)
         p_pairs = p_sb[:].rearrange("p u q r -> p q u r")
         vs_pairs = vs_t[:, P - 1 : P - 1 + PACK].unsqueeze(1).to_broadcast([P, NQ // 2, PACK]).rearrange("p q (u r) -> p q u r", r=2)
-        for u in range(2):
-            nc.vector.tensor_tensor(w_pairs[:, spans[0], u], p_pairs[:, spans[0], u], vs_pairs[:, :, u], ALU.mult)
-        nc.vector.tensor_tensor(w_pairs[:, spans[1]], p_pairs[:, spans[1]], vs_pairs, ALU.mult)
+        for qs in spans:
+            nc.vector.tensor_tensor(w_pairs[:, qs], p_pairs[:, qs], vs_pairs, ALU.mult)
         v_t = ps.tile([P, 2, DV], F32, name="v_t", tag="bank0")
         v_words = v_g[:].bitcast(F32)
         for u in range(2):

@@ -25,7 +25,7 @@ PACK = 4
 RUN = 8
 QUAD = 32
 ROWS = 4
-EARLY = 1088
+EARLY = 1152
 
 FLOPS = 2 * NQ * N * D + 2 * NQ * N * DV
 BYTES = 2 * 128 * 128 * 4 + 2 * 16 * 128 + 128 * T * 4 + 2 * 16 * T + DV * T * 4 + T * 4 + 128 * 32 * 2 + NQ * DV * 4
@@ -133,7 +133,7 @@ def tile_attend_silu_topkq128n512t2048_kernel(tc, q_words, q_scales, k_words, k_
         nc.vector.tensor_copy(
             v_g[:].rearrange("p (u b j r) -> p b u r j", u=2, j=RUN, r=2), v_pool[:].indirect(offsets[:])
         )
-        w_in = big.tile([P, NQ, PACK], BF16, name="w_in", offset=0, align_bytes=64)
+        w_in = sb.tile([P, NQ, PACK], BF16, name="w_in", align_bytes=64)
         spans = [slice(h * NQ // 2, (h + 1) * NQ // 2) for h in range(2)]
         w_pairs = w_in[:].rearrange("p q (u r) -> p q u r", r=2)
         p_pairs = p_sb[:].rearrange("p u q r -> p q u r")

@@ -122,11 +122,8 @@ def tile_attend_silu_topkq128n512t2048_kernel(tc, q_words, q_scales, k_words, k_
                     start=(o == 0),
                     stop=(o == PASSES - 1),
                 )
-            if t == 1:
-                nc.scalar.activation(p_sb[:, 0], scores[0][:].rearrange("p r q -> p q r"), ACT.Silu, bias=no_bias[:])
-        for h in range(2):
-            qs = slice(h * NQ // 2, (h + 1) * NQ // 2)
-            nc.scalar.activation(p_sb[:, 1, qs], scores[1][:, :, qs].rearrange("p r q -> p q r"), ACT.Silu, bias=no_bias[:])
+            if t % 2 == 1:
+                nc.scalar.activation(p_sb[:, t // 2], scores[t // 2][:].rearrange("p r q -> p q r"), ACT.Silu, bias=no_bias[:])
 
         spare = ps.tile([P, P], F32, name="spare")
         nc.tensor.transpose(spare[:], p_sb[:, 0, 0 : NQ // 2, :].rearrange("p q r -> p (q r)"), ident[:])

@@ -102,16 +102,11 @@ def tile_attend_silu_topkq128n512t2048_kernel(tc, q_words, q_scales, k_words, k_
             nc.tensor.transpose(vs_t[:, t : t + P], vs_g[:, t * P : (t + 1) * P], ident[:])
 
         p_sb = sb.tile([P, 2, NQ, 2], F32, name="p_sb", align_bytes=64)
-        for h in range(2):
-            nc.vector.tensor_copy(
-                kw_g[:, h * N // 2 : (h + 1) * N // 2],
-                kw_pool[:].bitcast(U32).indirect(offsets[:, h * N // 32 : (h + 1) * N // 32]),
-            )
-        halves = kw_g[:].bitcast(U16).rearrange("p (h b t j o) -> p h t o b j", h=2, t=PACK, j=RUN, o=PASSES)
-        parted = k_codes[:].bitcast(U16).rearrange("p (t o h b j) -> p h t o b j", h=2, t=PACK, j=RUN, o=PASSES)
-        nc.vector.tensor_copy(parted[:, 0], halves[:, 0])
+        nc.vector.tensor_copy(kw_g[:], kw_pool[:].bitcast(U32).indirect(offsets[:]))
+        halves = kw_g[:].bitcast(U16).rearrange("p (b t j o) -> p t o b j", t=PACK, j=RUN, o=PASSES)
+        parted = k_codes[:].bitcast(U16).rearrange("p (t o b j) -> p t o b j", t=PACK, j=RUN, o=PASSES)
         for t in range(PACK):
-            nc.vector.tensor_copy(parted[:, 1, t], halves[:, 1, t])
+            nc.vector.tensor_copy(parted[:, t], halves[:, t])
             for o in range(PASSES):
                 nc.tensor.matmul_mx(
                     out=scores[t // 2][:, t % 2, :],

@@ -44,21 +44,21 @@ def tile_attend_silu_topkq128n512t2048_kernel(tc, q_words, q_scales, k_words, k_
         kw_pool = sb.tile([P, T], I32, name="kw_pool", align_bytes=256)
         v_pool = big.tile([P, T], F32, name="v_pool", offset=0, align_bytes=256)
         qw = sb.tile([P, PASSES, NQ], I32, name="qw", align_bytes=256)
-        ident = sb.tile([P, P], F32, name="ident", align_bytes=64)
+        ident = sb.tile([P, P], F32, name="ident", align_bytes=256)
         warm = sb.tile([P, 1], F32, name="warm")
         warm_in = sb.tile([P, 1], F32, name="warm_in")
         ks_g = big.tile([P, N], U8, name="ks_g", offset=4 * T)
         staged = sb.tile([P, N + NQ], U8, name="staged", align_bytes=256)
         planes = sb.tile([P, PASSES * (N + NQ) + 4], U8, name="planes", align_bytes=256)
-        vs_g = sb.tile([P, N], F32, name="vs_g", align_bytes=64)
-        kw_g = sb.tile([P, N], U32, name="kw_g", align_bytes=64)
-        k_codes = sb.tile([P, PACK * PASSES * P * 2], U8, name="k_codes", align_bytes=64)
-        v_g = sb.tile([P, N], BF16, name="v_g", align_bytes=64)
-        v_in = sb.tile([P, DV, PACK], BF16, name="v_in", align_bytes=64)
-        w_codes = sb.tile([P, NQ], U32, name="w_codes", align_bytes=64)
-        w_scales = sb.tile([P, NQ], U8, name="w_scales", align_bytes=64)
-        v_codes = sb.tile([P, DV], U32, name="v_codes", align_bytes=64)
-        v_scales = sb.tile([P, DV], U8, name="v_scales", align_bytes=64)
+        vs_g = sb.tile([P, N], F32, name="vs_g", align_bytes=256)
+        kw_g = sb.tile([P, N], U32, name="kw_g", align_bytes=256)
+        k_codes = sb.tile([P, PACK * PASSES * P * 2], U8, name="k_codes", align_bytes=256)
+        v_g = sb.tile([P, N], BF16, name="v_g", align_bytes=256)
+        v_in = sb.tile([P, DV, PACK], BF16, name="v_in", align_bytes=256)
+        w_codes = sb.tile([P, NQ], U32, name="w_codes", align_bytes=256)
+        w_scales = sb.tile([P, NQ], U8, name="w_scales", align_bytes=256)
+        v_codes = sb.tile([P, DV], U32, name="v_codes", align_bytes=256)
+        v_scales = sb.tile([P, DV], U8, name="v_scales", align_bytes=256)
         y_sb = sb.tile([P, DV], F32, name="y_sb", align_bytes=256)
 
         scores = [ps.tile([P, 2, NQ], F32, name="score%d" % u, tag="bank%d" % u) for u in range(2)]
@@ -101,7 +101,7 @@ def tile_attend_silu_topkq128n512t2048_kernel(tc, q_words, q_scales, k_words, k_
         for t in reversed(range(PACK)):
             nc.tensor.transpose(vs_t[:, t : t + P], vs_g[:, t * P : (t + 1) * P], ident[:])
 
-        p_sb = sb.tile([P, 2, NQ, 2], F32, name="p_sb", align_bytes=64)
+        p_sb = sb.tile([P, 2, NQ, 2], F32, name="p_sb", align_bytes=256)
         nc.vector.tensor_copy(kw_g[:], kw_pool[:].bitcast(U32).indirect(offsets[:]))
         halves = kw_g[:].bitcast(U16).rearrange("p (b t j o) -> p t o b j", t=PACK, j=RUN, o=PASSES)
         parted = k_codes[:].bitcast(U16).rearrange("p (t o b j) -> p t o b j", t=PACK, j=RUN, o=PASSES)
@@ -125,7 +125,7 @@ def tile_attend_silu_topkq128n512t2048_kernel(tc, q_words, q_scales, k_words, k_
         nc.vector.tensor_copy(
             v_g[:].rearrange("p (u b j r) -> p b u r j", u=2, j=RUN, r=2), v_pool[:].indirect(offsets[:])
         )
-        w_in = sb.tile([P, NQ, PACK], BF16, name="w_in", align_bytes=64)
+        w_in = sb.tile([P, NQ, PACK], BF16, name="w_in", align_bytes=256)
         spans = [slice(h * NQ // 2, (h + 1) * NQ // 2) for h in range(2)]
         w_pairs = w_in[:].rearrange("p q (u r) -> p q u r", r=2)
         p_pairs = p_sb[:].rearrange("p u q r -> p q u r")

@@ -129,17 +129,15 @@ def tile_attend_silu_topkq128n512t2048_kernel(tc, q_words, q_scales, k_words, k_
         spans = [slice(h * NQ // 2, (h + 1) * NQ // 2) for h in range(2)]
         w_pairs = w_in[:].rearrange("p q (u r) -> p q u r", r=2)
         p_pairs = p_sb[:].rearrange("p u q r -> p q u r")
-        vs_pairs = vs_t[:, P - 1 : P - 1 + PACK].unsqueeze(1).to_broadcast([P, NQ // 2, PACK]).rearrange("p q (u r) -> p q u r", r=2)
-        for qs in spans:
-            nc.vector.tensor_tensor(w_pairs[:, qs], p_pairs[:, qs], vs_pairs, ALU.mult)
+        vs_pairs = vs_t[:, P - 1 : P - 1 + PACK].unsqueeze(1).to_broadcast([P, NQ, PACK]).rearrange("p q (u r) -> p q u r", r=2)
+        nc.vector.tensor_tensor(w_pairs, p_pairs, vs_pairs, ALU.mult)
         v_t = ps.tile([P, 2, DV], F32, name="v_t", tag="bank0")
         v_words = v_g[:].bitcast(F32)
         for u in range(2):
             nc.tensor.transpose(v_t[:, u, :], v_words[:, u * P : (u + 1) * P], ident[:])
         for es in spans:
             nc.scalar.copy(v_in[:, es, :].bitcast(F32), v_t[:, :, es].rearrange("p u e -> p e u"))
-        for qs in spans:
-            nc.vector.quantize_mx(out=w_codes[:, qs].bitcast(FP8X4), scales=w_scales[:, qs], in_=w_in[:, qs, :].rearrange("p q t -> p (q t)"))
+        nc.vector.quantize_mx(out=w_codes[:].bitcast(FP8X4), scales=w_scales[:], in_=w_in[:].rearrange("p q t -> p (q t)"))
         for es in spans:
             nc.vector.quantize_mx(out=v_codes[:, es].bitcast(FP8X4), scales=v_scales[:, es], in_=v_in[:, es, :].rearrange("p e t -> p (e t)"))
         for h, es in enumerate(spans):

@@ -25,6 +25,9 @@ PACK = 4
 RUN = 8
 QUAD = 32
 ROWS = 4
+SCALES = N + NQ
+WORD = 4
+ALIGN = 256
 EARLY = 1152
 
 FLOPS = 2 * NQ * N * D + 2 * NQ * N * DV
@@ -35,65 +38,68 @@ def tile_attend_silu_topkq128n512t2048_kernel(tc, q_words, q_scales, k_words, k_
     nc = tc.nc
     with ExitStack() as ctx:
         sb = ctx.enter_context(tc.tile_pool(name="sb", bufs=1))
-        big = ctx.enter_context(tc.tile_pool(name="big", bufs=1))
+        placed = ctx.enter_context(tc.tile_pool(name="placed", bufs=1))
         ps = ctx.enter_context(tc.psum_pool(name="ps", bufs=1))
 
         offsets = sb.tile([P, N // 16], U16, name="offsets")
-        ks_pool = sb.tile([P, T + 4], U8, name="ks_pool", align_bytes=256)
-        vs_pool = sb.tile([P, T], F32, name="vs_pool", align_bytes=256)
-        kw_pool = sb.tile([P, T], I32, name="kw_pool", align_bytes=256)
-        v_pool = big.tile([P, T], F32, name="v_pool", offset=0, align_bytes=256)
-        qw = sb.tile([P, PASSES, NQ], I32, name="qw", align_bytes=256)
-        ident = sb.tile([P, P], F32, name="ident", align_bytes=256)
+        ks_pool = sb.tile([P, T + WORD], U8, name="ks_pool", align_bytes=ALIGN)
+        vs_pool = sb.tile([P, T], F32, name="vs_pool", align_bytes=ALIGN)
+        kw_pool = sb.tile([P, T], I32, name="kw_pool", align_bytes=ALIGN)
+        v_pool = placed.tile([P, T], F32, name="v_pool", offset=0, align_bytes=ALIGN)
+        qw = sb.tile([P, PASSES, NQ], I32, name="qw", align_bytes=ALIGN)
+        ident = sb.tile([P, P], F32, name="ident", align_bytes=ALIGN)
         warm = sb.tile([P, 1], F32, name="warm")
-        warm_in = sb.tile([P, 1], F32, name="warm_in")
-        ks_g = big.tile([P, N], U8, name="ks_g", offset=4 * T)
-        staged = sb.tile([P, N + NQ], U8, name="staged", align_bytes=256)
-        planes = sb.tile([P, PASSES * (N + NQ) + 4], U8, name="planes", align_bytes=256)
-        vs_g = sb.tile([P, N], F32, name="vs_g", align_bytes=256)
-        kw_g = sb.tile([P, N], U32, name="kw_g", align_bytes=256)
-        k_codes = sb.tile([P, PACK * PASSES * P * 2], U8, name="k_codes", align_bytes=256)
-        v_g = sb.tile([P, N], BF16, name="v_g", align_bytes=256)
-        v_in = sb.tile([P, DV, PACK], BF16, name="v_in", align_bytes=256)
-        w_codes = sb.tile([P, NQ], U32, name="w_codes", align_bytes=256)
-        w_scales = sb.tile([P, NQ], U8, name="w_scales", align_bytes=256)
-        v_codes = sb.tile([P, DV], U32, name="v_codes", align_bytes=256)
-        v_scales = sb.tile([P, DV], U8, name="v_scales", align_bytes=256)
-        y_sb = sb.tile([P, DV], F32, name="y_sb", align_bytes=256)
+        ks_g = placed.tile([P, N], U8, name="ks_g", offset=WORD * T)
+        staged = sb.tile([P, SCALES], U8, name="staged", align_bytes=ALIGN)
+        planes = sb.tile([P, PASSES * SCALES + WORD], U8, name="planes", align_bytes=ALIGN)
+        vs_g = sb.tile([P, N], F32, name="vs_g", align_bytes=ALIGN)
+        kw_g = sb.tile([P, N], U32, name="kw_g", align_bytes=ALIGN)
+        k_codes = sb.tile([P, PACK, PASSES, P], U16, name="k_codes", align_bytes=ALIGN)
+        v_g = sb.tile([P, N], BF16, name="v_g", align_bytes=ALIGN)
+        v_in = sb.tile([P, DV, PACK], BF16, name="v_in", align_bytes=ALIGN)
+        w_codes = sb.tile([P, NQ], U32, name="w_codes", align_bytes=ALIGN)
+        w_scales = sb.tile([P, NQ], U8, name="w_scales", align_bytes=ALIGN)
+        v_codes = sb.tile([P, DV], U32, name="v_codes", align_bytes=ALIGN)
+        v_scales = sb.tile([P, DV], U8, name="v_scales", align_bytes=ALIGN)
+        y_sb = sb.tile([P, DV], F32, name="y_sb", align_bytes=ALIGN)
+        p_sb = sb.tile([P, 2, NQ, 2], F32, name="p_sb", align_bytes=ALIGN)
+        w_in = sb.tile([P, NQ, PACK], BF16, name="w_in", align_bytes=ALIGN)
 
         scores = [ps.tile([P, 2, NQ], F32, name="score%d" % u, tag="bank%d" % u) for u in range(2)]
-        vs_t = ps.tile([P, N], F32, name="vs_t")
+        vs_t = ps.tile([P, P + PACK - 1], F32, name="vs_t")
+        spare = ps.tile([P, P], F32, name="spare")
         y_ps = [ps.tile([P, DV // 2], F32, name="y_ps%d" % h) for h in range(2)]
 
         last = P - QUAD
-        nc.sync.dma_start(ks_pool[:].bitcast(I32)[last:P, 0 : T // 4], k_scales.bitcast(I32).rearrange("o f c -> f o c"))
+        nc.sync.dma_start(ks_pool[:].bitcast(I32)[last:P, 0 : T // WORD], k_scales.bitcast(I32).rearrange("o f c -> f o c"))
         nc.sync.dma_start(offsets[:], offs)
         nc.sync.dma_start(qw[:], q_words[0].rearrange("o g q r -> g o (q r)").bitcast(I32))
         nc.sync.dma_start(vs_pool[P - 1 : P, :], vs[0:1, :])
-        nc.sync.dma_start(staged[:].bitcast(I32)[last:P, N // 4 :], q_scales[0].bitcast(I32).rearrange("o f c -> f o c"))
+        nc.sync.dma_start(staged[:].bitcast(I32)[last:P, N // WORD :], q_scales[0].bitcast(I32).rearrange("o f c -> f o c"))
         nc.sync.dma_start(kw_pool[:], k_words[0].rearrange("g t r -> g (t r)").bitcast(I32))
         nc.sync.dma_start(v_pool[:, 0:EARLY], vT[:, 0:EARLY])
-        nc.vector.memset(v_pool[:, EARLY : EARLY + 1], 0.0)
-        nc.vector.memset(warm_in[:], 0.0)
+        zero = v_pool[:, EARLY : EARLY + 1]
+        nc.vector.memset(zero, 0.0)
         nc.vector.memset(ks_pool[:].bitcast(I32)[0:last, :], 0)
         nc.vector.memset(planes[:].bitcast(I32), 0)
         nc.gpsimd.memset(vs_pool[0 : P - 1, :].bitcast(I32), 0)
         make_identity(nc, ident[:])
-        nc.scalar.activation(warm[:], warm_in[:], ACT.Silu)
+        nc.scalar.activation(warm[:], zero, ACT.Silu)
 
         nc.vector.tensor_copy(ks_g[:], ks_pool[:, 0:T].indirect(offsets[:]))
         nc.vector.tensor_copy(
-            staged[:].bitcast(I32)[:, 0 : N // 4].rearrange("p (t b w) -> p t b w", t=PACK, w=RUN // 4),
-            ks_g[:].bitcast(I32).rearrange("p (b t w) -> p t b w", t=PACK, w=RUN // 4),
+            staged[:].bitcast(I32)[:, 0 : N // WORD].rearrange("p (t b w) -> p t b w", t=PACK, w=RUN // WORD),
+            ks_g[:].bitcast(I32).rearrange("p (b t w) -> p t b w", t=PACK, w=RUN // WORD),
         )
-        no_bias = big.tile([P, 1], F32, name="no_bias", offset=4 * T)
-        nc.scalar.copy(no_bias[:], v_pool[:, EARLY : EARLY + 1])
+        no_bias = placed.tile([P, 1], F32, name="no_bias", offset=WORD * T)
+        nc.scalar.copy(no_bias[:], zero)
         for a in range(P // QUAD):
-            (nc.sync, nc.sync, nc.sync, nc.sync)[a].dma_start(
-                planes[:].bitcast(I32)[a * QUAD : a * QUAD + ROWS, 0 : PASSES * (N + NQ) // 4].rearrange("i (o c) -> i o c", o=PASSES),
+            nc.sync.dma_start(
+                planes[:].bitcast(I32)[a * QUAD : a * QUAD + ROWS, 0 : PASSES * SCALES // WORD].rearrange("i (o c) -> i o c", o=PASSES),
                 staged[:].bitcast(I32)[last + a * ROWS * PASSES : last + (a + 1) * ROWS * PASSES, :],
             )
         nc.sync.dma_start(v_pool[:, EARLY:T], vT[:, EARLY:T])
+
         nc.vector.tensor_copy(
             vs_g[:].bitcast(U32).rearrange("p (t b j) -> p b t j", t=PACK, j=RUN),
             vs_pool[:].bitcast(U32).indirect(offsets[:]),
@@ -101,46 +107,45 @@ def tile_attend_silu_topkq128n512t2048_kernel(tc, q_words, q_scales, k_words, k_
         for t in reversed(range(PACK)):
             nc.tensor.transpose(vs_t[:, t : t + P], vs_g[:, t * P : (t + 1) * P], ident[:])
 
-        p_sb = sb.tile([P, 2, NQ, 2], F32, name="p_sb", align_bytes=256)
         nc.vector.tensor_copy(kw_g[:], kw_pool[:].bitcast(U32).indirect(offsets[:]))
-        halves = kw_g[:].bitcast(U16).rearrange("p (b t j o) -> p t o b j", t=PACK, j=RUN, o=PASSES)
-        parted = k_codes[:].bitcast(U16).rearrange("p (t o b j) -> p t o b j", t=PACK, j=RUN, o=PASSES)
+        kw_by_place = kw_g[:].bitcast(U16).rearrange("p (b t j o) -> p t o b j", t=PACK, j=RUN, o=PASSES)
         for t in range(PACK):
-            nc.vector.tensor_copy(parted[:, t], halves[:, t])
+            nc.vector.tensor_copy(k_codes[:, t].rearrange("p o (b j) -> p o b j", j=RUN), kw_by_place[:, t])
             for o in range(PASSES):
                 nc.tensor.matmul_mx(
                     out=scores[t // 2][:, t % 2, :],
-                    lhsT=k_codes[:, (t * PASSES + o) * 2 * P : (t * PASSES + o + 1) * 2 * P].bitcast(FP4X4),
-                    lhsT_scale=planes[:, o * (N + NQ) + t * P : o * (N + NQ) + (t + 1) * P],
+                    lhsT=k_codes[:, t, o, :].bitcast(FP4X4),
+                    lhsT_scale=planes[:, o * SCALES + t * P : o * SCALES + (t + 1) * P],
                     rhs=qw[:, o, :].bitcast(FP8X4),
-                    rhs_scale=planes[:, o * (N + NQ) + N : (o + 1) * (N + NQ)],
+                    rhs_scale=planes[:, o * SCALES + N : (o + 1) * SCALES],
                     start=(o == 0),
                     stop=(o == PASSES - 1),
                 )
             if t % 2 == 1:
                 nc.scalar.activation(p_sb[:, t // 2], scores[t // 2][:].rearrange("p r q -> p q r"), ACT.Silu, bias=no_bias[:])
-
-        spare = ps.tile([P, P], F32, name="spare")
         nc.tensor.transpose(spare[:], p_sb[:, 0, 0 : NQ // 2, :].rearrange("p q r -> p (q r)"), ident[:])
+
         nc.vector.tensor_copy(
             v_g[:].rearrange("p (u b j r) -> p b u r j", u=2, j=RUN, r=2), v_pool[:].indirect(offsets[:])
         )
-        w_in = sb.tile([P, NQ, PACK], BF16, name="w_in", align_bytes=256)
-        spans = [slice(h * NQ // 2, (h + 1) * NQ // 2) for h in range(2)]
-        w_pairs = w_in[:].rearrange("p q (u r) -> p q u r", r=2)
-        p_pairs = p_sb[:].rearrange("p u q r -> p q u r")
-        vs_pairs = vs_t[:, P - 1 : P - 1 + PACK].unsqueeze(1).to_broadcast([P, NQ, PACK]).rearrange("p q (u r) -> p q u r", r=2)
-        nc.vector.tensor_tensor(w_pairs, p_pairs, vs_pairs, ALU.mult)
+        nc.vector.tensor_tensor(
+            w_in[:].rearrange("p q (u r) -> p q u r", r=2),
+            p_sb[:].rearrange("p u q r -> p q u r"),
+            vs_t[:, P - 1 : P - 1 + PACK].unsqueeze(1).to_broadcast([P, NQ, PACK]).rearrange("p q (u r) -> p q u r", r=2),
+            ALU.mult,
+        )
         v_t = ps.tile([P, 2, DV], F32, name="v_t", tag="bank0")
         v_words = v_g[:].bitcast(F32)
         for u in range(2):
             nc.tensor.transpose(v_t[:, u, :], v_words[:, u * P : (u + 1) * P], ident[:])
-        for es in spans:
+
+        halves = [slice(h * DV // 2, (h + 1) * DV // 2) for h in range(2)]
+        for es in halves:
             nc.scalar.copy(v_in[:, es, :].bitcast(F32), v_t[:, :, es].rearrange("p u e -> p e u"))
         nc.vector.quantize_mx(out=w_codes[:].bitcast(FP8X4), scales=w_scales[:], in_=w_in[:].rearrange("p q t -> p (q t)"))
-        for es in spans:
+        for es in halves:
             nc.vector.quantize_mx(out=v_codes[:, es].bitcast(FP8X4), scales=v_scales[:, es], in_=v_in[:, es, :].rearrange("p e t -> p (e t)"))
-        for h, es in enumerate(spans):
+        for h, es in enumerate(halves):
             nc.tensor.matmul_mx(
                 out=y_ps[h][:],
                 lhsT=w_codes[:].bitcast(FP8X4),
@@ -150,6 +155,6 @@ def tile_attend_silu_topkq128n512t2048_kernel(tc, q_words, q_scales, k_words, k_
                 start=True,
                 stop=True,
             )
-        nc.scalar.activation(y_sb[:, spans[0]], y_ps[0][:], ACT.Copy, scale=1.0 / 16.0)
-        nc.scalar.activation(y_sb[:, spans[1]], y_ps[1][:], ACT.Copy, scale=1.0 / 16.0)
+        for h, es in enumerate(halves):
+            nc.scalar.activation(y_sb[:, es], y_ps[h][:], ACT.Copy, scale=1.0 / 16.0)
         nc.sync.dma_start(out[0], y_sb[:])

@@ -49,11 +49,11 @@ def tile_attend_silu_topkq128n512t2048_kernel(tc, q_words, q_scales, k_words, k_
         qw = sb.tile([P, PASSES, NQ], I32, name="qw", align_bytes=ALIGN)
         ident = sb.tile([P, P], F32, name="ident", align_bytes=ALIGN)
         warm = sb.tile([P, 1], F32, name="warm")
-        ks_g = placed.tile([P, N], U8, name="ks_g", offset=WORD * T)
+        ks_g = [placed.tile([P, N // 2], U8, name="ks_g%d" % h, offset=WORD * T + h * N // 2) for h in range(2)]
         staged = sb.tile([P, SCALES], U8, name="staged", align_bytes=ALIGN)
         planes = sb.tile([P, PASSES * SCALES + WORD], U8, name="planes", align_bytes=ALIGN)
         vs_g = sb.tile([P, N], F32, name="vs_g", align_bytes=ALIGN)
-        kw_g = sb.tile([P, N], U32, name="kw_g", align_bytes=ALIGN)
+        kw_g = [sb.tile([P, N // 2], U32, name="kw_g%d" % h, align_bytes=ALIGN) for h in range(2)]
         k_codes = sb.tile([P, PACK, PASSES, P], U16, name="k_codes", align_bytes=ALIGN)
         v_g = sb.tile([P, N], BF16, name="v_g", align_bytes=ALIGN)
         v_in = sb.tile([P, DV, PACK], BF16, name="v_in", align_bytes=ALIGN)
@@ -86,12 +86,15 @@ def tile_attend_silu_topkq128n512t2048_kernel(tc, q_words, q_scales, k_words, k_
         make_identity(nc, ident[:])
         nc.scalar.activation(warm[:], zero, ACT.Silu)
 
-        nc.vector.tensor_copy(ks_g[:], ks_pool[:, 0:T].indirect(offsets[:]))
-        nc.vector.tensor_copy(
-            staged[:].bitcast(I32)[:, 0 : N // WORD].rearrange("p (t b w) -> p t b w", t=PACK, w=RUN // WORD),
-            ks_g[:].bitcast(I32).rearrange("p (b t w) -> p t b w", t=PACK, w=RUN // WORD),
-        )
-        no_bias = placed.tile([P, 1], F32, name="no_bias", offset=WORD * T)
+        list_halves = [offsets[:, h * N // 32 : (h + 1) * N // 32] for h in range(2)]
+        for h in range(2):
+            nc.vector.tensor_copy(ks_g[h][:], ks_pool[:, 0:T].indirect(list_halves[h]))
+        for h in range(2):
+            nc.vector.tensor_copy(
+                staged[:].bitcast(I32)[:, 0 : N // WORD].rearrange("p (t h b w) -> p h t b w", t=PACK, h=2, w=RUN // WORD)[:, h],
+                ks_g[h][:].bitcast(I32).rearrange("p (b t w) -> p t b w", t=PACK, w=RUN // WORD),
+            )
+        no_bias = placed.tile([P, 1], F32, name="no_bias", offset=WORD * T + N // 2)
         nc.scalar.copy(no_bias[:], zero)
         for a in range(P // QUAD):
             nc.sync.dma_start(
@@ -107,10 +110,14 @@ def tile_attend_silu_topkq128n512t2048_kernel(tc, q_words, q_scales, k_words, k_
         for t in reversed(range(PACK)):
             nc.tensor.transpose(vs_t[:, t : t + P], vs_g[:, t * P : (t + 1) * P], ident[:])
 
-        nc.vector.tensor_copy(kw_g[:], kw_pool[:].bitcast(U32).indirect(offsets[:]))
-        kw_by_place = kw_g[:].bitcast(U16).rearrange("p (b t j o) -> p t o b j", t=PACK, j=RUN, o=PASSES)
+        for h in range(2):
+            nc.vector.tensor_copy(kw_g[h][:], kw_pool[:].bitcast(U32).indirect(list_halves[h]))
+        for h, ts in ((0, slice(0, PACK)), (1, slice(0, 1)), (1, slice(1, PACK))):
+            nc.vector.tensor_copy(
+                k_codes[:, ts, :, h * P // 2 : (h + 1) * P // 2].rearrange("p t o (b j) -> p t o b j", j=RUN),
+                kw_g[h][:].bitcast(U16).rearrange("p (b t j o) -> p t o b j", t=PACK, j=RUN, o=PASSES)[:, ts],
+            )
         for t in range(PACK):
-            nc.vector.tensor_copy(k_codes[:, t].rearrange("p o (b j) -> p o b j", j=RUN), kw_by_place[:, t])
             for o in range(PASSES):
                 nc.tensor.matmul_mx(
                     out=scores[t // 2][:, t % 2, :],
@@ -128,12 +135,14 @@ def tile_attend_silu_topkq128n512t2048_kernel(tc, q_words, q_scales, k_words, k_
         nc.vector.tensor_copy(
             v_g[:].rearrange("p (u b j r) -> p b u r j", u=2, j=RUN, r=2), v_pool[:].indirect(offsets[:])
         )
-        nc.vector.tensor_tensor(
-            w_in[:].rearrange("p q (u r) -> p q u r", r=2),
-            p_sb[:].rearrange("p u q r -> p q u r"),
-            vs_t[:, P - 1 : P - 1 + PACK].unsqueeze(1).to_broadcast([P, NQ, PACK]).rearrange("p q (u r) -> p q u r", r=2),
-            ALU.mult,
-        )
+        q_halves = [slice(h * NQ // 2, (h + 1) * NQ // 2) for h in range(2)]
+        for qs in q_halves:
+            nc.vector.tensor_tensor(
+                w_in[:, qs, :].rearrange("p q (u r) -> p q u r", r=2),
+                p_sb[:, :, qs, :].rearrange("p u q r -> p q u r"),
+                vs_t[:, P - 1 : P - 1 + PACK].unsqueeze(1).to_broadcast([P, NQ // 2, PACK]).rearrange("p q (u r) -> p q u r", r=2),
+                ALU.mult,
+            )
         v_t = ps.tile([P, 2, DV], F32, name="v_t", tag="bank0")
         v_words = v_g[:].bitcast(F32)
         for u in range(2):
@@ -142,7 +151,8 @@ def tile_attend_silu_topkq128n512t2048_kernel(tc, q_words, q_scales, k_words, k_
         halves = [slice(h * DV // 2, (h + 1) * DV // 2) for h in range(2)]
         for es in halves:
             nc.scalar.copy(v_in[:, es, :].bitcast(F32), v_t[:, :, es].rearrange("p u e -> p e u"))
-        nc.vector.quantize_mx(out=w_codes[:].bitcast(FP8X4), scales=w_scales[:], in_=w_in[:].rearrange("p q t -> p (q t)"))
+        for qs in q_halves:
+            nc.vector.quantize_mx(out=w_codes[:, qs].bitcast(FP8X4), scales=w_scales[:, qs], in_=w_in[:, qs, :].rearrange("p q t -> p (q t)"))
         for es in halves:
             nc.vector.quantize_mx(out=v_codes[:, es].bitcast(FP8X4), scales=v_scales[:, es], in_=v_in[:, es, :].rearrange("p e t -> p (e t)"))
         for h, es in enumerate(halves):

@@ -28,7 +28,7 @@ ROWS = 4
 SCALES = N + NQ
 WORD = 4
 ALIGN = 256
-EARLY = 1152
+EARLY = 1088
 
 FLOPS = 2 * NQ * N * D + 2 * NQ * N * DV
 BYTES = 2 * 128 * 128 * 4 + 2 * 16 * 128 + 128 * T * 4 + 2 * 16 * T + DV * T * 4 + T * 4 + 128 * 32 * 2 + NQ * DV * 4
@@ -117,6 +117,7 @@ def tile_attend_silu_topkq128n512t2048_kernel(tc, q_words, q_scales, k_words, k_
                 k_codes[:, ts, :, h * P // 2 : (h + 1) * P // 2].rearrange("p t o (b j) -> p t o b j", j=RUN),
                 kw_g[h][:].bitcast(U16).rearrange("p (b t j o) -> p t o b j", t=PACK, j=RUN, o=PASSES)[:, ts],
             )
+        q_halves = [slice(h * NQ // 2, (h + 1) * NQ // 2) for h in range(2)]
         for t in range(PACK):
             for o in range(PASSES):
                 nc.tensor.matmul_mx(
@@ -129,13 +130,13 @@ def tile_attend_silu_topkq128n512t2048_kernel(tc, q_words, q_scales, k_words, k_
                     stop=(o == PASSES - 1),
                 )
             if t % 2 == 1:
-                nc.scalar.activation(p_sb[:, t // 2], scores[t // 2][:].rearrange("p r q -> p q r"), ACT.Silu, bias=no_bias[:])
+                for qs in q_halves if t == PACK - 1 else [slice(0, NQ)]:
+                    nc.scalar.activation(p_sb[:, t // 2, qs], scores[t // 2][:, :, qs].rearrange("p r q -> p q r"), ACT.Silu, bias=no_bias[:])
         nc.tensor.transpose(spare[:], p_sb[:, 0, 0 : NQ // 2, :].rearrange("p q r -> p (q r)"), ident[:])
 
         nc.vector.tensor_copy(
             v_g[:].rearrange("p (u b j r) -> p b u r j", u=2, j=RUN, r=2), v_pool[:].indirect(offsets[:])
         )
-        q_halves = [slice(h * NQ // 2, (h + 1) * NQ // 2) for h in range(2)]
         for qs in q_halves:
             nc.vector.tensor_tensor(
                 w_in[:, qs, :].rearrange("p q (u r) -> p q u r", r=2),

@@ -48,7 +48,7 @@ def tile_attend_silu_topkq128n512t2048_kernel(tc, q_words, q_scales, k_words, k_
         v_pool = placed.tile([P, T], F32, name="v_pool", offset=0, align_bytes=ALIGN)
         qw = sb.tile([P, PASSES, NQ], I32, name="qw", align_bytes=ALIGN)
         ident = sb.tile([P, P], F32, name="ident", align_bytes=ALIGN)
-        warm = sb.tile([P, 1], F32, name="warm")
+        early_bias = sb.tile([P, 1], F32, name="early_bias")
         ks_g = [placed.tile([P, N // 2], U8, name="ks_g%d" % h, offset=WORD * T + h * N // 2) for h in range(2)]
         staged = sb.tile([P, SCALES], U8, name="staged", align_bytes=ALIGN)
         planes = sb.tile([P, PASSES * SCALES + WORD], U8, name="planes", align_bytes=ALIGN)
@@ -84,7 +84,7 @@ def tile_attend_silu_topkq128n512t2048_kernel(tc, q_words, q_scales, k_words, k_
         nc.vector.memset(planes[:].bitcast(I32), 0)
         nc.gpsimd.memset(vs_pool[0 : P - 1, :].bitcast(I32), 0)
         make_identity(nc, ident[:])
-        nc.scalar.activation(warm[:], zero, ACT.Silu)
+        nc.scalar.activation(early_bias[:], zero, ACT.Silu)
 
         list_halves = [offsets[:, h * N // 32 : (h + 1) * N // 32] for h in range(2)]
         for h in range(2):
@@ -131,7 +131,7 @@ def tile_attend_silu_topkq128n512t2048_kernel(tc, q_words, q_scales, k_words, k_
                 )
             if t % 2 == 1:
                 for qs in q_halves if t == PACK - 1 else [slice(0, NQ)]:
-                    nc.scalar.activation(p_sb[:, t // 2, qs], scores[t // 2][:, :, qs].rearrange("p r q -> p q r"), ACT.Silu, bias=no_bias[:])
+                    nc.scalar.activation(p_sb[:, t // 2, qs], scores[t // 2][:, :, qs].rearrange("p r q -> p q r"), ACT.Silu, bias=(no_bias, early_bias)[t // 2][:])
         nc.tensor.transpose(spare[:], p_sb[:, 0, 0 : NQ // 2, :].rearrange("p q r -> p (q r)"), ident[:])
 
         nc.vector.tensor_copy(

@@ -66,8 +66,7 @@ def tile_attend_silu_topkq128n512t2048_kernel(tc, q_words, q_scales, k_words, k_
         w_in = sb.tile([P, NQ, PACK], BF16, name="w_in", align_bytes=ALIGN)
 
         scores = [ps.tile([P, 2, NQ], F32, name="score%d" % u, tag="bank%d" % u) for u in range(2)]
-        vs_t = ps.tile([P, P + PACK - 1], F32, name="vs_t")
-        spare = ps.tile([P, P], F32, name="spare")
+        vs_t = ps.tile([P, N], F32, name="vs_t")
         y_ps = [ps.tile([P, DV // 2], F32, name="y_ps%d" % h) for h in range(2)]
 
         last = P - QUAD
@@ -117,6 +116,15 @@ def tile_attend_silu_topkq128n512t2048_kernel(tc, q_words, q_scales, k_words, k_
                 k_codes[:, ts, :, h * P // 2 : (h + 1) * P // 2].rearrange("p t o (b j) -> p t o b j", j=RUN),
                 kw_g[h][:].bitcast(U16).rearrange("p (b t j o) -> p t o b j", t=PACK, j=RUN, o=PASSES)[:, ts],
             )
+        nc.tensor.matmul_mx(
+            out=vs_t[:, N // 2 : N],
+            lhsT=kw_g[1][:, 0 : P // 2].bitcast(U16).bitcast(FP4X4),
+            lhsT_scale=staged[:, 0:P],
+            rhs=qw[:].rearrange("p o q -> p (o q)").bitcast(FP8X4),
+            rhs_scale=staged[:, 0 : PASSES * NQ],
+            start=True,
+            stop=True,
+        )
         q_halves = [slice(h * NQ // 2, (h + 1) * NQ // 2) for h in range(2)]
         for t in range(PACK):
             for o in range(PASSES):
@@ -132,7 +140,6 @@ def tile_attend_silu_topkq128n512t2048_kernel(tc, q_words, q_scales, k_words, k_
             if t % 2 == 1:
                 for qs in q_halves if t == PACK - 1 else [slice(0, NQ)]:
                     nc.scalar.activation(p_sb[:, t // 2, qs], scores[t // 2][:, :, qs].rearrange("p r q -> p q r"), ACT.Silu, bias=(no_bias, early_bias)[t // 2][:])
-        nc.tensor.transpose(spare[:], p_sb[:, 0, 0 : NQ // 2, :].rearrange("p q r -> p (q r)"), ident[:])
 
         nc.vector.tensor_copy(
             v_g[:].rearrange("p (u b j r) -> p b u r j", u=2, j=RUN, r=2), v_pool[:].indirect(offsets[:])

@@ -28,7 +28,7 @@ ROWS = 4
 SCALES = N + NQ
 WORD = 4
 ALIGN = 256
-EARLY = 1088
+EARLY = 1216
 
 FLOPS = 2 * NQ * N * D + 2 * NQ * N * DV
 BYTES = 2 * 128 * 128 * 4 + 2 * 16 * 128 + 128 * T * 4 + 2 * 16 * T + DV * T * 4 + T * 4 + 128 * 32 * 2 + NQ * DV * 4
@@ -70,11 +70,11 @@ def tile_attend_silu_topkq128n512t2048_kernel(tc, q_words, q_scales, k_words, k_
         y_ps = [ps.tile([P, DV // 2], F32, name="y_ps%d" % h) for h in range(2)]
 
         last = P - QUAD
-        nc.sync.dma_start(ks_pool[:].bitcast(I32)[last:P, 0 : T // WORD], k_scales.bitcast(I32).rearrange("o f c -> f o c"))
+        nc.scalar.dma_start(ks_pool[:].bitcast(I32)[last:P, 0 : T // WORD], k_scales.bitcast(I32).rearrange("o f c -> f o c"))
         nc.sync.dma_start(offsets[:], offs)
         nc.sync.dma_start(qw[:], q_words[0].rearrange("o g q r -> g o (q r)").bitcast(I32))
         nc.sync.dma_start(vs_pool[P - 1 : P, :], vs[0:1, :])
-        nc.sync.dma_start(staged[:].bitcast(I32)[last:P, N // WORD :], q_scales[0].bitcast(I32).rearrange("o f c -> f o c"))
+        nc.scalar.dma_start(staged[:].bitcast(I32)[last:P, N // WORD :], q_scales[0].bitcast(I32).rearrange("o f c -> f o c"))
         nc.sync.dma_start(kw_pool[:], k_words[0].rearrange("g t r -> g (t r)").bitcast(I32))
         nc.sync.dma_start(v_pool[:, 0:EARLY], vT[:, 0:EARLY])
         zero = v_pool[:, EARLY : EARLY + 1]

@@ -29,6 +29,7 @@ SCALES = N + NQ
 WORD = 4
 ALIGN = 256
 EARLY = 1216
+SHARE = 256
 
 FLOPS = 2 * NQ * N * D + 2 * NQ * N * DV
 BYTES = 2 * 128 * 128 * 4 + 2 * 16 * 128 + 128 * T * 4 + 2 * 16 * T + DV * T * 4 + T * 4 + 128 * 32 * 2 + NQ * DV * 4
@@ -42,14 +43,14 @@ def tile_attend_silu_topkq128n512t2048_kernel(tc, q_words, q_scales, k_words, k_
         ps = ctx.enter_context(tc.psum_pool(name="ps", bufs=1))
 
         offsets = sb.tile([P, N // 16], U16, name="offsets")
-        ks_pool = sb.tile([P, T + WORD], U8, name="ks_pool", align_bytes=ALIGN)
+        ks_pool = sb.tile([P, T], U8, name="ks_pool", align_bytes=ALIGN)
         vs_pool = sb.tile([P, T], F32, name="vs_pool", align_bytes=ALIGN)
         kw_pool = sb.tile([P, T], I32, name="kw_pool", align_bytes=ALIGN)
         v_pool = placed.tile([P, T], F32, name="v_pool", offset=0, align_bytes=ALIGN)
         qw = sb.tile([P, PASSES, NQ], I32, name="qw", align_bytes=ALIGN)
         ident = sb.tile([P, P], F32, name="ident", align_bytes=ALIGN)
         early_bias = sb.tile([P, 1], F32, name="early_bias")
-        ks_g = [placed.tile([P, N // 2], U8, name="ks_g%d" % h, offset=WORD * T + h * N // 2) for h in range(2)]
+        ks_g = placed.tile([P, N], U8, name="ks_g", offset=WORD * T)
         staged = sb.tile([P, SCALES], U8, name="staged", align_bytes=ALIGN)
         planes = sb.tile([P, PASSES * SCALES + WORD], U8, name="planes", align_bytes=ALIGN)
         vs_g = sb.tile([P, N], F32, name="vs_g", align_bytes=ALIGN)
@@ -62,15 +63,16 @@ def tile_attend_silu_topkq128n512t2048_kernel(tc, q_words, q_scales, k_words, k_
         v_codes = sb.tile([P, DV], U32, name="v_codes", align_bytes=ALIGN)
         v_scales = sb.tile([P, DV], U8, name="v_scales", align_bytes=ALIGN)
         y_sb = sb.tile([P, DV], F32, name="y_sb", align_bytes=ALIGN)
-        p_sb = sb.tile([P, 2, NQ, 2], F32, name="p_sb", align_bytes=ALIGN)
+        p_sb = placed.tile([P, NQ, PACK], F32, name="p_sb", offset=0, align_bytes=ALIGN)
         w_in = sb.tile([P, NQ, PACK], BF16, name="w_in", align_bytes=ALIGN)
 
-        scores = [ps.tile([P, 2, NQ], F32, name="score%d" % u, tag="bank%d" % u) for u in range(2)]
+        scores = ps.tile([P, PACK, NQ], F32, name="scores")
         vs_t = ps.tile([P, N], F32, name="vs_t")
+        v_t = ps.tile([P, 2, DV], F32, name="v_t")
         y_ps = [ps.tile([P, DV // 2], F32, name="y_ps%d" % h) for h in range(2)]
 
         last = P - QUAD
-        nc.scalar.dma_start(ks_pool[:].bitcast(I32)[last:P, 0 : T // WORD], k_scales.bitcast(I32).rearrange("o f c -> f o c"))
+        nc.scalar.dma_start(ks_pool[:].bitcast(I32)[last:P, :], k_scales.bitcast(I32).rearrange("o f c -> f o c"))
         nc.sync.dma_start(offsets[:], offs)
         nc.sync.dma_start(qw[:], q_words[0].rearrange("o g q r -> g o (q r)").bitcast(I32))
         nc.sync.dma_start(vs_pool[P - 1 : P, :], vs[0:1, :])
@@ -85,16 +87,10 @@ def tile_attend_silu_topkq128n512t2048_kernel(tc, q_words, q_scales, k_words, k_
         make_identity(nc, ident[:])
         nc.scalar.activation(early_bias[:], zero, ACT.Silu)
 
-        list_halves = [offsets[:, h * N // 32 : (h + 1) * N // 32] for h in range(2)]
-        for h in range(2):
-            nc.vector.tensor_copy(ks_g[h][:], ks_pool[:, 0:T].indirect(list_halves[h]))
-        for h in range(2):
-            nc.vector.tensor_copy(
-                staged[:].bitcast(I32)[:, 0 : N // WORD].rearrange("p (t h b w) -> p h t b w", t=PACK, h=2, w=RUN // WORD)[:, h],
-                ks_g[h][:].bitcast(I32).rearrange("p (b t w) -> p t b w", t=PACK, w=RUN // WORD),
-            )
-        no_bias = placed.tile([P, 1], F32, name="no_bias", offset=WORD * T + N // 2)
-        nc.scalar.copy(no_bias[:], zero)
+        nc.vector.tensor_copy(ks_g[:].rearrange("p (t s) -> p s t", t=PACK), ks_pool[:].indirect(offsets[:]))
+        nc.vector.tensor_copy(staged[:].bitcast(I32)[:, 0 : N // WORD], ks_g[:].bitcast(I32))
+        no_bias = placed.tile([P, 1], F32, name="no_bias", offset=WORD * T)
+        nc.vector.tensor_copy(no_bias[:], zero)
         for a in range(P // QUAD):
             nc.sync.dma_start(
                 planes[:].bitcast(I32)[a * QUAD : a * QUAD + ROWS, 0 : PASSES * SCALES // WORD].rearrange("i (o c) -> i o c", o=PASSES),
@@ -102,34 +98,22 @@ def tile_attend_silu_topkq128n512t2048_kernel(tc, q_words, q_scales, k_words, k_
             )
         nc.sync.dma_start(v_pool[:, EARLY:T], vT[:, EARLY:T])
 
-        nc.vector.tensor_copy(
-            vs_g[:].bitcast(U32).rearrange("p (t b j) -> p b t j", t=PACK, j=RUN),
-            vs_pool[:].bitcast(U32).indirect(offsets[:]),
-        )
+        nc.scalar.activation(vs_g[:], vs_pool[:].indirect(offsets[:]), ACT.Copy)
         for t in reversed(range(PACK)):
-            nc.tensor.transpose(vs_t[:, t : t + P], vs_g[:, t * P : (t + 1) * P], ident[:])
+            nc.tensor.transpose(vs_t[:, t : t + P], vs_g[:, t:N:PACK], ident[:])
 
+        list_halves = [offsets[:, h * N // 32 : (h + 1) * N // 32] for h in range(2)]
         for h in range(2):
-            nc.vector.tensor_copy(kw_g[h][:], kw_pool[:].bitcast(U32).indirect(list_halves[h]))
+            nc.vector.tensor_copy(kw_g[h][:].rearrange("p (t s) -> p s t", t=PACK), kw_pool[:].bitcast(U32).indirect(list_halves[h]))
         for h, ts in ((0, slice(0, PACK)), (1, slice(0, 1)), (1, slice(1, PACK))):
             nc.vector.tensor_copy(
-                k_codes[:, ts, :, h * P // 2 : (h + 1) * P // 2].rearrange("p t o (b j) -> p t o b j", j=RUN),
-                kw_g[h][:].bitcast(U16).rearrange("p (b t j o) -> p t o b j", t=PACK, j=RUN, o=PASSES)[:, ts],
+                k_codes[:, ts, :, h * P // 2 : (h + 1) * P // 2],
+                kw_g[h][:].bitcast(U16).rearrange("p (t s o) -> p t o s", t=PACK, o=PASSES)[:, ts],
             )
-        nc.tensor.matmul_mx(
-            out=vs_t[:, N // 2 : N],
-            lhsT=kw_g[1][:, 0 : P // 2].bitcast(U16).bitcast(FP4X4),
-            lhsT_scale=staged[:, 0:P],
-            rhs=qw[:].rearrange("p o q -> p (o q)").bitcast(FP8X4),
-            rhs_scale=staged[:, 0 : PASSES * NQ],
-            start=True,
-            stop=True,
-        )
-        q_halves = [slice(h * NQ // 2, (h + 1) * NQ // 2) for h in range(2)]
         for t in range(PACK):
             for o in range(PASSES):
                 nc.tensor.matmul_mx(
-                    out=scores[t // 2][:, t % 2, :],
+                    out=scores[:, t, :],
                     lhsT=k_codes[:, t, o, :].bitcast(FP4X4),
                     lhsT_scale=planes[:, o * SCALES + t * P : o * SCALES + (t + 1) * P],
                     rhs=qw[:, o, :].bitcast(FP8X4),
@@ -137,25 +121,23 @@ def tile_attend_silu_topkq128n512t2048_kernel(tc, q_words, q_scales, k_words, k_
                     start=(o == 0),
                     stop=(o == PASSES - 1),
                 )
-            if t % 2 == 1:
-                for qs in q_halves if t == PACK - 1 else [slice(0, NQ)]:
-                    nc.scalar.activation(p_sb[:, t // 2, qs], scores[t // 2][:, :, qs].rearrange("p r q -> p q r"), ACT.Silu, bias=(no_bias, early_bias)[t // 2][:])
 
-        nc.vector.tensor_copy(
-            v_g[:].rearrange("p (u b j r) -> p b u r j", u=2, j=RUN, r=2), v_pool[:].indirect(offsets[:])
-        )
-        for qs in q_halves:
-            nc.vector.tensor_tensor(
-                w_in[:, qs, :].rearrange("p q (u r) -> p q u r", r=2),
-                p_sb[:, :, qs, :].rearrange("p u q r -> p q u r"),
-                vs_t[:, P - 1 : P - 1 + PACK].unsqueeze(1).to_broadcast([P, NQ // 2, PACK]).rearrange("p q (u r) -> p q u r", r=2),
-                ALU.mult,
-            )
-        v_t = ps.tile([P, 2, DV], F32, name="v_t", tag="bank0")
+        nc.vector.tensor_copy(v_g[:, 0:SHARE], v_pool[:].indirect(offsets[:, 0 : SHARE // 16]))
+        nc.scalar.activation(v_g[:, SHARE:N], v_pool[:].indirect(offsets[:, SHARE // 16 : N // 16]), ACT.Copy)
         v_words = v_g[:].bitcast(F32)
         for u in range(2):
-            nc.tensor.transpose(v_t[:, u, :], v_words[:, u * P : (u + 1) * P], ident[:])
+            nc.tensor.transpose(v_t[:, u, :], v_words[:, u : N // 2 : 2], ident[:])
 
+        q_halves = [slice(h * NQ // 2, (h + 1) * NQ // 2) for h in range(2)]
+        for qs, bias in zip(q_halves, (no_bias, early_bias)):
+            nc.scalar.activation(p_sb[:, qs], scores[:, :, qs].rearrange("p t q -> p q t"), ACT.Silu, bias=bias[:])
+        for qs in q_halves:
+            nc.vector.tensor_tensor(
+                w_in[:, qs, :],
+                p_sb[:, qs, :],
+                vs_t[:, P - 1 : P - 1 + PACK].unsqueeze(1).to_broadcast([P, NQ // 2, PACK]),
+                ALU.mult,
+            )
         halves = [slice(h * DV // 2, (h + 1) * DV // 2) for h in range(2)]
         for es in halves:
             nc.scalar.copy(v_in[:, es, :].bitcast(F32), v_t[:, :, es].rearrange("p u e -> p e u"))

@@ -43,16 +43,18 @@ def tile_attend_silu_topkq128n512t2048_kernel(tc, q_words, q_scales, k_words, k_
         ps = ctx.enter_context(tc.psum_pool(name="ps", bufs=1))
 
         offsets = sb.tile([P, N // 16], U16, name="offsets")
-        ks_pool = sb.tile([P, T], U8, name="ks_pool", align_bytes=ALIGN)
+        ks_pool = sb.tile([P, T + WORD], U8, name="ks_pool", align_bytes=ALIGN)
         vs_pool = sb.tile([P, T], F32, name="vs_pool", align_bytes=ALIGN)
         kw_pool = sb.tile([P, T], I32, name="kw_pool", align_bytes=ALIGN)
         v_pool = placed.tile([P, T], F32, name="v_pool", offset=0, align_bytes=ALIGN)
         qw = sb.tile([P, PASSES, NQ], I32, name="qw", align_bytes=ALIGN)
         ident = sb.tile([P, P], F32, name="ident", align_bytes=ALIGN)
         early_bias = sb.tile([P, 1], F32, name="early_bias")
-        ks_g = placed.tile([P, N], U8, name="ks_g", offset=WORD * T)
+        ks_g = [placed.tile([P, N // 2], U8, name="ks_g%d" % h, offset=WORD * T + h * N // 2) for h in range(2)]
         staged = sb.tile([P, SCALES], U8, name="staged", align_bytes=ALIGN)
         planes = sb.tile([P, PASSES * SCALES + WORD], U8, name="planes", align_bytes=ALIGN)
+        vs_l = sb.tile([P, N], F32, name="vs_l", align_bytes=ALIGN)
+        v_l = sb.tile([P, N - SHARE], BF16, name="v_l", align_bytes=ALIGN)
         vs_g = sb.tile([P, N], F32, name="vs_g", align_bytes=ALIGN)
         kw_g = [sb.tile([P, N // 2], U32, name="kw_g%d" % h, align_bytes=ALIGN) for h in range(2)]
         k_codes = sb.tile([P, PACK, PASSES, P], U16, name="k_codes", align_bytes=ALIGN)
@@ -72,7 +74,7 @@ def tile_attend_silu_topkq128n512t2048_kernel(tc, q_words, q_scales, k_words, k_
         y_ps = [ps.tile([P, DV // 2], F32, name="y_ps%d" % h) for h in range(2)]
 
         last = P - QUAD
-        nc.scalar.dma_start(ks_pool[:].bitcast(I32)[last:P, :], k_scales.bitcast(I32).rearrange("o f c -> f o c"))
+        nc.scalar.dma_start(ks_pool[:].bitcast(I32)[last:P, 0 : T // WORD], k_scales.bitcast(I32).rearrange("o f c -> f o c"))
         nc.sync.dma_start(offsets[:], offs)
         nc.sync.dma_start(qw[:], q_words[0].rearrange("o g q r -> g o (q r)").bitcast(I32))
         nc.sync.dma_start(vs_pool[P - 1 : P, :], vs[0:1, :])
@@ -87,9 +89,15 @@ def tile_attend_silu_topkq128n512t2048_kernel(tc, q_words, q_scales, k_words, k_
         make_identity(nc, ident[:])
         nc.scalar.activation(early_bias[:], zero, ACT.Silu)
 
-        nc.vector.tensor_copy(ks_g[:].rearrange("p (t s) -> p s t", t=PACK), ks_pool[:].indirect(offsets[:]))
-        nc.vector.tensor_copy(staged[:].bitcast(I32)[:, 0 : N // WORD], ks_g[:].bitcast(I32))
-        no_bias = placed.tile([P, 1], F32, name="no_bias", offset=WORD * T)
+        list_halves = [offsets[:, h * N // 32 : (h + 1) * N // 32] for h in range(2)]
+        for h in range(2):
+            nc.vector.tensor_copy(ks_g[h][:], ks_pool[:, 0:T].indirect(list_halves[h]))
+        for h in range(2):
+            nc.vector.tensor_copy(
+                staged[:].bitcast(I32)[:, 0 : N // WORD].rearrange("p (t h b w) -> p h t b w", t=PACK, h=2, w=RUN // WORD)[:, h],
+                ks_g[h][:].bitcast(I32).rearrange("p (b t w) -> p t b w", t=PACK, w=RUN // WORD),
+            )
+        no_bias = placed.tile([P, 1], F32, name="no_bias", offset=WORD * T + N // 2)
         nc.vector.tensor_copy(no_bias[:], zero)
         for a in range(P // QUAD):
             nc.sync.dma_start(
@@ -98,17 +106,17 @@ def tile_attend_silu_topkq128n512t2048_kernel(tc, q_words, q_scales, k_words, k_
             )
         nc.sync.dma_start(v_pool[:, EARLY:T], vT[:, EARLY:T])
 
-        nc.scalar.activation(vs_g[:], vs_pool[:].indirect(offsets[:]), ACT.Copy)
+        nc.scalar.activation(vs_l[:], vs_pool[:].indirect(offsets[:]), ACT.Copy)
+        nc.scalar.copy(vs_g[:].rearrange("p (t b j) -> p t b j", t=PACK, j=RUN), vs_l[:].rearrange("p (b t j) -> p t b j", t=PACK, j=RUN))
         for t in reversed(range(PACK)):
-            nc.tensor.transpose(vs_t[:, t : t + P], vs_g[:, t:N:PACK], ident[:])
+            nc.tensor.transpose(vs_t[:, t : t + P], vs_g[:, t * P : (t + 1) * P], ident[:])
 
-        list_halves = [offsets[:, h * N // 32 : (h + 1) * N // 32] for h in range(2)]
         for h in range(2):
-            nc.vector.tensor_copy(kw_g[h][:].rearrange("p (t s) -> p s t", t=PACK), kw_pool[:].bitcast(U32).indirect(list_halves[h]))
+            nc.vector.tensor_copy(kw_g[h][:], kw_pool[:].bitcast(U32).indirect(list_halves[h]))
         for h, ts in ((0, slice(0, PACK)), (1, slice(0, 1)), (1, slice(1, PACK))):
             nc.vector.tensor_copy(
-                k_codes[:, ts, :, h * P // 2 : (h + 1) * P // 2],
-                kw_g[h][:].bitcast(U16).rearrange("p (t s o) -> p t o s", t=PACK, o=PASSES)[:, ts],
+                k_codes[:, ts, :, h * P // 2 : (h + 1) * P // 2].rearrange("p t o (b j) -> p t o b j", j=RUN),
+                kw_g[h][:].bitcast(U16).rearrange("p (b t j o) -> p t o b j", t=PACK, j=RUN, o=PASSES)[:, ts],
             )
         for t in range(PACK):
             for o in range(PASSES):
@@ -122,11 +130,14 @@ def tile_attend_silu_topkq128n512t2048_kernel(tc, q_words, q_scales, k_words, k_
                     stop=(o == PASSES - 1),
                 )
 
-        nc.vector.tensor_copy(v_g[:, 0:SHARE], v_pool[:].indirect(offsets[:, 0 : SHARE // 16]))
-        nc.scalar.activation(v_g[:, SHARE:N], v_pool[:].indirect(offsets[:, SHARE // 16 : N // 16]), ACT.Copy)
+        v_dealt = v_g[:].rearrange("p (u b j r) -> p u b j r", u=2, j=RUN, r=2)
+        own = SHARE // QUAD
+        nc.vector.tensor_copy(v_dealt[:, :, 0:own].rearrange("p u b j r -> p b u r j"), v_pool[:].indirect(offsets[:, 0 : SHARE // 16]))
+        nc.scalar.activation(v_l[:], v_pool[:].indirect(offsets[:, SHARE // 16 : N // 16]), ACT.Copy)
+        nc.vector.tensor_copy(v_dealt[:, :, own:], v_l[:].rearrange("p (b u r j) -> p u b j r", u=2, j=RUN, r=2))
         v_words = v_g[:].bitcast(F32)
         for u in range(2):
-            nc.tensor.transpose(v_t[:, u, :], v_words[:, u : N // 2 : 2], ident[:])
+            nc.tensor.transpose(v_t[:, u, :], v_words[:, u * P : (u + 1) * P], ident[:])
 
         q_halves = [slice(h * NQ // 2, (h + 1) * NQ // 2) for h in range(2)]
         for qs, bias in zip(q_halves, (no_bias, early_bias)):

@@ -29,7 +29,7 @@ SCALES = N + NQ
 WORD = 4
 ALIGN = 256
 EARLY = 1216
-SHARE = 256
+SHARE = 288
 
 FLOPS = 2 * NQ * N * D + 2 * NQ * N * DV
 BYTES = 2 * 128 * 128 * 4 + 2 * 16 * 128 + 128 * T * 4 + 2 * 16 * T + DV * T * 4 + T * 4 + 128 * 32 * 2 + NQ * DV * 4
@@ -140,13 +140,14 @@ def tile_attend_silu_topkq128n512t2048_kernel(tc, q_words, q_scales, k_words, k_
             nc.tensor.transpose(v_t[:, u, :], v_words[:, u * P : (u + 1) * P], ident[:])
 
         q_halves = [slice(h * NQ // 2, (h + 1) * NQ // 2) for h in range(2)]
-        for qs, bias in zip(q_halves, (no_bias, early_bias)):
+        q_quarters = [slice(c * NQ // 4, (c + 1) * NQ // 4) for c in range(4)]
+        for qs, bias in zip(q_quarters, (no_bias, no_bias, early_bias, early_bias)):
             nc.scalar.activation(p_sb[:, qs], scores[:, :, qs].rearrange("p t q -> p q t"), ACT.Silu, bias=bias[:])
-        for qs in q_halves:
+        for qs in q_quarters:
             nc.vector.tensor_tensor(
                 w_in[:, qs, :],
                 p_sb[:, qs, :],
-                vs_t[:, P - 1 : P - 1 + PACK].unsqueeze(1).to_broadcast([P, NQ // 2, PACK]),
+                vs_t[:, P - 1 : P - 1 + PACK].unsqueeze(1).to_broadcast([P, NQ // 4, PACK]),
                 ALU.mult,
             )
         halves = [slice(h * DV // 2, (h + 1) * DV // 2) for h in range(2)]

@@ -55,7 +55,7 @@ def tile_attend_silu_topkq128n512t2048_kernel(tc, q_words, q_scales, k_words, k_
         planes = sb.tile([P, PASSES * SCALES + WORD], U8, name="planes", align_bytes=ALIGN)
         vs_l = sb.tile([P, N], F32, name="vs_l", align_bytes=ALIGN)
         v_l = sb.tile([P, N - SHARE], BF16, name="v_l", align_bytes=ALIGN)
-        vs_g = sb.tile([P, N], F32, name="vs_g", align_bytes=ALIGN)
+        vs_g = placed.tile([P, N], F32, name="vs_g", offset=WORD * T + 3 * N // 4, align_bytes=64)
         kw_g = [sb.tile([P, N // 2], U32, name="kw_g%d" % h, align_bytes=ALIGN) for h in range(2)]
         k_codes = sb.tile([P, PACK, PASSES, P], U16, name="k_codes", align_bytes=ALIGN)
         v_g = sb.tile([P, N], BF16, name="v_g", align_bytes=ALIGN)
@@ -85,7 +85,8 @@ def tile_attend_silu_topkq128n512t2048_kernel(tc, q_words, q_scales, k_words, k_
         nc.vector.memset(zero, 0.0)
         nc.vector.memset(ks_pool[:].bitcast(I32)[0:last, :], 0)
         nc.vector.memset(planes[:].bitcast(I32), 0)
-        nc.gpsimd.memset(vs_pool[0 : P - 1, :].bitcast(I32), 0)
+        nc.gpsimd.memset(vs_pool[0 : P - 1, 0 : T // 2].bitcast(I32), 0)
+        nc.vector.memset(vs_pool[0 : P - 1, T // 2 : T].bitcast(I32), 0)
         make_identity(nc, ident[:])
         nc.scalar.activation(early_bias[:], zero, ACT.Silu)
 

@@ -29,7 +29,7 @@ SCALES = N + NQ
 WORD = 4
 ALIGN = 256
 EARLY = 1216
-SHARE = 288
+HALF = N // 2
 
 FLOPS = 2 * NQ * N * D + 2 * NQ * N * DV
 BYTES = 2 * 128 * 128 * 4 + 2 * 16 * 128 + 128 * T * 4 + 2 * 16 * T + DV * T * 4 + T * 4 + 128 * 32 * 2 + NQ * DV * 4
@@ -54,7 +54,6 @@ def tile_attend_silu_topkq128n512t2048_kernel(tc, q_words, q_scales, k_words, k_
         staged = sb.tile([P, SCALES], U8, name="staged", align_bytes=ALIGN)
         planes = sb.tile([P, PASSES * SCALES + WORD], U8, name="planes", align_bytes=ALIGN)
         vs_l = sb.tile([P, N], F32, name="vs_l", align_bytes=ALIGN)
-        v_l = sb.tile([P, N - SHARE], BF16, name="v_l", align_bytes=ALIGN)
         vs_g = placed.tile([P, N], F32, name="vs_g", offset=WORD * T + 3 * N // 4, align_bytes=64)
         kw_g = [sb.tile([P, N // 2], U32, name="kw_g%d" % h, align_bytes=ALIGN) for h in range(2)]
         k_codes = sb.tile([P, PACK, PASSES, P], U16, name="k_codes", align_bytes=ALIGN)
@@ -93,11 +92,14 @@ def tile_attend_silu_topkq128n512t2048_kernel(tc, q_words, q_scales, k_words, k_
         list_halves = [offsets[:, h * N // 32 : (h + 1) * N // 32] for h in range(2)]
         for h in range(2):
             nc.vector.tensor_copy(ks_g[h][:], ks_pool[:, 0:T].indirect(list_halves[h]))
-        for h in range(2):
-            nc.vector.tensor_copy(
-                staged[:].bitcast(I32)[:, 0 : N // WORD].rearrange("p (t h b w) -> p h t b w", t=PACK, h=2, w=RUN // WORD)[:, h],
-                ks_g[h][:].bitcast(I32).rearrange("p (b t w) -> p t b w", t=PACK, w=RUN // WORD),
-            )
+        nc.vector.tensor_copy(
+            staged[:, 0:N].rearrange("p (t h s) -> p h t s", t=PACK, h=2)[:, 0],
+            ks_g[0][:].rearrange("p (s t) -> p t s", t=PACK),
+        )
+        nc.vector.tensor_copy(
+            staged[:].bitcast(I32)[:, 0 : N // WORD].rearrange("p (t h b w) -> p h t b w", t=PACK, h=2, w=RUN // WORD)[:, 1],
+            ks_g[1][:].bitcast(I32).rearrange("p (b t w) -> p t b w", t=PACK, w=RUN // WORD),
+        )
         no_bias = placed.tile([P, 1], F32, name="no_bias", offset=WORD * T + N // 2)
         nc.vector.tensor_copy(no_bias[:], zero)
         for a in range(P // QUAD):
@@ -108,16 +110,25 @@ def tile_attend_silu_topkq128n512t2048_kernel(tc, q_words, q_scales, k_words, k_
         nc.sync.dma_start(v_pool[:, EARLY:T], vT[:, EARLY:T])
 
         nc.scalar.activation(vs_l[:], vs_pool[:].indirect(offsets[:]), ACT.Copy)
-        nc.scalar.copy(vs_g[:].rearrange("p (t b j) -> p t b j", t=PACK, j=RUN), vs_l[:].rearrange("p (b t j) -> p t b j", t=PACK, j=RUN))
+        vs_dealt = vs_g[:].rearrange("p (t h s) -> p h t s", t=PACK, h=2)
+        nc.scalar.copy(vs_dealt[:, 0].rearrange("p t s -> p s t"), vs_l[:, 0:HALF].rearrange("p (s t) -> p s t", t=PACK))
+        nc.scalar.copy(
+            vs_dealt[:, 1].rearrange("p t (b j) -> p t b j", j=RUN),
+            vs_l[:, HALF:N].rearrange("p (b t j) -> p t b j", t=PACK, j=RUN),
+        )
         for t in reversed(range(PACK)):
             nc.tensor.transpose(vs_t[:, t : t + P], vs_g[:, t * P : (t + 1) * P], ident[:])
 
-        for h in range(2):
-            nc.vector.tensor_copy(kw_g[h][:], kw_pool[:].bitcast(U32).indirect(list_halves[h]))
-        for h, ts in ((0, slice(0, PACK)), (1, slice(0, 1)), (1, slice(1, PACK))):
+        nc.vector.tensor_copy(kw_g[0][:].rearrange("p (t s) -> p s t", t=PACK), kw_pool[:].bitcast(U32).indirect(list_halves[0]))
+        nc.vector.tensor_copy(kw_g[1][:], kw_pool[:].bitcast(U32).indirect(list_halves[1]))
+        nc.vector.tensor_copy(
+            k_codes[:, :, :, 0 : P // 2],
+            kw_g[0][:].bitcast(U16).rearrange("p (t s o) -> p t o s", t=PACK, o=PASSES),
+        )
+        for ts in (slice(0, 1), slice(1, PACK)):
             nc.vector.tensor_copy(
-                k_codes[:, ts, :, h * P // 2 : (h + 1) * P // 2].rearrange("p t o (b j) -> p t o b j", j=RUN),
-                kw_g[h][:].bitcast(U16).rearrange("p (b t j o) -> p t o b j", t=PACK, j=RUN, o=PASSES)[:, ts],
+                k_codes[:, ts, :, P // 2 : P].rearrange("p t o (b j) -> p t o b j", j=RUN),
+                kw_g[1][:].bitcast(U16).rearrange("p (b t j o) -> p t o b j", t=PACK, j=RUN, o=PASSES)[:, ts],
             )
         for t in range(PACK):
             for o in range(PASSES):
@@ -131,14 +142,11 @@ def tile_attend_silu_topkq128n512t2048_kernel(tc, q_words, q_scales, k_words, k_
                     stop=(o == PASSES - 1),
                 )
 
-        v_dealt = v_g[:].rearrange("p (u b j r) -> p u b j r", u=2, j=RUN, r=2)
-        own = SHARE // QUAD
-        nc.vector.tensor_copy(v_dealt[:, :, 0:own].rearrange("p u b j r -> p b u r j"), v_pool[:].indirect(offsets[:, 0 : SHARE // 16]))
-        nc.scalar.activation(v_l[:], v_pool[:].indirect(offsets[:, SHARE // 16 : N // 16]), ACT.Copy)
-        nc.vector.tensor_copy(v_dealt[:, :, own:], v_l[:].rearrange("p (b u r j) -> p u b j r", u=2, j=RUN, r=2))
-        v_words = v_g[:].bitcast(F32)
+        nc.scalar.activation(v_g[:, 0:HALF], v_pool[:].indirect(list_halves[0]), ACT.Copy)
+        nc.vector.tensor_copy(v_g[:, HALF:N].rearrange("p (b j t) -> p b t j", j=RUN, t=PACK), v_pool[:].indirect(list_halves[1]))
+        v_words = v_g[:].bitcast(F32).rearrange("p (s u) -> p u s", u=2)
         for u in range(2):
-            nc.tensor.transpose(v_t[:, u, :], v_words[:, u * P : (u + 1) * P], ident[:])
+            nc.tensor.transpose(v_t[:, u, :], v_words[:, u], ident[:])
 
         q_halves = [slice(h * NQ // 2, (h + 1) * NQ // 2) for h in range(2)]
         q_quarters = [slice(c * NQ // 4, (c + 1) * NQ // 4) for c in range(4)]

@@ -30,6 +30,9 @@ WORD = 4
 ALIGN = 256
 EARLY = 1216
 HALF = N // 2
+PIECES = 4
+SPARE = PIECES * PACK
+HELD = WORD * (T + N)
 
 FLOPS = 2 * NQ * N * D + 2 * NQ * N * DV
 BYTES = 2 * 128 * 128 * 4 + 2 * 16 * 128 + 128 * T * 4 + 2 * 16 * T + DV * T * 4 + T * 4 + 128 * 32 * 2 + NQ * DV * 4
@@ -46,15 +49,15 @@ def tile_attend_silu_topkq128n512t2048_kernel(tc, q_words, q_scales, k_words, k_
         ks_pool = sb.tile([P, T + WORD], U8, name="ks_pool", align_bytes=ALIGN)
         vs_pool = sb.tile([P, T], F32, name="vs_pool", align_bytes=ALIGN)
         kw_pool = sb.tile([P, T], I32, name="kw_pool", align_bytes=ALIGN)
-        v_pool = placed.tile([P, T], F32, name="v_pool", offset=0, align_bytes=ALIGN)
+        v_pool = placed.tile([P, T + SPARE], F32, name="v_pool", offset=0, align_bytes=ALIGN)
         qw = sb.tile([P, PASSES, NQ], I32, name="qw", align_bytes=ALIGN)
         ident = sb.tile([P, P], F32, name="ident", align_bytes=ALIGN)
         early_bias = sb.tile([P, 1], F32, name="early_bias")
-        ks_g = [placed.tile([P, N // 2], U8, name="ks_g%d" % h, offset=WORD * T + h * N // 2) for h in range(2)]
+        ks_g = [placed.tile([P, N // 2], U8, name="ks_g%d" % h, offset=HELD + h * N // 2) for h in range(2)]
         staged = sb.tile([P, SCALES], U8, name="staged", align_bytes=ALIGN)
         planes = sb.tile([P, PASSES * SCALES + WORD], U8, name="planes", align_bytes=ALIGN)
         vs_l = sb.tile([P, N], F32, name="vs_l", align_bytes=ALIGN)
-        vs_g = placed.tile([P, N], F32, name="vs_g", offset=WORD * T + 3 * N // 4, align_bytes=64)
+        vs_g = placed.tile([P, N], F32, name="vs_g", offset=HELD + 3 * N // 4, align_bytes=64)
         kw_g = [sb.tile([P, N // 2], U32, name="kw_g%d" % h, align_bytes=ALIGN) for h in range(2)]
         k_codes = sb.tile([P, PACK, PASSES, P], U16, name="k_codes", align_bytes=ALIGN)
         v_g = sb.tile([P, N], BF16, name="v_g", align_bytes=ALIGN)
@@ -64,7 +67,7 @@ def tile_attend_silu_topkq128n512t2048_kernel(tc, q_words, q_scales, k_words, k_
         v_codes = sb.tile([P, DV], U32, name="v_codes", align_bytes=ALIGN)
         v_scales = sb.tile([P, DV], U8, name="v_scales", align_bytes=ALIGN)
         y_sb = sb.tile([P, DV], F32, name="y_sb", align_bytes=ALIGN)
-        p_sb = placed.tile([P, NQ, PACK], F32, name="p_sb", offset=0, align_bytes=ALIGN)
+        p_sb = placed.tile([P, NQ // PIECES, PIECES, PACK], F32, name="p_sb", offset=WORD * T, align_bytes=ALIGN)
         w_in = sb.tile([P, NQ, PACK], BF16, name="w_in", align_bytes=ALIGN)
 
         scores = ps.tile([P, PACK, NQ], F32, name="scores")
@@ -82,12 +85,13 @@ def tile_attend_silu_topkq128n512t2048_kernel(tc, q_words, q_scales, k_words, k_
         nc.sync.dma_start(v_pool[:, 0:EARLY], vT[:, 0:EARLY])
         zero = v_pool[:, EARLY : EARLY + 1]
         nc.vector.memset(zero, 0.0)
+        nc.vector.memset(v_pool[:, T : T + SPARE], 0.0)
         nc.vector.memset(ks_pool[:].bitcast(I32)[0:last, :], 0)
         nc.vector.memset(planes[:].bitcast(I32), 0)
         nc.gpsimd.memset(vs_pool[0 : P - 1, 0 : T // 2].bitcast(I32), 0)
         nc.vector.memset(vs_pool[0 : P - 1, T // 2 : T].bitcast(I32), 0)
         make_identity(nc, ident[:])
-        nc.scalar.activation(early_bias[:], zero, ACT.Silu)
+        nc.scalar.activation(early_bias[:], v_pool[:, T : T + 1], ACT.Silu)
 
         list_halves = [offsets[:, h * N // 32 : (h + 1) * N // 32] for h in range(2)]
         for h in range(2):
@@ -100,7 +104,7 @@ def tile_attend_silu_topkq128n512t2048_kernel(tc, q_words, q_scales, k_words, k_
             staged[:].bitcast(I32)[:, 0 : N // WORD].rearrange("p (t h b w) -> p h t b w", t=PACK, h=2, w=RUN // WORD)[:, 1],
             ks_g[1][:].bitcast(I32).rearrange("p (b t w) -> p t b w", t=PACK, w=RUN // WORD),
         )
-        no_bias = placed.tile([P, 1], F32, name="no_bias", offset=WORD * T + N // 2)
+        no_bias = placed.tile([P, 1], F32, name="no_bias", offset=HELD + N // 2)
         nc.vector.tensor_copy(no_bias[:], zero)
         for a in range(P // QUAD):
             nc.sync.dma_start(
@@ -143,19 +147,19 @@ def tile_attend_silu_topkq128n512t2048_kernel(tc, q_words, q_scales, k_words, k_
                 )
 
         nc.scalar.activation(v_g[:, 0:HALF], v_pool[:].indirect(list_halves[0]), ACT.Copy)
-        nc.vector.tensor_copy(v_g[:, HALF:N].rearrange("p (b j t) -> p b t j", j=RUN, t=PACK), v_pool[:].indirect(list_halves[1]))
+        nc.vector.tensor_copy(v_g[:, HALF:N].rearrange("p (b j t) -> p b t j", j=RUN, t=PACK), v_pool[:, 0:T].indirect(list_halves[1]))
         v_words = v_g[:].bitcast(F32).rearrange("p (s u) -> p u s", u=2)
         for u in range(2):
             nc.tensor.transpose(v_t[:, u, :], v_words[:, u], ident[:])
 
         q_halves = [slice(h * NQ // 2, (h + 1) * NQ // 2) for h in range(2)]
         q_quarters = [slice(c * NQ // 4, (c + 1) * NQ // 4) for c in range(4)]
-        for qs, bias in zip(q_quarters, (no_bias, no_bias, early_bias, early_bias)):
-            nc.scalar.activation(p_sb[:, qs], scores[:, :, qs].rearrange("p t q -> p q t"), ACT.Silu, bias=bias[:])
-        for qs in q_quarters:
+        for c, (qs, bias) in enumerate(zip(q_quarters, (no_bias, no_bias, early_bias, early_bias))):
+            nc.scalar.activation(p_sb[:, :, c], scores[:, :, qs].rearrange("p t q -> p q t"), ACT.Silu, bias=bias[:])
+        for c, qs in enumerate(q_quarters):
             nc.vector.tensor_tensor(
                 w_in[:, qs, :],
-                p_sb[:, qs, :],
+                p_sb[:, :, c],
                 vs_t[:, P - 1 : P - 1 + PACK].unsqueeze(1).to_broadcast([P, NQ // 4, PACK]),
                 ALU.mult,
             )

@@ -75,21 +75,21 @@ def tile_attend_silu_topkq128n512t2048_kernel(tc, q_words, q_scales, k_words, k_
         v_t = ps.tile([P, 2, DV], F32, name="v_t")
         y_ps = [ps.tile([P, DV // 2], F32, name="y_ps%d" % h) for h in range(2)]
 
-        last = P - QUAD
-        nc.scalar.dma_start(ks_pool[:].bitcast(I32)[last:P, 0 : T // WORD], k_scales.bitcast(I32).rearrange("o f c -> f o c"))
+        first, behind = QUAD, 2 * QUAD
+        nc.scalar.dma_start(ks_pool[:].bitcast(I32)[first:behind, 0 : T // WORD], k_scales.bitcast(I32).rearrange("o f c -> f o c"))
         nc.sync.dma_start(offsets[:], offs)
-        nc.sync.dma_start(qw[:], q_words[0].rearrange("o g q r -> g o (q r)").bitcast(I32))
         nc.sync.dma_start(vs_pool[P - 1 : P, :], vs[0:1, :])
-        nc.scalar.dma_start(staged[:].bitcast(I32)[last:P, N // WORD :], q_scales[0].bitcast(I32).rearrange("o f c -> f o c"))
+        nc.sync.dma_start(qw[:], q_words[0].rearrange("o g q r -> g o (q r)").bitcast(I32))
+        nc.scalar.dma_start(staged[:].bitcast(I32)[first:behind, N // WORD :], q_scales[0].bitcast(I32).rearrange("o f c -> f o c"))
         nc.sync.dma_start(kw_pool[:], k_words[0].rearrange("g t r -> g (t r)").bitcast(I32))
         nc.sync.dma_start(v_pool[:, 0:EARLY], vT[:, 0:EARLY])
         zero = v_pool[:, EARLY : EARLY + 1]
         nc.vector.memset(zero, 0.0)
         nc.vector.memset(v_pool[:, T : T + SPARE], 0.0)
-        nc.vector.memset(ks_pool[:].bitcast(I32)[0:last, :], 0)
+        nc.vector.memset(ks_pool[:].bitcast(I32)[0:first, :], 0)
+        nc.vector.memset(ks_pool[:].bitcast(I32)[behind:P, :], 0)
         nc.vector.memset(planes[:].bitcast(I32), 0)
-        nc.gpsimd.memset(vs_pool[0 : P - 1, 0 : T // 2].bitcast(I32), 0)
-        nc.vector.memset(vs_pool[0 : P - 1, T // 2 : T].bitcast(I32), 0)
+        nc.gpsimd.memset(vs_pool[0 : P - 1, :].bitcast(I32), 0)
         make_identity(nc, ident[:])
         nc.scalar.activation(early_bias[:], v_pool[:, T : T + 1], ACT.Silu)
 
@@ -109,7 +109,7 @@ def tile_attend_silu_topkq128n512t2048_kernel(tc, q_words, q_scales, k_words, k_
         for a in range(P // QUAD):
             nc.sync.dma_start(
                 planes[:].bitcast(I32)[a * QUAD : a * QUAD + ROWS, 0 : PASSES * SCALES // WORD].rearrange("i (o c) -> i o c", o=PASSES),
-                staged[:].bitcast(I32)[last + a * ROWS * PASSES : last + (a + 1) * ROWS * PASSES, :],
+                staged[:].bitcast(I32)[first + a * ROWS * PASSES : first + (a + 1) * ROWS * PASSES, :],
             )
         nc.sync.dma_start(v_pool[:, EARLY:T], vT[:, EARLY:T])
 

@@ -31,7 +31,7 @@ ALIGN = 256
 EARLY = 1216
 HALF = N // 2
 PIECES = 4
-SPARE = PIECES * PACK
+SPARE = PIECES * PACK + 1
 HELD = WORD * (T + N)
 
 FLOPS = 2 * NQ * N * D + 2 * NQ * N * DV

@@ -28,7 +28,7 @@ ROWS = 4
 SCALES = N + NQ
 WORD = 4
 ALIGN = 256
-EARLY = 1216
+EARLY = 1344
 HALF = N // 2
 PIECES = 4
 SPARE = PIECES * PACK + 1
@@ -79,9 +79,9 @@ def tile_attend_silu_topkq128n512t2048_kernel(tc, q_words, q_scales, k_words, k_
         nc.scalar.dma_start(ks_pool[:].bitcast(I32)[first:behind, 0 : T // WORD], k_scales.bitcast(I32).rearrange("o f c -> f o c"))
         nc.sync.dma_start(offsets[:], offs)
         nc.sync.dma_start(vs_pool[P - 1 : P, :], vs[0:1, :])
-        nc.sync.dma_start(qw[:], q_words[0].rearrange("o g q r -> g o (q r)").bitcast(I32))
         nc.scalar.dma_start(staged[:].bitcast(I32)[first:behind, N // WORD :], q_scales[0].bitcast(I32).rearrange("o f c -> f o c"))
         nc.sync.dma_start(kw_pool[:], k_words[0].rearrange("g t r -> g (t r)").bitcast(I32))
+        nc.sync.dma_start(qw[:], q_words[0].rearrange("o g q r -> g o (q r)").bitcast(I32))
         nc.sync.dma_start(v_pool[:, 0:EARLY], vT[:, 0:EARLY])
         zero = v_pool[:, EARLY : EARLY + 1]
         nc.vector.memset(zero, 0.0)

@@ -28,7 +28,7 @@ ROWS = 4
 SCALES = N + NQ
 WORD = 4
 ALIGN = 256
-EARLY = 1344
+EARLY = 1152
 HALF = N // 2
 PIECES = 4
 SPARE = PIECES * PACK + 1

@@ -28,11 +28,13 @@ ROWS = 4
 SCALES = N + NQ
 WORD = 4
 ALIGN = 256
-EARLY = 1152
+EARLY = 1088
 HALF = N // 2
+CLEARED = 3 * T // 4
 PIECES = 4
 SPARE = PIECES * PACK + 1
 HELD = WORD * (T + N)
+KS_AT = HELD + (WORD + 1) * N
 
 FLOPS = 2 * NQ * N * D + 2 * NQ * N * DV
 BYTES = 2 * 128 * 128 * 4 + 2 * 16 * 128 + 128 * T * 4 + 2 * 16 * T + DV * T * 4 + T * 4 + 128 * 32 * 2 + NQ * DV * 4
@@ -46,8 +48,8 @@ def tile_attend_silu_topkq128n512t2048_kernel(tc, q_words, q_scales, k_words, k_
         ps = ctx.enter_context(tc.psum_pool(name="ps", bufs=1))
 
         offsets = sb.tile([P, N // 16], U16, name="offsets")
-        ks_pool = sb.tile([P, T + WORD], U8, name="ks_pool", align_bytes=ALIGN)
-        vs_pool = sb.tile([P, T], F32, name="vs_pool", align_bytes=ALIGN)
+        ks_pool = placed.tile([P, T + WORD], U8, name="ks_pool", offset=KS_AT, align_bytes=ALIGN)
+        vs_pool = sb.tile([P, T + 1], F32, name="vs_pool", align_bytes=ALIGN)
         kw_pool = sb.tile([P, T], I32, name="kw_pool", align_bytes=ALIGN)
         v_pool = placed.tile([P, T + SPARE], F32, name="v_pool", offset=0, align_bytes=ALIGN)
         qw = sb.tile([P, PASSES, NQ], I32, name="qw", align_bytes=ALIGN)
@@ -55,7 +57,7 @@ def tile_attend_silu_topkq128n512t2048_kernel(tc, q_words, q_scales, k_words, k_
         early_bias = sb.tile([P, 1], F32, name="early_bias")
         ks_g = [placed.tile([P, N // 2], U8, name="ks_g%d" % h, offset=HELD + h * N // 2) for h in range(2)]
         staged = sb.tile([P, SCALES], U8, name="staged", align_bytes=ALIGN)
-        planes = sb.tile([P, PASSES * SCALES + WORD], U8, name="planes", align_bytes=ALIGN)
+        planes = placed.tile([P, PASSES * SCALES], U8, name="planes", offset=KS_AT, align_bytes=ALIGN)
         vs_l = sb.tile([P, N], F32, name="vs_l", align_bytes=ALIGN)
         vs_g = placed.tile([P, N], F32, name="vs_g", offset=HELD + 3 * N // 4, align_bytes=64)
         kw_g = [sb.tile([P, N // 2], U32, name="kw_g%d" % h, align_bytes=ALIGN) for h in range(2)]
@@ -78,7 +80,7 @@ def tile_attend_silu_topkq128n512t2048_kernel(tc, q_words, q_scales, k_words, k_
         first, behind = QUAD, 2 * QUAD
         nc.scalar.dma_start(ks_pool[:].bitcast(I32)[first:behind, 0 : T // WORD], k_scales.bitcast(I32).rearrange("o f c -> f o c"))
         nc.sync.dma_start(offsets[:], offs)
-        nc.sync.dma_start(vs_pool[P - 1 : P, :], vs[0:1, :])
+        nc.sync.dma_start(vs_pool[P - 1 : P, 0:T], vs[0:1, :])
         nc.scalar.dma_start(staged[:].bitcast(I32)[first:behind, N // WORD :], q_scales[0].bitcast(I32).rearrange("o f c -> f o c"))
         nc.sync.dma_start(kw_pool[:], k_words[0].rearrange("g t r -> g (t r)").bitcast(I32))
         nc.sync.dma_start(qw[:], q_words[0].rearrange("o g q r -> g o (q r)").bitcast(I32))
@@ -88,8 +90,8 @@ def tile_attend_silu_topkq128n512t2048_kernel(tc, q_words, q_scales, k_words, k_
         nc.vector.memset(v_pool[:, T : T + SPARE], 0.0)
         nc.vector.memset(ks_pool[:].bitcast(I32)[0:first, :], 0)
         nc.vector.memset(ks_pool[:].bitcast(I32)[behind:P, :], 0)
-        nc.vector.memset(planes[:].bitcast(I32), 0)
-        nc.gpsimd.memset(vs_pool[0 : P - 1, :].bitcast(I32), 0)
+        nc.gpsimd.memset(vs_pool[0 : P - 1, 0:CLEARED].bitcast(I32), 0)
+        nc.vector.memset(vs_pool[0 : P - 1, CLEARED:].bitcast(I32), 0)
         make_identity(nc, ident[:])
         nc.scalar.activation(early_bias[:], v_pool[:, T : T + 1], ACT.Silu)
 
@@ -108,12 +110,12 @@ def tile_attend_silu_topkq128n512t2048_kernel(tc, q_words, q_scales, k_words, k_
         nc.vector.tensor_copy(no_bias[:], zero)
         for a in range(P // QUAD):
             nc.sync.dma_start(
-                planes[:].bitcast(I32)[a * QUAD : a * QUAD + ROWS, 0 : PASSES * SCALES // WORD].rearrange("i (o c) -> i o c", o=PASSES),
+                planes[:].bitcast(I32)[a * QUAD : a * QUAD + ROWS, :].rearrange("i (o c) -> i o c", o=PASSES),
                 staged[:].bitcast(I32)[first + a * ROWS * PASSES : first + (a + 1) * ROWS * PASSES, :],
             )
         nc.sync.dma_start(v_pool[:, EARLY:T], vT[:, EARLY:T])
 
-        nc.scalar.activation(vs_l[:], vs_pool[:].indirect(offsets[:]), ACT.Copy)
+        nc.scalar.activation(vs_l[:], vs_pool[:, 0:T].indirect(offsets[:]), ACT.Copy)
         vs_dealt = vs_g[:].rearrange("p (t h s) -> p h t s", t=PACK, h=2)
         nc.scalar.copy(vs_dealt[:, 0].rearrange("p t s -> p s t"), vs_l[:, 0:HALF].rearrange("p (s t) -> p s t", t=PACK))
         nc.scalar.copy(

@@ -22,7 +22,7 @@ DV = 128
 NQ = 128
 PASSES = 2
 PACK = 4
-RUN = 8
+RUN = 4
 QUAD = 32
 ROWS = 4
 SCALES = N + NQ
@@ -103,8 +103,8 @@ def tile_attend_silu_topkq128n512t2048_kernel(tc, q_words, q_scales, k_words, k_
             ks_g[0][:].rearrange("p (s t) -> p t s", t=PACK),
         )
         nc.vector.tensor_copy(
-            staged[:].bitcast(I32)[:, 0 : N // WORD].rearrange("p (t h b w) -> p h t b w", t=PACK, h=2, w=RUN // WORD)[:, 1],
-            ks_g[1][:].bitcast(I32).rearrange("p (b t w) -> p t b w", t=PACK, w=RUN // WORD),
+            staged[:].bitcast(I32)[:, 0 : N // WORD].rearrange("p (t h b) -> p h b t", t=PACK, h=2)[:, 1],
+            ks_g[1][:].bitcast(I32).rearrange("p (b t) -> p b t", t=PACK),
         )
         no_bias = placed.tile([P, 1], F32, name="no_bias", offset=HELD + N // 2)
         nc.vector.tensor_copy(no_bias[:], zero)

@@ -35,6 +35,7 @@ PIECES = 4
 SPARE = PIECES * PACK + 1
 HELD = WORD * (T + N)
 KS_AT = HELD + (WORD + 1) * N
+STAGED_AT = KS_AT + T + ALIGN
 
 FLOPS = 2 * NQ * N * D + 2 * NQ * N * DV
 BYTES = 2 * 128 * 128 * 4 + 2 * 16 * 128 + 128 * T * 4 + 2 * 16 * T + DV * T * 4 + T * 4 + 128 * 32 * 2 + NQ * DV * 4
@@ -56,7 +57,8 @@ def tile_attend_silu_topkq128n512t2048_kernel(tc, q_words, q_scales, k_words, k_
         ident = sb.tile([P, P], F32, name="ident", align_bytes=ALIGN)
         early_bias = sb.tile([P, 1], F32, name="early_bias")
         ks_g = [placed.tile([P, N // 2], U8, name="ks_g%d" % h, offset=HELD + h * N // 2) for h in range(2)]
-        staged = sb.tile([P, SCALES], U8, name="staged", align_bytes=ALIGN)
+        staged = placed.tile([P, SCALES], U8, name="staged", offset=STAGED_AT, align_bytes=ALIGN)
+        vs_last = placed.tile([P, P], F32, name="vs_last", offset=STAGED_AT, align_bytes=ALIGN)
         planes = placed.tile([P, PASSES * SCALES], U8, name="planes", offset=KS_AT, align_bytes=ALIGN)
         vs_l = sb.tile([P, N], F32, name="vs_l", align_bytes=ALIGN)
         vs_g = placed.tile([P, N], F32, name="vs_g", offset=HELD + 3 * N // 4, align_bytes=64)
@@ -116,13 +118,12 @@ def tile_attend_silu_topkq128n512t2048_kernel(tc, q_words, q_scales, k_words, k_
         nc.sync.dma_start(v_pool[:, EARLY:T], vT[:, EARLY:T])
 
         nc.scalar.activation(vs_l[:], vs_pool[:, 0:T].indirect(offsets[:]), ACT.Copy)
-        vs_dealt = vs_g[:].rearrange("p (t h s) -> p h t s", t=PACK, h=2)
-        nc.scalar.copy(vs_dealt[:, 0].rearrange("p t s -> p s t"), vs_l[:, 0:HALF].rearrange("p (s t) -> p s t", t=PACK))
-        nc.scalar.copy(
-            vs_dealt[:, 1].rearrange("p t (b j) -> p t b j", j=RUN),
-            vs_l[:, HALF:N].rearrange("p (b t j) -> p t b j", t=PACK, j=RUN),
-        )
-        for t in reversed(range(PACK)):
+        vs_dealt = vs_g[:].rearrange("p (t h s) -> p h t s", t=PACK, h=2)[:, :, 1:PACK]
+        vs_plain = vs_l[:, 0:HALF].rearrange("p (s t) -> p s t", t=PACK)
+        vs_runs = vs_l[:, HALF:N].rearrange("p (b t j) -> p t b j", t=PACK, j=RUN)
+        nc.scalar.copy(vs_dealt[:, 0].rearrange("p t s -> p s t"), vs_plain[:, :, 1:PACK])
+        nc.scalar.copy(vs_dealt[:, 1].rearrange("p t (b j) -> p t b j", j=RUN), vs_runs[:, 1:PACK])
+        for t in reversed(range(1, PACK)):
             nc.tensor.transpose(vs_t[:, t : t + P], vs_g[:, t * P : (t + 1) * P], ident[:])
 
         nc.vector.tensor_copy(kw_g[0][:].rearrange("p (t s) -> p s t", t=PACK), kw_pool[:].bitcast(U32).indirect(list_halves[0]))
@@ -147,6 +148,9 @@ def tile_attend_silu_topkq128n512t2048_kernel(tc, q_words, q_scales, k_words, k_
                     start=(o == 0),
                     stop=(o == PASSES - 1),
                 )
+        nc.scalar.copy(vs_last[:, 0 : P // 2], vs_plain[:, :, 0])
+        nc.scalar.copy(vs_last[:, P // 2 : P].rearrange("p (b j) -> p b j", j=RUN), vs_runs[:, 0])
+        nc.tensor.transpose(vs_t[:, 0:P], vs_last[:], ident[:])
 
         nc.scalar.activation(v_g[:, 0:HALF], v_pool[:].indirect(list_halves[0]), ACT.Copy)
         nc.vector.tensor_copy(v_g[:, HALF:N].rearrange("p (b j t) -> p b t j", j=RUN, t=PACK), v_pool[:, 0:T].indirect(list_halves[1]))

@@ -22,7 +22,6 @@ DV = 128
 NQ = 128
 PASSES = 2
 PACK = 4
-RUN = 4
 QUAD = 32
 ROWS = 4
 SCALES = N + NQ
@@ -30,12 +29,9 @@ WORD = 4
 ALIGN = 256
 EARLY = 1088
 HALF = N // 2
-CLEARED = 3 * T // 4
+CLEARED = T // 4
 PIECES = 4
-SPARE = PIECES * PACK + 1
-HELD = WORD * (T + N)
-KS_AT = HELD + (WORD + 1) * N
-STAGED_AT = KS_AT + T + ALIGN
+PLANES_AT = T - PASSES * SCALES
 
 FLOPS = 2 * NQ * N * D + 2 * NQ * N * DV
 BYTES = 2 * 128 * 128 * 4 + 2 * 16 * 128 + 128 * T * 4 + 2 * 16 * T + DV * T * 4 + T * 4 + 128 * 32 * 2 + NQ * DV * 4
@@ -49,20 +45,21 @@ def tile_attend_silu_topkq128n512t2048_kernel(tc, q_words, q_scales, k_words, k_
         ps = ctx.enter_context(tc.psum_pool(name="ps", bufs=1))
 
         offsets = sb.tile([P, N // 16], U16, name="offsets")
-        ks_pool = placed.tile([P, T + WORD], U8, name="ks_pool", offset=KS_AT, align_bytes=ALIGN)
+        ks_pool = placed.tile([P, T], U8, name="ks_pool", offset=0, align_bytes=ALIGN)
+        ks_g = sb.tile([P, N], U8, name="ks_g", align_bytes=ALIGN)
+        staged = sb.tile([P, SCALES // WORD], I32, name="staged", align_bytes=ALIGN)
+        planes = placed.tile([P, PASSES * SCALES], U8, name="planes", offset=PLANES_AT, align_bytes=ALIGN)
+        held_zero = placed.tile([P, 1], F32, name="held_zero", offset=0)
         vs_pool = sb.tile([P, T + 1], F32, name="vs_pool", align_bytes=ALIGN)
         kw_pool = sb.tile([P, T], I32, name="kw_pool", align_bytes=ALIGN)
-        v_pool = placed.tile([P, T + SPARE], F32, name="v_pool", offset=0, align_bytes=ALIGN)
+        v_pool = sb.tile([P, T], F32, name="v_pool", align_bytes=ALIGN)
         qw = sb.tile([P, PASSES, NQ], I32, name="qw", align_bytes=ALIGN)
         ident = sb.tile([P, P], F32, name="ident", align_bytes=ALIGN)
-        early_bias = sb.tile([P, 1], F32, name="early_bias")
-        ks_g = [placed.tile([P, N // 2], U8, name="ks_g%d" % h, offset=HELD + h * N // 2) for h in range(2)]
-        staged = placed.tile([P, SCALES], U8, name="staged", offset=STAGED_AT, align_bytes=ALIGN)
-        vs_last = placed.tile([P, P], F32, name="vs_last", offset=STAGED_AT, align_bytes=ALIGN)
-        planes = placed.tile([P, PASSES * SCALES], U8, name="planes", offset=KS_AT, align_bytes=ALIGN)
+        early_zero = sb.tile([P, 1], F32, name="early_zero")
+        late_zero = sb.tile([P, 1], F32, name="late_zero")
         vs_l = sb.tile([P, N], F32, name="vs_l", align_bytes=ALIGN)
-        vs_g = placed.tile([P, N], F32, name="vs_g", offset=HELD + 3 * N // 4, align_bytes=64)
-        kw_g = [sb.tile([P, N // 2], U32, name="kw_g%d" % h, align_bytes=ALIGN) for h in range(2)]
+        vs_g = sb.tile([P, PACK, P], F32, name="vs_g", align_bytes=ALIGN)
+        kw_g = [sb.tile([P, HALF], U32, name="kw_g%d" % h, align_bytes=ALIGN) for h in range(2)]
         k_codes = sb.tile([P, PACK, PASSES, P], U16, name="k_codes", align_bytes=ALIGN)
         v_g = sb.tile([P, N], BF16, name="v_g", align_bytes=ALIGN)
         v_in = sb.tile([P, DV, PACK], BF16, name="v_in", align_bytes=ALIGN)
@@ -71,7 +68,7 @@ def tile_attend_silu_topkq128n512t2048_kernel(tc, q_words, q_scales, k_words, k_
         v_codes = sb.tile([P, DV], U32, name="v_codes", align_bytes=ALIGN)
         v_scales = sb.tile([P, DV], U8, name="v_scales", align_bytes=ALIGN)
         y_sb = sb.tile([P, DV], F32, name="y_sb", align_bytes=ALIGN)
-        p_sb = placed.tile([P, NQ // PIECES, PIECES, PACK], F32, name="p_sb", offset=WORD * T, align_bytes=ALIGN)
+        p_sb = sb.tile([P, NQ, PACK], F32, name="p_sb", align_bytes=ALIGN)
         w_in = sb.tile([P, NQ, PACK], BF16, name="w_in", align_bytes=ALIGN)
 
         scores = ps.tile([P, PACK, NQ], F32, name="scores")
@@ -80,63 +77,45 @@ def tile_attend_silu_topkq128n512t2048_kernel(tc, q_words, q_scales, k_words, k_
         y_ps = [ps.tile([P, DV // 2], F32, name="y_ps%d" % h) for h in range(2)]
 
         first, behind = QUAD, 2 * QUAD
-        nc.scalar.dma_start(ks_pool[:].bitcast(I32)[first:behind, 0 : T // WORD], k_scales.bitcast(I32).rearrange("o f c -> f o c"))
+        nc.scalar.dma_start(ks_pool[:].bitcast(I32)[first:behind, :], k_scales.bitcast(I32).rearrange("o f c -> f o c"))
         nc.sync.dma_start(offsets[:], offs)
         nc.sync.dma_start(vs_pool[P - 1 : P, 0:T], vs[0:1, :])
-        nc.scalar.dma_start(staged[:].bitcast(I32)[first:behind, N // WORD :], q_scales[0].bitcast(I32).rearrange("o f c -> f o c"))
+        nc.scalar.dma_start(staged[first:behind, N // WORD :], q_scales[0].bitcast(I32).rearrange("o f c -> f o c"))
         nc.sync.dma_start(kw_pool[:], k_words[0].rearrange("g t r -> g (t r)").bitcast(I32))
         nc.sync.dma_start(qw[:], q_words[0].rearrange("o g q r -> g o (q r)").bitcast(I32))
         nc.sync.dma_start(v_pool[:, 0:EARLY], vT[:, 0:EARLY])
         zero = v_pool[:, EARLY : EARLY + 1]
         nc.vector.memset(zero, 0.0)
-        nc.vector.memset(v_pool[:, T : T + SPARE], 0.0)
-        nc.vector.memset(ks_pool[:].bitcast(I32)[0:first, :], 0)
-        nc.vector.memset(ks_pool[:].bitcast(I32)[behind:P, :], 0)
+        nc.gpsimd.memset(ks_pool[:].bitcast(I32)[0:first, :], 0)
+        nc.gpsimd.memset(ks_pool[:].bitcast(I32)[behind:P, :], 0)
         nc.gpsimd.memset(vs_pool[0 : P - 1, 0:CLEARED].bitcast(I32), 0)
         nc.vector.memset(vs_pool[0 : P - 1, CLEARED:].bitcast(I32), 0)
         make_identity(nc, ident[:])
-        nc.scalar.activation(early_bias[:], v_pool[:, T : T + 1], ACT.Silu)
+        nc.scalar.activation(early_zero[:], zero, ACT.Silu)
 
-        list_halves = [offsets[:, h * N // 32 : (h + 1) * N // 32] for h in range(2)]
-        for h in range(2):
-            nc.vector.tensor_copy(ks_g[h][:], ks_pool[:, 0:T].indirect(list_halves[h]))
-        nc.vector.tensor_copy(
-            staged[:, 0:N].rearrange("p (t h s) -> p h t s", t=PACK, h=2)[:, 0],
-            ks_g[0][:].rearrange("p (s t) -> p t s", t=PACK),
-        )
-        nc.vector.tensor_copy(
-            staged[:].bitcast(I32)[:, 0 : N // WORD].rearrange("p (t h b) -> p h b t", t=PACK, h=2)[:, 1],
-            ks_g[1][:].bitcast(I32).rearrange("p (b t) -> p b t", t=PACK),
-        )
-        no_bias = placed.tile([P, 1], F32, name="no_bias", offset=HELD + N // 2)
-        nc.vector.tensor_copy(no_bias[:], zero)
+        nc.vector.tensor_copy(ks_g[:].rearrange("p (t s) -> p s t", t=PACK), ks_pool[:].indirect(offsets[:]))
+        nc.vector.tensor_copy(staged[:, 0 : N // WORD], ks_g[:].bitcast(I32))
         for a in range(P // QUAD):
             nc.sync.dma_start(
                 planes[:].bitcast(I32)[a * QUAD : a * QUAD + ROWS, :].rearrange("i (o c) -> i o c", o=PASSES),
-                staged[:].bitcast(I32)[first + a * ROWS * PASSES : first + (a + 1) * ROWS * PASSES, :],
+                staged[first + a * ROWS * PASSES : first + (a + 1) * ROWS * PASSES, :],
             )
+        nc.vector.tensor_tensor(held_zero[:], zero, early_zero[:], ALU.add)
         nc.sync.dma_start(v_pool[:, EARLY:T], vT[:, EARLY:T])
+        nc.gpsimd.tensor_scalar(late_zero[:], v_pool[:, T - 1 : T], 0.0, held_zero[:], ALU.is_ge, ALU.mult)
 
-        nc.scalar.activation(vs_l[:], vs_pool[:, 0:T].indirect(offsets[:]), ACT.Copy)
-        vs_dealt = vs_g[:].rearrange("p (t h s) -> p h t s", t=PACK, h=2)[:, :, 1:PACK]
-        vs_plain = vs_l[:, 0:HALF].rearrange("p (s t) -> p s t", t=PACK)
-        vs_runs = vs_l[:, HALF:N].rearrange("p (b t j) -> p t b j", t=PACK, j=RUN)
-        nc.scalar.copy(vs_dealt[:, 0].rearrange("p t s -> p s t"), vs_plain[:, :, 1:PACK])
-        nc.scalar.copy(vs_dealt[:, 1].rearrange("p t (b j) -> p t b j", j=RUN), vs_runs[:, 1:PACK])
-        for t in reversed(range(1, PACK)):
-            nc.tensor.transpose(vs_t[:, t : t + P], vs_g[:, t * P : (t + 1) * P], ident[:])
+        nc.scalar.activation(vs_l[:], vs_pool[:].indirect(offsets[:]), ACT.Copy)
+        nc.scalar.copy(vs_g[:], vs_l[:].rearrange("p (s t) -> p t s", t=PACK))
+        for t in reversed(range(PACK)):
+            nc.tensor.transpose(vs_t[:, t : t + P], vs_g[:, t, :], ident[:])
 
-        nc.vector.tensor_copy(kw_g[0][:].rearrange("p (t s) -> p s t", t=PACK), kw_pool[:].bitcast(U32).indirect(list_halves[0]))
-        nc.vector.tensor_copy(kw_g[1][:], kw_pool[:].bitcast(U32).indirect(list_halves[1]))
-        nc.vector.tensor_copy(
-            k_codes[:, :, :, 0 : P // 2],
-            kw_g[0][:].bitcast(U16).rearrange("p (t s o) -> p t o s", t=PACK, o=PASSES),
-        )
+        list_halves = [offsets[:, h * N // 32 : (h + 1) * N // 32] for h in range(2)]
+        for h in range(2):
+            nc.vector.tensor_copy(kw_g[h][:].rearrange("p (t s) -> p s t", t=PACK), kw_pool[:].bitcast(U32).indirect(list_halves[h]))
+        words = [kw_g[h][:].bitcast(U16).rearrange("p (t s o) -> p t o s", t=PACK, o=PASSES) for h in range(2)]
+        nc.vector.tensor_copy(k_codes[:, :, :, 0 : P // 2], words[0])
         for ts in (slice(0, 1), slice(1, PACK)):
-            nc.vector.tensor_copy(
-                k_codes[:, ts, :, P // 2 : P].rearrange("p t o (b j) -> p t o b j", j=RUN),
-                kw_g[1][:].bitcast(U16).rearrange("p (b t j o) -> p t o b j", t=PACK, j=RUN, o=PASSES)[:, ts],
-            )
+            nc.vector.tensor_copy(k_codes[:, ts, :, P // 2 : P], words[1][:, ts])
         for t in range(PACK):
             for o in range(PASSES):
                 nc.tensor.matmul_mx(
@@ -148,25 +127,22 @@ def tile_attend_silu_topkq128n512t2048_kernel(tc, q_words, q_scales, k_words, k_
                     start=(o == 0),
                     stop=(o == PASSES - 1),
                 )
-        nc.scalar.copy(vs_last[:, 0 : P // 2], vs_plain[:, :, 0])
-        nc.scalar.copy(vs_last[:, P // 2 : P].rearrange("p (b j) -> p b j", j=RUN), vs_runs[:, 0])
-        nc.tensor.transpose(vs_t[:, 0:P], vs_last[:], ident[:])
 
         nc.scalar.activation(v_g[:, 0:HALF], v_pool[:].indirect(list_halves[0]), ACT.Copy)
-        nc.vector.tensor_copy(v_g[:, HALF:N].rearrange("p (b j t) -> p b t j", j=RUN, t=PACK), v_pool[:, 0:T].indirect(list_halves[1]))
+        nc.vector.tensor_copy(v_g[:, HALF:N], v_pool[:].indirect(list_halves[1]))
         v_words = v_g[:].bitcast(F32).rearrange("p (s u) -> p u s", u=2)
         for u in range(2):
             nc.tensor.transpose(v_t[:, u, :], v_words[:, u], ident[:])
 
         q_halves = [slice(h * NQ // 2, (h + 1) * NQ // 2) for h in range(2)]
-        q_quarters = [slice(c * NQ // 4, (c + 1) * NQ // 4) for c in range(4)]
-        for c, (qs, bias) in enumerate(zip(q_quarters, (no_bias, no_bias, early_bias, early_bias))):
-            nc.scalar.activation(p_sb[:, :, c], scores[:, :, qs].rearrange("p t q -> p q t"), ACT.Silu, bias=bias[:])
-        for c, qs in enumerate(q_quarters):
+        q_pieces = [slice(c * NQ // PIECES, (c + 1) * NQ // PIECES) for c in range(PIECES)]
+        for qs in q_pieces:
+            nc.scalar.activation(p_sb[:, qs, :], scores[:, :, qs].rearrange("p t q -> p q t"), ACT.Silu, bias=late_zero[:])
+        for qs in q_pieces:
             nc.vector.tensor_tensor(
                 w_in[:, qs, :],
-                p_sb[:, :, c],
-                vs_t[:, P - 1 : P - 1 + PACK].unsqueeze(1).to_broadcast([P, NQ // 4, PACK]),
+                p_sb[:, qs, :],
+                vs_t[:, P - 1 : P - 1 + PACK].unsqueeze(1).to_broadcast([P, NQ // PIECES, PACK]),
                 ALU.mult,
             )
         halves = [slice(h * DV // 2, (h + 1) * DV // 2) for h in range(2)]

@@ -47,7 +47,7 @@ def tile_attend_silu_topkq128n512t2048_kernel(tc, q_words, q_scales, k_words, k_
         offsets = sb.tile([P, N // 16], U16, name="offsets")
         ks_pool = placed.tile([P, T], U8, name="ks_pool", offset=0, align_bytes=ALIGN)
         ks_g = sb.tile([P, N], U8, name="ks_g", align_bytes=ALIGN)
-        staged = sb.tile([P, SCALES // WORD], I32, name="staged", align_bytes=ALIGN)
+        staged = placed.tile([P, SCALES // WORD], I32, name="staged", offset=T, align_bytes=ALIGN)
         planes = placed.tile([P, PASSES * SCALES], U8, name="planes", offset=PLANES_AT, align_bytes=ALIGN)
         held_zero = placed.tile([P, 1], F32, name="held_zero", offset=0)
         vs_pool = sb.tile([P, T + 1], F32, name="vs_pool", align_bytes=ALIGN)
@@ -58,7 +58,8 @@ def tile_attend_silu_topkq128n512t2048_kernel(tc, q_words, q_scales, k_words, k_
         early_zero = sb.tile([P, 1], F32, name="early_zero")
         late_zero = sb.tile([P, 1], F32, name="late_zero")
         vs_l = sb.tile([P, N], F32, name="vs_l", align_bytes=ALIGN)
-        vs_g = sb.tile([P, PACK, P], F32, name="vs_g", align_bytes=ALIGN)
+        vs_g = sb.tile([P, PACK - 1, P], F32, name="vs_g", align_bytes=ALIGN)
+        vs_last = placed.tile([P, P], F32, name="vs_last", offset=T, align_bytes=ALIGN)
         kw_g = [sb.tile([P, HALF], U32, name="kw_g%d" % h, align_bytes=ALIGN) for h in range(2)]
         k_codes = sb.tile([P, PACK, PASSES, P], U16, name="k_codes", align_bytes=ALIGN)
         v_g = sb.tile([P, N], BF16, name="v_g", align_bytes=ALIGN)
@@ -68,10 +69,11 @@ def tile_attend_silu_topkq128n512t2048_kernel(tc, q_words, q_scales, k_words, k_
         v_codes = sb.tile([P, DV], U32, name="v_codes", align_bytes=ALIGN)
         v_scales = sb.tile([P, DV], U8, name="v_scales", align_bytes=ALIGN)
         y_sb = sb.tile([P, DV], F32, name="y_sb", align_bytes=ALIGN)
-        p_sb = sb.tile([P, NQ, PACK], F32, name="p_sb", align_bytes=ALIGN)
+        p_sb = sb.tile([P, PACK, NQ], F32, name="p_sb", align_bytes=ALIGN)
         w_in = sb.tile([P, NQ, PACK], BF16, name="w_in", align_bytes=ALIGN)
 
-        scores = ps.tile([P, PACK, NQ], F32, name="scores")
+        scores_first = ps.tile([P, NQ], F32, name="scores_first")
+        scores_rest = ps.tile([P, PACK - 1, NQ], F32, name="scores_rest")
         vs_t = ps.tile([P, N], F32, name="vs_t")
         v_t = ps.tile([P, 2, DV], F32, name="v_t")
         y_ps = [ps.tile([P, DV // 2], F32, name="y_ps%d" % h) for h in range(2)]
@@ -105,9 +107,11 @@ def tile_attend_silu_topkq128n512t2048_kernel(tc, q_words, q_scales, k_words, k_
         nc.gpsimd.tensor_scalar(late_zero[:], v_pool[:, T - 1 : T], 0.0, held_zero[:], ALU.is_ge, ALU.mult)
 
         nc.scalar.activation(vs_l[:], vs_pool[:].indirect(offsets[:]), ACT.Copy)
-        nc.scalar.copy(vs_g[:], vs_l[:].rearrange("p (s t) -> p t s", t=PACK))
-        for t in reversed(range(PACK)):
-            nc.tensor.transpose(vs_t[:, t : t + P], vs_g[:, t, :], ident[:])
+        vs_places = vs_l[:].rearrange("p (s t) -> p t s", t=PACK)
+        nc.scalar.copy(vs_g[:], vs_places[:, 1:PACK, :])
+        for t in reversed(range(1, PACK)):
+            nc.tensor.transpose(vs_t[:, t : t + P], vs_g[:, t - 1, :], ident[:])
+        nc.scalar.copy(vs_last[:], vs_places[:, 0, :])
 
         list_halves = [offsets[:, h * N // 32 : (h + 1) * N // 32] for h in range(2)]
         for h in range(2):
@@ -119,7 +123,7 @@ def tile_attend_silu_topkq128n512t2048_kernel(tc, q_words, q_scales, k_words, k_
         for t in range(PACK):
             for o in range(PASSES):
                 nc.tensor.matmul_mx(
-                    out=scores[:, t, :],
+                    out=scores_first[:] if t == 0 else scores_rest[:, t - 1, :],
                     lhsT=k_codes[:, t, o, :].bitcast(FP4X4),
                     lhsT_scale=planes[:, o * SCALES + t * P : o * SCALES + (t + 1) * P],
                     rhs=qw[:, o, :].bitcast(FP8X4),
@@ -128,6 +132,8 @@ def tile_attend_silu_topkq128n512t2048_kernel(tc, q_words, q_scales, k_words, k_
                     stop=(o == PASSES - 1),
                 )
 
+        nc.tensor.transpose(vs_t[:, 0:P], vs_last[:], ident[:])
+        nc.scalar.activation(p_sb[:, 0, :], scores_first[:], ACT.Silu)
         nc.scalar.activation(v_g[:, 0:HALF], v_pool[:].indirect(list_halves[0]), ACT.Copy)
         nc.vector.tensor_copy(v_g[:, HALF:N], v_pool[:].indirect(list_halves[1]))
         v_words = v_g[:].bitcast(F32).rearrange("p (s u) -> p u s", u=2)
@@ -137,11 +143,11 @@ def tile_attend_silu_topkq128n512t2048_kernel(tc, q_words, q_scales, k_words, k_
         q_halves = [slice(h * NQ // 2, (h + 1) * NQ // 2) for h in range(2)]
         q_pieces = [slice(c * NQ // PIECES, (c + 1) * NQ // PIECES) for c in range(PIECES)]
         for qs in q_pieces:
-            nc.scalar.activation(p_sb[:, qs, :], scores[:, :, qs].rearrange("p t q -> p q t"), ACT.Silu, bias=late_zero[:])
+            nc.scalar.activation(p_sb[:, 1:PACK, qs], scores_rest[:, :, qs], ACT.Silu, bias=late_zero[:])
         for qs in q_pieces:
             nc.vector.tensor_tensor(
                 w_in[:, qs, :],
-                p_sb[:, qs, :],
+                p_sb[:, :, qs].rearrange("p t q -> p q t"),
                 vs_t[:, P - 1 : P - 1 + PACK].unsqueeze(1).to_broadcast([P, NQ // PIECES, PACK]),
                 ALU.mult,
             )

@@ -151,6 +151,15 @@ def tile_attend_silu_topkq128n512t2048_kernel(tc, q_words, q_scales, k_words, k_
                 vs_t[:, P - 1 : P - 1 + PACK].unsqueeze(1).to_broadcast([P, NQ // PIECES, PACK]),
                 ALU.mult,
             )
+        nc.tensor.matmul_mx(
+            out=scores_rest[:, 0, 0 : NQ // 2],
+            lhsT=qw[:, 0, :].bitcast(FP8X4),
+            lhsT_scale=planes[:, N:SCALES],
+            rhs=qw[:, 0, 0 : NQ // 2].bitcast(FP8X4),
+            rhs_scale=planes[:, N : N + NQ // 2],
+            start=True,
+            stop=True,
+        )
         halves = [slice(h * DV // 2, (h + 1) * DV // 2) for h in range(2)]
         for es in halves:
             nc.scalar.copy(v_in[:, es, :].bitcast(F32), v_t[:, :, es].rearrange("p u e -> p e u"))

@@ -69,11 +69,10 @@ def tile_attend_silu_topkq128n512t2048_kernel(tc, q_words, q_scales, k_words, k_
         v_codes = sb.tile([P, DV], U32, name="v_codes", align_bytes=ALIGN)
         v_scales = sb.tile([P, DV], U8, name="v_scales", align_bytes=ALIGN)
         y_sb = sb.tile([P, DV], F32, name="y_sb", align_bytes=ALIGN)
-        p_sb = sb.tile([P, PACK, NQ], F32, name="p_sb", align_bytes=ALIGN)
+        p_sb = sb.tile([P, NQ, PACK], F32, name="p_sb", align_bytes=ALIGN)
         w_in = sb.tile([P, NQ, PACK], BF16, name="w_in", align_bytes=ALIGN)
 
-        scores_first = ps.tile([P, NQ], F32, name="scores_first")
-        scores_rest = ps.tile([P, PACK - 1, NQ], F32, name="scores_rest")
+        scores = ps.tile([P, PACK, NQ], F32, name="scores")
         vs_t = ps.tile([P, N], F32, name="vs_t")
         v_t = ps.tile([P, 2, DV], F32, name="v_t")
         y_ps = [ps.tile([P, DV // 2], F32, name="y_ps%d" % h) for h in range(2)]
@@ -123,7 +122,7 @@ def tile_attend_silu_topkq128n512t2048_kernel(tc, q_words, q_scales, k_words, k_
         for t in range(PACK):
             for o in range(PASSES):
                 nc.tensor.matmul_mx(
-                    out=scores_first[:] if t == 0 else scores_rest[:, t - 1, :],
+                    out=scores[:, t, :],
                     lhsT=k_codes[:, t, o, :].bitcast(FP4X4),
                     lhsT_scale=planes[:, o * SCALES + t * P : o * SCALES + (t + 1) * P],
                     rhs=qw[:, o, :].bitcast(FP8X4),
@@ -133,7 +132,7 @@ def tile_attend_silu_topkq128n512t2048_kernel(tc, q_words, q_scales, k_words, k_
                 )
 
         nc.tensor.transpose(vs_t[:, 0:P], vs_last[:], ident[:])
-        nc.scalar.activation(p_sb[:, 0, :], scores_first[:], ACT.Silu)
+
         nc.scalar.activation(v_g[:, 0:HALF], v_pool[:].indirect(list_halves[0]), ACT.Copy)
         nc.vector.tensor_copy(v_g[:, HALF:N], v_pool[:].indirect(list_halves[1]))
         v_words = v_g[:].bitcast(F32).rearrange("p (s u) -> p u s", u=2)
@@ -143,16 +142,16 @@ def tile_attend_silu_topkq128n512t2048_kernel(tc, q_words, q_scales, k_words, k_
         q_halves = [slice(h * NQ // 2, (h + 1) * NQ // 2) for h in range(2)]
         q_pieces = [slice(c * NQ // PIECES, (c + 1) * NQ // PIECES) for c in range(PIECES)]
         for qs in q_pieces:
-            nc.scalar.activation(p_sb[:, 1:PACK, qs], scores_rest[:, :, qs], ACT.Silu, bias=late_zero[:])
+            nc.scalar.activation(p_sb[:, qs, :], scores[:, :, qs].rearrange("p t q -> p q t"), ACT.Silu, bias=late_zero[:])
         for qs in q_pieces:
             nc.vector.tensor_tensor(
                 w_in[:, qs, :],
-                p_sb[:, :, qs].rearrange("p t q -> p q t"),
+                p_sb[:, qs, :],
                 vs_t[:, P - 1 : P - 1 + PACK].unsqueeze(1).to_broadcast([P, NQ // PIECES, PACK]),
                 ALU.mult,
             )
         nc.tensor.matmul_mx(
-            out=scores_rest[:, 0, 0 : NQ // 2],
+            out=scores[:, 0, 0 : NQ // 2],
             lhsT=qw[:, 0, :].bitcast(FP8X4),
             lhsT_scale=planes[:, N:SCALES],
             rhs=qw[:, 0, 0 : NQ // 2].bitcast(FP8X4),

@@ -32,6 +32,7 @@ HALF = N // 2
 CLEARED = T // 4
 PIECES = 4
 PLANES_AT = T - PASSES * SCALES
+RESULTS_AT = T + 3 * ALIGN
 
 FLOPS = 2 * NQ * N * D + 2 * NQ * N * DV
 BYTES = 2 * 128 * 128 * 4 + 2 * 16 * 128 + 128 * T * 4 + 2 * 16 * T + DV * T * 4 + T * 4 + 128 * 32 * 2 + NQ * DV * 4
@@ -66,10 +67,13 @@ def tile_attend_silu_topkq128n512t2048_kernel(tc, q_words, q_scales, k_words, k_
         v_in = sb.tile([P, DV, PACK], BF16, name="v_in", align_bytes=ALIGN)
         w_codes = sb.tile([P, NQ], U32, name="w_codes", align_bytes=ALIGN)
         w_scales = sb.tile([P, NQ], U8, name="w_scales", align_bytes=ALIGN)
-        v_codes = sb.tile([P, DV], U32, name="v_codes", align_bytes=ALIGN)
         v_scales = sb.tile([P, DV], U8, name="v_scales", align_bytes=ALIGN)
         y_sb = sb.tile([P, DV], F32, name="y_sb", align_bytes=ALIGN)
-        p_sb = sb.tile([P, NQ, PACK], F32, name="p_sb", align_bytes=ALIGN)
+        p_sb = placed.tile([P, NQ, PACK], F32, name="p_sb", offset=RESULTS_AT, align_bytes=ALIGN)
+        v_codes = [
+            sb.tile([P, DV // 2], U32, name="v_codes0", align_bytes=ALIGN),
+            placed.tile([P, DV // 2], U32, name="v_codes1", offset=RESULTS_AT, align_bytes=ALIGN),
+        ]
         w_in = sb.tile([P, NQ, PACK], BF16, name="w_in", align_bytes=ALIGN)
 
         scores = ps.tile([P, PACK, NQ], F32, name="scores")
@@ -164,14 +168,14 @@ def tile_attend_silu_topkq128n512t2048_kernel(tc, q_words, q_scales, k_words, k_
             nc.scalar.copy(v_in[:, es, :].bitcast(F32), v_t[:, :, es].rearrange("p u e -> p e u"))
         for qs in q_halves:
             nc.vector.quantize_mx(out=w_codes[:, qs].bitcast(FP8X4), scales=w_scales[:, qs], in_=w_in[:, qs, :].rearrange("p q t -> p (q t)"))
-        for es in halves:
-            nc.vector.quantize_mx(out=v_codes[:, es].bitcast(FP8X4), scales=v_scales[:, es], in_=v_in[:, es, :].rearrange("p e t -> p (e t)"))
+        for h, es in enumerate(halves):
+            nc.vector.quantize_mx(out=v_codes[h][:].bitcast(FP8X4), scales=v_scales[:, es], in_=v_in[:, es, :].rearrange("p e t -> p (e t)"))
         for h, es in enumerate(halves):
             nc.tensor.matmul_mx(
                 out=y_ps[h][:],
                 lhsT=w_codes[:].bitcast(FP8X4),
                 lhsT_scale=w_scales[:],
-                rhs=v_codes[:, es].bitcast(FP8X4),
+                rhs=v_codes[h][:].bitcast(FP8X4),
                 rhs_scale=v_scales[:, es],
                 start=True,
                 stop=True,

from contextlib import ExitStack

import concourse.mybir as mybir
from concourse.masks import make_identity

F32 = mybir.dt.float32
BF16 = mybir.dt.bfloat16
I32 = mybir.dt.int32
U32 = mybir.dt.uint32
U16 = mybir.dt.uint16
U8 = mybir.dt.uint8
FP8X4 = mybir.dt.float8_e4m3fn_x4
FP4X4 = mybir.dt.float4_e2m1fn_x4
ACT = mybir.ActivationFunctionType
ALU = mybir.AluOpType

P = 128
T = 2048
N = 512
D = 1024
DV = 128
NQ = 128
PASSES = 2
PACK = 4
QUAD = 32
ROWS = 4
SCALES = N + NQ
WORD = 4
ALIGN = 256
EARLY = 1088
HALF = N // 2
CLEARED = T // 4
PIECES = 4
PLANES_AT = T - PASSES * SCALES
RESULTS_AT = T + 3 * ALIGN

FLOPS = 2 * NQ * N * D + 2 * NQ * N * DV
BYTES = 2 * 128 * 128 * 4 + 2 * 16 * 128 + 128 * T * 4 + 2 * 16 * T + DV * T * 4 + T * 4 + 128 * 32 * 2 + NQ * DV * 4


def tile_attend_silu_topkq128n512t2048_kernel(tc, q_words, q_scales, k_words, k_scales, vT, vs, offs, out):
    nc = tc.nc
    with ExitStack() as ctx:
        sb = ctx.enter_context(tc.tile_pool(name="sb", bufs=1))
        placed = ctx.enter_context(tc.tile_pool(name="placed", bufs=1))
        ps = ctx.enter_context(tc.psum_pool(name="ps", bufs=1))

        offsets = sb.tile([P, N // 16], U16, name="offsets")
        ks_pool = placed.tile([P, T], U8, name="ks_pool", offset=0, align_bytes=ALIGN)
        ks_g = sb.tile([P, N], U8, name="ks_g", align_bytes=ALIGN)
        staged = placed.tile([P, SCALES // WORD], I32, name="staged", offset=T, align_bytes=ALIGN)
        planes = placed.tile([P, PASSES * SCALES], U8, name="planes", offset=PLANES_AT, align_bytes=ALIGN)
        held_zero = placed.tile([P, 1], F32, name="held_zero", offset=0)
        vs_pool = sb.tile([P, T + 1], F32, name="vs_pool", align_bytes=ALIGN)
        kw_pool = sb.tile([P, T], I32, name="kw_pool", align_bytes=ALIGN)
        v_pool = sb.tile([P, T], F32, name="v_pool", align_bytes=ALIGN)
        qw = sb.tile([P, PASSES, NQ], I32, name="qw", align_bytes=ALIGN)
        ident = sb.tile([P, P], F32, name="ident", align_bytes=ALIGN)
        early_zero = sb.tile([P, 1], F32, name="early_zero")
        late_zero = sb.tile([P, 1], F32, name="late_zero")
        vs_l = sb.tile([P, N], F32, name="vs_l", align_bytes=ALIGN)
        vs_g = sb.tile([P, PACK - 1, P], F32, name="vs_g", align_bytes=ALIGN)
        vs_last = placed.tile([P, P], F32, name="vs_last", offset=T, align_bytes=ALIGN)
        kw_g = [sb.tile([P, HALF], U32, name="kw_g%d" % h, align_bytes=ALIGN) for h in range(2)]
        k_codes = sb.tile([P, PACK, PASSES, P], U16, name="k_codes", align_bytes=ALIGN)
        v_g = sb.tile([P, N], BF16, name="v_g", align_bytes=ALIGN)
        v_in = sb.tile([P, DV, PACK], BF16, name="v_in", align_bytes=ALIGN)
        w_codes = sb.tile([P, NQ], U32, name="w_codes", align_bytes=ALIGN)
        w_scales = sb.tile([P, NQ], U8, name="w_scales", align_bytes=ALIGN)
        v_scales = sb.tile([P, DV], U8, name="v_scales", align_bytes=ALIGN)
        y_sb = sb.tile([P, DV], F32, name="y_sb", align_bytes=ALIGN)
        p_sb = placed.tile([P, NQ, PACK], F32, name="p_sb", offset=RESULTS_AT, align_bytes=ALIGN)
        v_codes = [
            sb.tile([P, DV // 2], U32, name="v_codes0", align_bytes=ALIGN),
            placed.tile([P, DV // 2], U32, name="v_codes1", offset=RESULTS_AT, align_bytes=ALIGN),
        ]
        w_in = sb.tile([P, NQ, PACK], BF16, name="w_in", align_bytes=ALIGN)

        scores = ps.tile([P, PACK, NQ], F32, name="scores")
        vs_t = ps.tile([P, N], F32, name="vs_t")
        v_t = ps.tile([P, 2, DV], F32, name="v_t")
        y_ps = [ps.tile([P, DV // 2], F32, name="y_ps%d" % h) for h in range(2)]

        first, behind = QUAD, 2 * QUAD
        nc.scalar.dma_start(ks_pool[:].bitcast(I32)[first:behind, :], k_scales.bitcast(I32).rearrange("o f c -> f o c"))
        nc.sync.dma_start(offsets[:], offs)
        nc.sync.dma_start(vs_pool[P - 1 : P, 0:T], vs[0:1, :])
        nc.scalar.dma_start(staged[first:behind, N // WORD :], q_scales[0].bitcast(I32).rearrange("o f c -> f o c"))
        nc.sync.dma_start(kw_pool[:], k_words[0].rearrange("g t r -> g (t r)").bitcast(I32))
        nc.sync.dma_start(qw[:], q_words[0].rearrange("o g q r -> g o (q r)").bitcast(I32))
        nc.sync.dma_start(v_pool[:, 0:EARLY], vT[:, 0:EARLY])
        zero = v_pool[:, EARLY : EARLY + 1]
        nc.vector.memset(zero, 0.0)
        nc.gpsimd.memset(ks_pool[:].bitcast(I32)[0:first, :], 0)
        nc.gpsimd.memset(ks_pool[:].bitcast(I32)[behind:P, :], 0)
        nc.gpsimd.memset(vs_pool[0 : P - 1, 0:CLEARED].bitcast(I32), 0)
        nc.vector.memset(vs_pool[0 : P - 1, CLEARED:].bitcast(I32), 0)
        make_identity(nc, ident[:])
        nc.scalar.activation(early_zero[:], zero, ACT.Silu)

        nc.vector.tensor_copy(ks_g[:].rearrange("p (t s) -> p s t", t=PACK), ks_pool[:].indirect(offsets[:]))
        nc.vector.tensor_copy(staged[:, 0 : N // WORD], ks_g[:].bitcast(I32))
        for a in range(P // QUAD):
            nc.sync.dma_start(
                planes[:].bitcast(I32)[a * QUAD : a * QUAD + ROWS, :].rearrange("i (o c) -> i o c", o=PASSES),
                staged[first + a * ROWS * PASSES : first + (a + 1) * ROWS * PASSES, :],
            )
        nc.vector.tensor_tensor(held_zero[:], zero, early_zero[:], ALU.add)
        nc.sync.dma_start(v_pool[:, EARLY:T], vT[:, EARLY:T])
        nc.gpsimd.tensor_scalar(late_zero[:], v_pool[:, T - 1 : T], 0.0, held_zero[:], ALU.is_ge, ALU.mult)

        nc.scalar.activation(vs_l[:], vs_pool[:].indirect(offsets[:]), ACT.Copy)
        vs_places = vs_l[:].rearrange("p (s t) -> p t s", t=PACK)
        nc.scalar.copy(vs_g[:], vs_places[:, 1:PACK, :])
        for t in reversed(range(1, PACK)):
            nc.tensor.transpose(vs_t[:, t : t + P], vs_g[:, t - 1, :], ident[:])
        nc.scalar.copy(vs_last[:], vs_places[:, 0, :])

        list_halves = [offsets[:, h * N // 32 : (h + 1) * N // 32] for h in range(2)]
        for h in range(2):
            nc.vector.tensor_copy(kw_g[h][:].rearrange("p (t s) -> p s t", t=PACK), kw_pool[:].bitcast(U32).indirect(list_halves[h]))
        words = [kw_g[h][:].bitcast(U16).rearrange("p (t s o) -> p t o s", t=PACK, o=PASSES) for h in range(2)]
        nc.vector.tensor_copy(k_codes[:, :, :, 0 : P // 2], words[0])
        for ts in (slice(0, 1), slice(1, PACK)):
            nc.vector.tensor_copy(k_codes[:, ts, :, P // 2 : P], words[1][:, ts])
        for t in range(PACK):
            for o in range(PASSES):
                nc.tensor.matmul_mx(
                    out=scores[:, t, :],
                    lhsT=k_codes[:, t, o, :].bitcast(FP4X4),
                    lhsT_scale=planes[:, o * SCALES + t * P : o * SCALES + (t + 1) * P],
                    rhs=qw[:, o, :].bitcast(FP8X4),
                    rhs_scale=planes[:, o * SCALES + N : (o + 1) * SCALES],
                    start=(o == 0),
                    stop=(o == PASSES - 1),
                )

        nc.tensor.transpose(vs_t[:, 0:P], vs_last[:], ident[:])

        nc.scalar.activation(v_g[:, 0:HALF], v_pool[:].indirect(list_halves[0]), ACT.Copy)
        nc.vector.tensor_copy(v_g[:, HALF:N], v_pool[:].indirect(list_halves[1]))
        v_words = v_g[:].bitcast(F32).rearrange("p (s u) -> p u s", u=2)
        for u in range(2):
            nc.tensor.transpose(v_t[:, u, :], v_words[:, u], ident[:])

        q_halves = [slice(h * NQ // 2, (h + 1) * NQ // 2) for h in range(2)]
        q_pieces = [slice(c * NQ // PIECES, (c + 1) * NQ // PIECES) for c in range(PIECES)]
        for qs in q_pieces:
            nc.scalar.activation(p_sb[:, qs, :], scores[:, :, qs].rearrange("p t q -> p q t"), ACT.Silu, bias=late_zero[:])
        for qs in q_pieces:
            nc.vector.tensor_tensor(
                w_in[:, qs, :],
                p_sb[:, qs, :],
                vs_t[:, P - 1 : P - 1 + PACK].unsqueeze(1).to_broadcast([P, NQ // PIECES, PACK]),
                ALU.mult,
            )
        nc.tensor.matmul_mx(
            out=scores[:, 0, 0 : NQ // 2],
            lhsT=qw[:, 0, :].bitcast(FP8X4),
            lhsT_scale=planes[:, N:SCALES],
            rhs=qw[:, 0, 0 : NQ // 2].bitcast(FP8X4),
            rhs_scale=planes[:, N : N + NQ // 2],
            start=True,
            stop=True,
        )
        halves = [slice(h * DV // 2, (h + 1) * DV // 2) for h in range(2)]
        for es in halves:
            nc.scalar.copy(v_in[:, es, :].bitcast(F32), v_t[:, :, es].rearrange("p u e -> p e u"))
        for qs in q_halves:
            nc.vector.quantize_mx(out=w_codes[:, qs].bitcast(FP8X4), scales=w_scales[:, qs], in_=w_in[:, qs, :].rearrange("p q t -> p (q t)"))
        for h, es in enumerate(halves):
            nc.vector.quantize_mx(out=v_codes[h][:].bitcast(FP8X4), scales=v_scales[:, es], in_=v_in[:, es, :].rearrange("p e t -> p (e t)"))
        for h, es in enumerate(halves):
            nc.tensor.matmul_mx(
                out=y_ps[h][:],
                lhsT=w_codes[:].bitcast(FP8X4),
                lhsT_scale=w_scales[:],
                rhs=v_codes[h][:].bitcast(FP8X4),
                rhs_scale=v_scales[:, es],
                start=True,
                stop=True,
            )
        for h, es in enumerate(halves):
            nc.scalar.activation(y_sb[:, es], y_ps[h][:], ACT.Copy, scale=1.0 / 16.0)
        nc.sync.dma_start(out[0], y_sb[:])
